import numpy as np
import ml_dtypes


def mxq(x, axis, fmt="e4m3"):
    dtype, down = {"e4m3": (ml_dtypes.float8_e4m3fn, 7), "e5m2": (ml_dtypes.float8_e5m2, 14)}[fmt]
    v = np.moveaxis(np.asarray(x, np.float32).astype(ml_dtypes.bfloat16).astype(np.float64), axis, -1)
    blocks = v.reshape(v.shape[:-1] + (-1, 32))
    amax = np.abs(blocks).max(-1, keepdims=True)
    byte = np.maximum(np.where(amax > 0, np.frexp(amax)[1] - 1 + 127, 0) - down, 1)
    scale = np.exp2(byte - 127.0)
    codes = (blocks / scale).astype(np.float32).astype(dtype).astype(np.float64)
    return np.moveaxis((codes * scale).reshape(v.shape), -1, axis)


WIDE = False


def mx_kscale(k):
    if not WIDE:
        return np.ones(k)
    levels = np.array([10, -10, 5, -5, 0])
    if k % 512:
        return np.exp2(np.random.permutation(np.resize(levels, k // 32))).repeat(32)
    a = np.empty((k // 512, 16))
    for p in range(k // 512):
        a[p, :8] = np.random.permutation(np.resize(levels, 8))
        for g in range(8):
            far = levels[np.abs(levels - a[p, g]) >= 10]
            a[p, g + 8] = far[np.random.randint(len(far))]
    return np.exp2(a.ravel()).repeat(32)


def f64(x):
    return np.asarray(x).astype(np.float64)


def striped(idx):
    return np.tile(idx.reshape(-1, 16).T, (8, 1)).astype(np.uint16)


def unstriped(offs):
    return offs[:16].T.reshape(-1).astype(np.int64)


def pack_weight(w):
    k, n = w.shape
    w = f64(np.asarray(w, np.float32).astype(ml_dtypes.bfloat16)).reshape(k // 32, 32, n)
    amax = np.abs(w).max(1)
    byte = np.clip(np.where(amax > 0, np.frexp(amax)[1] - 1 + 127 - 7, 1), 1, 254)
    scaled = (w * np.exp2(127.0 - byte)[:, None, :]).reshape(k, n).astype(np.float32)
    words = np.ascontiguousarray(scaled.reshape(k // 512, 128, 4, n).transpose(0, 1, 3, 2)).astype(ml_dtypes.float8_e4m3fn).view(np.uint8)
    return words, np.ascontiguousarray(byte.astype(np.uint8).reshape(k // 512, 16, n))


def unpack_weight(words, scales):
    g, p, n, _ = words.shape
    vals = np.ascontiguousarray(words).view(ml_dtypes.float8_e4m3fn).astype(np.float64) * np.repeat(np.exp2(scales.astype(np.float64) - 127.0), 8, axis=1)[..., None]
    return vals.transpose(0, 1, 3, 2).reshape(g * 512, n)


E2M1 = np.array([0.0, 0.5, 1.0, 1.5, 2.0, 3.0, 4.0, 6.0, -0.0, -0.5, -1.0, -1.5, -2.0, -3.0, -4.0, -6.0])


def pack_fp4(w):
    k, n = w.shape
    w = f64(np.asarray(w, np.float32).astype(ml_dtypes.bfloat16)).reshape(k // 32, 32, n)
    amax = np.abs(w).max(1)
    mant, ex = np.frexp(amax / 6.0)
    byte = np.clip(np.where(amax > 0, np.where(mant > 0.5, ex, ex - 1) + 127, 1), 1, 254)
    scaled = (w * np.exp2(127.0 - byte)[:, None, :]).reshape(k, n).astype(np.float32)
    c = np.ascontiguousarray(scaled.reshape(k // 512, 128, 4, n).transpose(0, 1, 3, 2)).astype(ml_dtypes.float4_e2m1fn).view(np.uint8) & 0xF
    words = (c[..., 0::2] | (c[..., 1::2] << 4)).reshape(k // 512, 128, 2 * n)
    return np.ascontiguousarray(words), np.ascontiguousarray(byte.astype(np.uint8).reshape(k // 512, 16, n))


def unpack_fp4(words, scales):
    g, _, n = scales.shape
    words = np.ascontiguousarray(words).reshape(g, 128, n, 2)
    nib = np.empty((g, 128, n, 4), np.uint8)
    nib[..., 0::2] = words & 0xF
    nib[..., 1::2] = words >> 4
    vals = E2M1[nib] * np.repeat(np.exp2(scales.astype(np.float64) - 127.0), 8, axis=1)[..., None]
    return vals.transpose(0, 1, 3, 2).reshape(g * 512, n)


def relu(v):
    return np.maximum(v, 0.0)


K, T, S, V, H, N = 512, 2048, 1024, 512, 512, 128


def setup_inputs():
    n = np.random.standard_normal
    s = mx_kscale(K)[:, None]
    u = mx_kscale(H)
    packed_xT = pack_weight(n((K, T)) * s)
    packed_w2 = pack_fp4(n((H, N)) / np.sqrt(2 * H) / u[:, None])
    packed_w3 = pack_fp4(n((H, N)) / np.sqrt(2 * H) / u[:, None])
    return {
        "x_words": packed_xT[0],
        "x_scales": packed_xT[1],
        "w1": (n((K, H)) / np.sqrt(K) / s * u).astype(np.float32),
        "w2_words": packed_w2[0],
        "w2_scales": packed_w2[1],
        "w3_words": packed_w3[0],
        "w3_scales": packed_w3[1],
        "offs": striped(np.random.permutation(T)[:S]),
        "cen": striped(np.random.permutation(S)[:V]),
        "pos1": striped(np.random.permutation(S)[:V]),
        "pos2": striped(np.random.permutation(S)[:V]),
        "pos3": striped(np.random.permutation(S)[:V]),
        "pos4": striped(np.random.permutation(S)[:V]),
    }


def reference(x_words, x_scales, w1, w2_words, w2_scales, w3_words, w3_scales, offs, cen, pos1, pos2, pos3, pos4):
    xq = unpack_weight(x_words, x_scales)[:, unstriped(offs)]
    h = relu(mxq(f64(w1), 0, "e4m3").T @ xq)
    hc = h[:, unstriped(cen)]
    z = np.maximum(np.maximum(np.maximum(h[:, unstriped(pos1)], h[:, unstriped(pos2)]), h[:, unstriped(pos3)]), h[:, unstriped(pos4)])
    return relu(unpack_fp4(w2_words, w2_scales).T @ mxq(hc, 0, "e4m3") + unpack_fp4(w3_words, w3_scales).T @ mxq(z, 0, "e4m3"))

@@ -1,0 +1,186 @@
+from contextlib import ExitStack
+
+import concourse.mybir as mybir
+
+K, T, S, V, H, N = 512, 2048, 1024, 512, 512, 128
+FLOPS = 2 * K * H * S + 2 * 2 * H * N * V
+
+F32 = mybir.dt.float32
+BF16 = mybir.dt.bfloat16
+I32 = mybir.dt.int32
+U32 = mybir.dt.uint32
+U16 = mybir.dt.uint16
+U8 = mybir.dt.uint8
+FP8X4 = mybir.dt.float8_e4m3fn_x4
+FP4X4 = mybir.dt.float4_e2m1fn_x4
+MAX = mybir.AluOpType.max
+RELU = mybir.ActivationFunctionType.Relu
+COPY = mybir.ActivationFunctionType.Copy
+
+P = 128
+PACK = 4
+BANK = 512
+GROUP = 128
+EARLY = 384
+LATE = 768
+
+
+def tile_picked_sagecat_maxrelu_p_kernel(
+    tc, x_words, x_scales, w1, w2_words, w2_scales, w3_words, w3_scales, offs, cen, pos1, pos2, pos3, pos4, out
+):
+    nc = tc.nc
+    with ExitStack() as ctx:
+        lists = ctx.enter_context(tc.tile_pool(name="lists", bufs=1))
+        keep = ctx.enter_context(tc.tile_pool(name="keep", bufs=1))
+        psum_h = ctx.enter_context(tc.psum_pool(name="psum_h", bufs=4))
+        psum_o = ctx.enter_context(tc.psum_pool(name="psum_o", bufs=1))
+
+        offs_sb = lists.tile([P, S // 16], U16, name="offs_sb")
+        cen_sb = lists.tile([P, V // 16], U16, name="cen_sb")
+        pos_sb = [lists.tile([P, V // 16], U16, name=f"pos_sb{d}") for d in range(4)]
+
+        xw = keep.tile([P, T], I32, name="xw", align_bytes=64)
+        xs = keep.tile([P, T], U8, name="xs", align_bytes=64)
+        ws = keep.tile([P, 2 * N], U8, name="ws", align_bytes=64)
+        w2w = keep.tile([P, 2 * N], U8, name="w2w", align_bytes=64)
+        w3w = keep.tile([P, 2 * N], U8, name="w3w", align_bytes=64)
+        w1_raw = [keep.tile([P, PACK, H // 2], F32, name=f"w1_raw{a}", align_bytes=64) for a in range(2)]
+
+        nc.vector.memset(xs[:].bitcast(I32), 0)
+        nc.vector.memset(ws[:].bitcast(I32), 0)
+
+        nc.sync.dma_start(offs_sb[:], offs)
+        nc.sync.dma_start(xw[:], x_words[0].rearrange("p n r -> p (n r)").bitcast(I32))
+        for r in range(4):
+            nc.sync.dma_start(xs[r:P:32, :].bitcast(I32), x_scales[0, r:16:4, :].bitcast(I32))
+        w1_rows = w1.rearrange("(p j) c -> p j c", j=PACK)
+        for a in range(2):
+            nc.sync.dma_start(w1_raw[a][:], w1_rows[:, :, a * (H // 2):(a + 1) * (H // 2)])
+        for d, pos in enumerate((pos1, pos2, pos3, pos4)):
+            nc.sync.dma_start(pos_sb[d][:], pos)
+        nc.sync.dma_start(cen_sb[:], cen)
+        nc.sync.dma_start(w3w[:].bitcast(I32), w3_words[0].bitcast(I32))
+        nc.sync.dma_start(w2w[:].bitcast(I32), w2_words[0].bitcast(I32))
+        for r in range(4):
+            nc.sync.dma_start(ws[r:P:32, N:2 * N].bitcast(I32), w3_scales[0, r:16:4, :].bitcast(I32))
+        for r in range(4):
+            nc.sync.dma_start(ws[r:P:32, 0:N].bitcast(I32), w2_scales[0, r:16:4, :].bitcast(I32))
+
+        xg = keep.tile([P, S], U32, name="xg", align_bytes=64)
+        nc.vector.tensor_copy(xg[:], xw[:].bitcast(U32).indirect(offs_sb[:]))
+
+        def fetch_scales(tile, lo, hi):
+            nc.vector.tensor_copy(tile, xs[:].indirect(offs_sb[:, lo // 16:hi // 16]))
+
+        sg = keep.tile([P, LATE], U8, name="sg", align_bytes=64)
+        fetch_scales(sg[:, 0:BANK], 0, BANK)
+        fetch_scales(sg[:, BANK:LATE], BANK, LATE)
+
+        w1g0 = keep.tile([P, PACK * P], BF16, name="w1g0", tag="shared", align_bytes=64)
+        w1g = keep.tile([P, (PACK - 1) * PACK * P], BF16, name="w1g", align_bytes=64)
+        w1c = keep.tile([P, H], U32, name="w1c", align_bytes=64)
+        w1s = keep.tile([P, H], U8, name="w1s", align_bytes=64)
+        for a in range(2):
+            ms = slice(a * (P // 2), (a + 1) * (P // 2))
+            raw = w1_raw[a][:].rearrange("p j (m t) -> p m t j", t=PACK)
+            nc.scalar.activation(w1g0[:].rearrange("p (m j) -> p m j", j=PACK)[:, ms, :], raw[:, :, 0, :], COPY)
+            nc.scalar.activation(
+                w1g[:].rearrange("p (t m j) -> p m t j", t=PACK - 1, j=PACK)[:, ms, :, :], raw[:, :, 1:PACK, :], COPY
+            )
+        nc.vector.quantize_mx(out=w1c[:, 0:P].bitcast(FP8X4), scales=w1s[:, 0:P], in_=w1g0[:])
+        sg_late = keep.tile([P, S - LATE], U8, name="sg_late", tag="shared", align_bytes=64)
+        fetch_scales(sg_late[:], LATE, S)
+        nc.vector.quantize_mx(out=w1c[:, P:2 * P].bitcast(FP8X4), scales=w1s[:, P:2 * P], in_=w1g[:, 0:PACK * P])
+        nc.vector.quantize_mx(out=w1c[:, 2 * P:H].bitcast(FP8X4), scales=w1s[:, 2 * P:H], in_=w1g[:, PACK * P:3 * PACK * P])
+
+        h = [keep.tile([P, S], F32, name=f"h{t}", align_bytes=64) for t in range(PACK)]
+        pieces = ((0, BANK, sg[:, 0:BANK]), (BANK, LATE, sg[:, BANK:LATE]), (LATE, S, sg_late[:]))
+        for t in range(PACK):
+            for lo, hi, scales in pieces:
+                acc = psum_h.tile([P, hi - lo], F32, name="acc")
+                nc.tensor.matmul_mx(
+                    out=acc[:],
+                    lhsT=w1c[:, t * P:(t + 1) * P].bitcast(FP8X4),
+                    lhsT_scale=w1s[:, t * P:(t + 1) * P],
+                    rhs=xg[:, lo:hi].bitcast(FP8X4),
+                    rhs_scale=scales,
+                    start=True,
+                    stop=True,
+                )
+                if t == 0 and hi == S:
+                    nc.vector.tensor_scalar_max(h[t][:, lo:hi], acc[:], 0.0)
+                else:
+                    nc.scalar.activation(h[t][:, lo:hi], acc[:], RELU)
+
+        g = keep.tile([P, PACK, V], BF16, name="g", align_bytes=64)
+        m2 = keep.tile([P, V], BF16, name="m2", align_bytes=64)
+        m3 = keep.tile([P, V], BF16, name="m3", align_bytes=64)
+        z = keep.tile([P, PACK, V], BF16, name="z", align_bytes=64)
+
+        def fetch_pos(t, d):
+            nc.vector.tensor_copy(g[:, d, :], h[t][:].indirect(pos_sb[d][:]))
+
+        def fetch_cen(t, lo, hi):
+            nc.vector.tensor_copy(g[:, t, lo:hi], h[t][:].indirect(cen_sb[:, lo // 16:hi // 16]))
+
+        fetch_pos(0, 0)
+        for t in range(PACK):
+            fetch_pos(t, 1)
+            fetch_pos(t, 2)
+            nc.vector.tensor_tensor(m2[:], g[:, 0, :], g[:, 1, :], MAX)
+            fetch_pos(t, 3)
+            nc.vector.tensor_tensor(m3[:], m2[:], g[:, 2, :], MAX)
+            if t + 1 < PACK:
+                fetch_pos(t + 1, 0)
+            else:
+                fetch_cen(0, 0, EARLY)
+            nc.vector.tensor_tensor(z[:, t, :], m3[:], g[:, 3, :], MAX)
+
+        zi = keep.tile([P, V * PACK], BF16, name="zi", align_bytes=64)
+        zc = keep.tile([P, V], U32, name="zc", align_bytes=64)
+        zs = keep.tile([P, V], U8, name="zs", align_bytes=64)
+        nc.scalar.copy(
+            zi[:].rearrange("p (c i t) -> p c t i", i=4, t=PACK),
+            z[:].rearrange("p t (c i) -> p c t i", i=4),
+        )
+        for t in range(1, PACK):
+            fetch_cen(t, 0, EARLY)
+
+        ci_a = keep.tile([P, EARLY * PACK], BF16, name="ci_a", align_bytes=64)
+        ci_b = keep.tile([P, (V - EARLY) * PACK], BF16, name="ci_b", align_bytes=64)
+        cc = keep.tile([P, V], U32, name="cc", align_bytes=64)
+        cs = keep.tile([P, V], U8, name="cs", align_bytes=64)
+        nc.scalar.copy(
+            ci_a[:].rearrange("p (c i t) -> p c t i", i=4, t=PACK),
+            g[:, :, 0:EARLY].rearrange("p t (c i) -> p c t i", i=4),
+        )
+        for t in range(PACK):
+            fetch_cen(t, EARLY, V)
+        nc.vector.quantize_mx(out=zc[:].bitcast(FP8X4), scales=zs[:], in_=zi[:])
+        nc.vector.tensor_copy(
+            ci_b[:].rearrange("p (c i t) -> p c t i", i=4, t=PACK),
+            g[:, :, EARLY:V].rearrange("p t (c i) -> p c t i", i=4),
+        )
+        nc.vector.quantize_mx(out=cc[:, 0:256].bitcast(FP8X4), scales=cs[:, 0:256], in_=ci_a[:, 0:1024])
+        nc.vector.quantize_mx(out=cc[:, 256:EARLY].bitcast(FP8X4), scales=cs[:, 256:EARLY], in_=ci_a[:, 1024:EARLY * PACK])
+        nc.vector.quantize_mx(out=cc[:, EARLY:V].bitcast(FP8X4), scales=cs[:, EARLY:V], in_=ci_b[:])
+
+        res = [keep.tile([P, GROUP], F32, name=f"res{q}", align_bytes=64) for q in range(V // GROUP)]
+        acc_o = [psum_o.tile([P, GROUP], F32, name=f"acc_o{q}") for q in range(V // GROUP)]
+        for q in range(V // GROUP):
+            cols = slice(q * GROUP, (q + 1) * GROUP)
+            nc.tensor.matmul_mx(
+                out=acc_o[q][:], lhsT=w3w[:].bitcast(FP4X4), lhsT_scale=ws[:, N:2 * N],
+                rhs=zc[:, cols].bitcast(FP8X4), rhs_scale=zs[:, cols], start=True, stop=False,
+            )
+        for q in range(V // GROUP):
+            cols = slice(q * GROUP, (q + 1) * GROUP)
+            nc.tensor.matmul_mx(
+                out=acc_o[q][:], lhsT=w2w[:].bitcast(FP4X4), lhsT_scale=ws[:, 0:N],
+                rhs=cc[:, cols].bitcast(FP8X4), rhs_scale=cs[:, cols], start=False, stop=True,
+            )
+            if q != 2:
+                nc.scalar.activation(res[q][:], acc_o[q][:], RELU)
+            else:
+                nc.vector.tensor_scalar_max(res[q][:], acc_o[q][:], 0.0)
+            nc.sync.dma_start(out[:, cols], res[q][:])

@@ -49,13 +49,13 @@ def tile_picked_sagecat_maxrelu_p_kernel(
         nc.vector.memset(xs[:].bitcast(I32), 0)
         nc.vector.memset(ws[:].bitcast(I32), 0)
 
+        w1_rows = w1.rearrange("(p j) c -> p j c", j=PACK)
         nc.sync.dma_start(offs_sb[:], offs)
-        nc.sync.dma_start(xw[:], x_words[0].rearrange("p n r -> p (n r)").bitcast(I32))
+        nc.sync.dma_start(w1_raw[0][:], w1_rows[:, :, 0:H // 2])
         for r in range(4):
             nc.sync.dma_start(xs[r:P:32, :].bitcast(I32), x_scales[0, r:16:4, :].bitcast(I32))
-        w1_rows = w1.rearrange("(p j) c -> p j c", j=PACK)
-        for a in range(2):
-            nc.sync.dma_start(w1_raw[a][:], w1_rows[:, :, a * (H // 2):(a + 1) * (H // 2)])
+        nc.sync.dma_start(xw[:], x_words[0].rearrange("p n r -> p (n r)").bitcast(I32))
+        nc.sync.dma_start(w1_raw[1][:], w1_rows[:, :, H // 2:H])
         for d, pos in enumerate((pos1, pos2, pos3, pos4)):
             nc.sync.dma_start(pos_sb[d][:], pos)
         nc.sync.dma_start(cen_sb[:], cen)
@@ -66,15 +66,14 @@ def tile_picked_sagecat_maxrelu_p_kernel(
         for r in range(4):
             nc.sync.dma_start(ws[r:P:32, 0:N].bitcast(I32), w2_scales[0, r:16:4, :].bitcast(I32))
 
-        xg = keep.tile([P, S], U32, name="xg", align_bytes=64)
-        nc.vector.tensor_copy(xg[:], xw[:].bitcast(U32).indirect(offs_sb[:]))
+        sg = keep.tile([P, S], U8, name="sg", align_bytes=64)
+        nc.vector.tensor_copy(sg[:], xs[:].indirect(offs_sb[:]))
 
-        def fetch_scales(tile, lo, hi):
-            nc.vector.tensor_copy(tile, xs[:].indirect(offs_sb[:, lo // 16:hi // 16]))
+        def fetch_words(tile, lo, hi):
+            nc.vector.tensor_copy(tile, xw[:].bitcast(U32).indirect(offs_sb[:, lo // 16:hi // 16]))
 
-        sg = keep.tile([P, LATE], U8, name="sg", align_bytes=64)
-        fetch_scales(sg[:, 0:BANK], 0, BANK)
-        fetch_scales(sg[:, BANK:LATE], BANK, LATE)
+        xg = keep.tile([P, LATE], U32, name="xg", align_bytes=64)
+        fetch_words(xg[:], 0, LATE)
 
         w1g0 = keep.tile([P, PACK * P], BF16, name="w1g0", tag="shared", align_bytes=64)
         w1g = keep.tile([P, (PACK - 1) * PACK * P], BF16, name="w1g", align_bytes=64)
@@ -88,26 +87,26 @@ def tile_picked_sagecat_maxrelu_p_kernel(
                 w1g[:].rearrange("p (t m j) -> p m t j", t=PACK - 1, j=PACK)[:, ms, :, :], raw[:, :, 1:PACK, :], COPY
             )
         nc.vector.quantize_mx(out=w1c[:, 0:P].bitcast(FP8X4), scales=w1s[:, 0:P], in_=w1g0[:])
-        sg_late = keep.tile([P, S - LATE], U8, name="sg_late", tag="shared", align_bytes=64)
-        fetch_scales(sg_late[:], LATE, S)
+        xg_late = keep.tile([P, S - LATE], U32, name="xg_late", tag="shared", align_bytes=64)
+        fetch_words(xg_late[:], LATE, S)
         nc.vector.quantize_mx(out=w1c[:, P:2 * P].bitcast(FP8X4), scales=w1s[:, P:2 * P], in_=w1g[:, 0:PACK * P])
         nc.vector.quantize_mx(out=w1c[:, 2 * P:H].bitcast(FP8X4), scales=w1s[:, 2 * P:H], in_=w1g[:, PACK * P:3 * PACK * P])
 
         h = [keep.tile([P, S], F32, name=f"h{t}", align_bytes=64) for t in range(PACK)]
-        pieces = ((0, BANK, sg[:, 0:BANK]), (BANK, LATE, sg[:, BANK:LATE]), (LATE, S, sg_late[:]))
+        pieces = ((0, BANK, xg[:, 0:BANK]), (BANK, LATE, xg[:, BANK:LATE]), (LATE, S, xg_late[:]))
         for t in range(PACK):
-            for lo, hi, scales in pieces:
+            for lo, hi, words in pieces:
                 acc = psum_h.tile([P, hi - lo], F32, name="acc")
                 nc.tensor.matmul_mx(
                     out=acc[:],
                     lhsT=w1c[:, t * P:(t + 1) * P].bitcast(FP8X4),
                     lhsT_scale=w1s[:, t * P:(t + 1) * P],
-                    rhs=xg[:, lo:hi].bitcast(FP8X4),
-                    rhs_scale=scales,
+                    rhs=words.bitcast(FP8X4),
+                    rhs_scale=sg[:, lo:hi],
                     start=True,
                     stop=True,
                 )
-                if t == 0 and hi == S:
+                if t == 0 and lo == BANK:
                     nc.vector.tensor_scalar_max(h[t][:, lo:hi], acc[:], 0.0)
                 else:
                     nc.scalar.activation(h[t][:, lo:hi], acc[:], RELU)

@@ -122,6 +122,14 @@ def tile_picked_sagecat_maxrelu_p_kernel(
         def fetch_cen(t, lo, hi):
             nc.vector.tensor_copy(g[:, t, lo:hi], h[t][:].indirect(cen_sb[:, lo // 16:hi // 16]))
 
+        stage = keep.tile([P, (EARLY + V) * PACK], BF16, name="stage", align_bytes=64)
+        ci = stage[:, 0:V * PACK]
+        zi = stage[:, EARLY * PACK:(EARLY + V) * PACK]
+        zc = keep.tile([P, V], U32, name="zc", align_bytes=64)
+        zs = keep.tile([P, V], U8, name="zs", align_bytes=64)
+        cc = keep.tile([P, V], U32, name="cc", align_bytes=64)
+        cs = keep.tile([P, V], U8, name="cs", align_bytes=64)
+
         fetch_pos(0, 0)
         for t in range(PACK):
             fetch_pos(t, 1)
@@ -134,37 +142,31 @@ def tile_picked_sagecat_maxrelu_p_kernel(
             else:
                 fetch_cen(0, 0, EARLY)
             nc.vector.tensor_tensor(z[:, t, :], m3[:], g[:, 3, :], MAX)
-
-        zi = keep.tile([P, V * PACK], BF16, name="zi", align_bytes=64)
-        zc = keep.tile([P, V], U32, name="zc", align_bytes=64)
-        zs = keep.tile([P, V], U8, name="zs", align_bytes=64)
-        nc.scalar.copy(
-            zi[:].rearrange("p (c i t) -> p c t i", i=4, t=PACK),
-            z[:].rearrange("p t (c i) -> p c t i", i=4),
-        )
+            if t % 2 == 1:
+                nc.scalar.copy(
+                    zi.rearrange("p (v t) -> p v t", t=PACK)[:, :, t - 1:t + 1],
+                    z[:, t - 1:t + 1, :].rearrange("p t v -> p v t"),
+                )
         for t in range(1, PACK):
             fetch_cen(t, 0, EARLY)
-
-        ci_a = keep.tile([P, EARLY * PACK], BF16, name="ci_a", align_bytes=64)
-        ci_b = keep.tile([P, (V - EARLY) * PACK], BF16, name="ci_b", align_bytes=64)
-        cc = keep.tile([P, V], U32, name="cc", align_bytes=64)
-        cs = keep.tile([P, V], U8, name="cs", align_bytes=64)
         nc.scalar.copy(
-            ci_a[:].rearrange("p (c i t) -> p c t i", i=4, t=PACK),
+            ci[:, 0:EARLY * PACK].rearrange("p (c i t) -> p c t i", i=4, t=PACK),
             g[:, :, 0:EARLY].rearrange("p t (c i) -> p c t i", i=4),
         )
+        nc.vector.quantize_mx(out=zc[:].bitcast(FP8X4), scales=zs[:], in_=zi)
         for t in range(PACK):
-            fetch_cen(t, EARLY, V)
-        nc.vector.quantize_mx(out=zc[:].bitcast(FP8X4), scales=zs[:], in_=zi[:])
-        nc.vector.tensor_copy(
-            ci_b[:].rearrange("p (c i t) -> p c t i", i=4, t=PACK),
-            g[:, :, EARLY:V].rearrange("p t (c i) -> p c t i", i=4),
-        )
-        nc.vector.quantize_mx(out=cc[:, 0:256].bitcast(FP8X4), scales=cs[:, 0:256], in_=ci_a[:, 0:1024])
-        nc.vector.quantize_mx(out=cc[:, 256:EARLY].bitcast(FP8X4), scales=cs[:, 256:EARLY], in_=ci_a[:, 1024:EARLY * PACK])
-        nc.vector.quantize_mx(out=cc[:, EARLY:V].bitcast(FP8X4), scales=cs[:, EARLY:V], in_=ci_b[:])
+            nc.vector.tensor_copy(
+                ci.rearrange("p (v t) -> p v t", t=PACK)[:, EARLY:V, t],
+                h[t][:].indirect(cen_sb[:, EARLY // 16:V // 16]),
+            )
+        for half in range(2):
+            cols = slice(half * V // 2, (half + 1) * V // 2)
+            nc.vector.quantize_mx(
+                out=cc[:, cols].bitcast(FP8X4), scales=cs[:, cols],
+                in_=ci[:, half * V // 2 * PACK:(half + 1) * V // 2 * PACK],
+            )
 
-        res = [keep.tile([P, GROUP], F32, name=f"res{q}", align_bytes=64) for q in range(V // GROUP)]
+        res = [keep.tile([P, 2 * GROUP], F32, name=f"res{q}", align_bytes=64) for q in range(2)]
         acc_o = [psum_o.tile([P, GROUP], F32, name=f"acc_o{q}") for q in range(V // GROUP)]
         for q in range(V // GROUP):
             cols = slice(q * GROUP, (q + 1) * GROUP)
@@ -178,8 +180,9 @@ def tile_picked_sagecat_maxrelu_p_kernel(
                 out=acc_o[q][:], lhsT=w2w[:].bitcast(FP4X4), lhsT_scale=ws[:, 0:N],
                 rhs=cc[:, cols].bitcast(FP8X4), rhs_scale=cs[:, cols], start=False, stop=True,
             )
-            if q != 2:
-                nc.scalar.activation(res[q][:], acc_o[q][:], RELU)
+            dst = res[q // 2][:, (q % 2) * GROUP:(q % 2 + 1) * GROUP]
+            if q % 2 == 0:
+                nc.scalar.activation(dst, acc_o[q][:], RELU)
             else:
-                nc.vector.tensor_scalar_max(res[q][:], acc_o[q][:], 0.0)
-            nc.sync.dma_start(out[:, cols], res[q][:])
+                nc.vector.tensor_scalar_max(dst, acc_o[q][:], 0.0)
+                nc.sync.dma_start(out[:, (q - 1) * GROUP:(q + 1) * GROUP], res[q // 2][:])

@@ -44,18 +44,18 @@ def tile_picked_sagecat_maxrelu_p_kernel(
         ws = keep.tile([P, 2 * N], U8, name="ws", align_bytes=64)
         w2w = keep.tile([P, 2 * N], U8, name="w2w", align_bytes=64)
         w3w = keep.tile([P, 2 * N], U8, name="w3w", align_bytes=64)
-        w1_raw = [keep.tile([P, PACK, H // 2], F32, name=f"w1_raw{a}", align_bytes=64) for a in range(2)]
+        w1_raw = [keep.tile([P, 2, H], F32, name=f"w1_raw{a}", align_bytes=64) for a in range(2)]
 
         nc.vector.memset(xs[:].bitcast(I32), 0)
         nc.vector.memset(ws[:].bitcast(I32), 0)
 
         w1_rows = w1.rearrange("(p j) c -> p j c", j=PACK)
         nc.sync.dma_start(offs_sb[:], offs)
-        nc.sync.dma_start(w1_raw[0][:], w1_rows[:, :, 0:H // 2])
+        nc.sync.dma_start(w1_raw[0][:], w1_rows[:, 0:2, :])
         for r in range(4):
             nc.sync.dma_start(xs[r:P:32, :].bitcast(I32), x_scales[0, r:16:4, :].bitcast(I32))
         nc.sync.dma_start(xw[:], x_words[0].rearrange("p n r -> p (n r)").bitcast(I32))
-        nc.sync.dma_start(w1_raw[1][:], w1_rows[:, :, H // 2:H])
+        nc.sync.dma_start(w1_raw[1][:], w1_rows[:, 2:PACK, :])
         for d, pos in enumerate((pos1, pos2, pos3, pos4)):
             nc.sync.dma_start(pos_sb[d][:], pos)
         nc.sync.dma_start(cen_sb[:], cen)
@@ -80,11 +80,11 @@ def tile_picked_sagecat_maxrelu_p_kernel(
         w1c = keep.tile([P, H], U32, name="w1c", align_bytes=64)
         w1s = keep.tile([P, H], U8, name="w1s", align_bytes=64)
         for a in range(2):
-            ms = slice(a * (P // 2), (a + 1) * (P // 2))
+            js = slice(2 * a, 2 * a + 2)
             raw = w1_raw[a][:].rearrange("p j (m t) -> p m t j", t=PACK)
-            nc.scalar.activation(w1g0[:].rearrange("p (m j) -> p m j", j=PACK)[:, ms, :], raw[:, :, 0, :], COPY)
+            nc.scalar.activation(w1g0[:].rearrange("p (m j) -> p m j", j=PACK)[:, :, js], raw[:, :, 0, :], COPY)
             nc.scalar.activation(
-                w1g[:].rearrange("p (t m j) -> p m t j", t=PACK - 1, j=PACK)[:, ms, :, :], raw[:, :, 1:PACK, :], COPY
+                w1g[:].rearrange("p (t m j) -> p m t j", t=PACK - 1, j=PACK)[:, :, :, js], raw[:, :, 1:PACK, :], COPY
             )
         nc.vector.quantize_mx(out=w1c[:, 0:P].bitcast(FP8X4), scales=w1s[:, 0:P], in_=w1g0[:])
         xg_late = keep.tile([P, S - LATE], U32, name="xg_late", tag="shared", align_bytes=64)
@@ -140,25 +140,27 @@ def tile_picked_sagecat_maxrelu_p_kernel(
             if t + 1 < PACK:
                 fetch_pos(t + 1, 0)
             else:
-                fetch_cen(0, 0, EARLY)
+                fetch_cen(0, 0, V)
             nc.vector.tensor_tensor(z[:, t, :], m3[:], g[:, 3, :], MAX)
             if t % 2 == 1:
                 nc.scalar.copy(
                     zi.rearrange("p (v t) -> p v t", t=PACK)[:, :, t - 1:t + 1],
                     z[:, t - 1:t + 1, :].rearrange("p t v -> p v t"),
                 )
-        for t in range(1, PACK):
-            fetch_cen(t, 0, EARLY)
-        nc.scalar.copy(
-            ci[:, 0:EARLY * PACK].rearrange("p (c i t) -> p c t i", i=4, t=PACK),
-            g[:, :, 0:EARLY].rearrange("p t (c i) -> p c t i", i=4),
-        )
+        ci_planes = ci.rearrange("p (v t) -> p v t", t=PACK)
+
+        def interleave_cen(t0, lo, hi):
+            nc.scalar.copy(ci_planes[:, lo:hi, t0:t0 + 2], g[:, t0:t0 + 2, lo:hi].rearrange("p t v -> p v t"))
+
+        fetch_cen(1, 0, V)
+        interleave_cen(0, 0, EARLY)
+        fetch_cen(2, 0, EARLY)
+        fetch_cen(3, 0, EARLY)
+        interleave_cen(2, 0, EARLY)
         nc.vector.quantize_mx(out=zc[:].bitcast(FP8X4), scales=zs[:], in_=zi)
-        for t in range(PACK):
-            nc.vector.tensor_copy(
-                ci.rearrange("p (v t) -> p v t", t=PACK)[:, EARLY:V, t],
-                h[t][:].indirect(cen_sb[:, EARLY // 16:V // 16]),
-            )
+        interleave_cen(0, EARLY, V)
+        for t in range(2, PACK):
+            nc.vector.tensor_copy(ci_planes[:, EARLY:V, t], h[t][:].indirect(cen_sb[:, EARLY // 16:V // 16]))
         for half in range(2):
             cols = slice(half * V // 2, (half + 1) * V // 2)
             nc.vector.quantize_mx(

@@ -14,6 +14,8 @@ U8 = mybir.dt.uint8
 FP8X4 = mybir.dt.float8_e4m3fn_x4
 FP4X4 = mybir.dt.float4_e2m1fn_x4
 MAX = mybir.AluOpType.max
+SUB = mybir.AluOpType.subtract
+ADD = mybir.AluOpType.add
 RELU = mybir.ActivationFunctionType.Relu
 COPY = mybir.ActivationFunctionType.Copy
 
@@ -111,42 +113,60 @@ def tile_picked_sagecat_maxrelu_p_kernel(
                 else:
                     nc.scalar.activation(h[t][:, lo:hi], acc[:], RELU)
 
-        g = keep.tile([P, PACK, V], BF16, name="g", align_bytes=64)
-        m2 = keep.tile([P, V], BF16, name="m2", align_bytes=64)
-        m3 = keep.tile([P, V], BF16, name="m3", align_bytes=64)
+        ga = keep.tile([P, PACK, 2, V], BF16, name="ga", align_bytes=64)
+        gb = keep.tile([P, PACK, 2, V], BF16, name="gb", align_bytes=64)
+        g = gb[:, :, 0, :]
+        m2 = keep.tile([P, 2, V], BF16, name="m2", align_bytes=64)
+        m3 = keep.tile([P, 2, V], BF16, name="m3", align_bytes=64)
         z = keep.tile([P, PACK, V], BF16, name="z", align_bytes=64)
 
         def fetch_pos(t, d):
-            nc.vector.tensor_copy(g[:, d, :], h[t][:].indirect(pos_sb[d][:]))
+            nc.vector.tensor_copy((ga, gb)[t // 2][:, d, t % 2, :], h[t][:].indirect(pos_sb[d][:]))
 
         def fetch_cen(t, lo, hi):
             nc.vector.tensor_copy(g[:, t, lo:hi], h[t][:].indirect(cen_sb[:, lo // 16:hi // 16]))
 
+        def side_max(dst, a, b, name, diff=None):
+            rise = keep.tile([P, V], F32, name=f"rise{name}", align_bytes=64)
+            if diff is None:
+                diff = keep.tile([P, V], F32, name=f"diff{name}", align_bytes=64)[:]
+            nc.gpsimd.tensor_tensor(diff, b, a, SUB)
+            nc.scalar.activation(rise[:], diff, RELU)
+            nc.gpsimd.tensor_tensor(dst, rise[:], a, ADD)
+
         stage = keep.tile([P, (EARLY + V) * PACK], BF16, name="stage", align_bytes=64)
         ci = stage[:, 0:V * PACK]
         zi = stage[:, EARLY * PACK:(EARLY + V) * PACK]
+        last_diff = stage[:, EARLY * PACK - V:EARLY * PACK + V].bitcast(F32)
         zc = keep.tile([P, V], U32, name="zc", align_bytes=64)
         zs = keep.tile([P, V], U8, name="zs", align_bytes=64)
         cc = keep.tile([P, V], U32, name="cc", align_bytes=64)
         cs = keep.tile([P, V], U8, name="cs", align_bytes=64)
 
-        fetch_pos(0, 0)
-        for t in range(PACK):
-            fetch_pos(t, 1)
-            fetch_pos(t, 2)
-            nc.vector.tensor_tensor(m2[:], g[:, 0, :], g[:, 1, :], MAX)
-            fetch_pos(t, 3)
-            nc.vector.tensor_tensor(m3[:], m2[:], g[:, 2, :], MAX)
-            if t + 1 < PACK:
-                fetch_pos(t + 1, 0)
-            else:
-                fetch_cen(0, 0, V)
-            nc.vector.tensor_tensor(z[:, t, :], m3[:], g[:, 3, :], MAX)
-            if t % 2 == 1:
-                nc.scalar.copy(
-                    zi.rearrange("p (v t) -> p v t", t=PACK)[:, :, t - 1:t + 1],
-                    z[:, t - 1:t + 1, :].rearrange("p t v -> p v t"),
-                )
+        def interleave_z(t0):
+            nc.scalar.copy(
+                zi.rearrange("p (v t) -> p v t", t=PACK)[:, :, t0:t0 + 2],
+                z[:, t0:t0 + 2, :].rearrange("p t v -> p v t"),
+            )
+
+        for t in range(2):
+            for d in range(4):
+                fetch_pos(t, d)
+            pair = keep.tile([P, 2, V], BF16, name=f"pair{t}", align_bytes=64)
+            side_max(pair[:, 0, :], ga[:, 0, t, :], ga[:, 1, t, :], f"{t}a")
+            side_max(pair[:, 1, :], ga[:, 2, t, :], ga[:, 3, t, :], f"{t}b")
+            side_max(z[:, t, :], pair[:, 0, :], pair[:, 1, :], f"{t}c", last_diff if t == 1 else None)
+        interleave_z(0)
+        for d in range(4):
+            fetch_pos(2, d)
+        for d in range(3):
+            fetch_pos(3, d)
+        nc.vector.tensor_tensor(m2[:], gb[:, 0], gb[:, 1], MAX)
+        fetch_pos(3, 3)
+        nc.vector.tensor_tensor(m3[:], m2[:], gb[:, 2], MAX)
+        fetch_cen(0, 0, V)
+        nc.vector.tensor_tensor(z[:, 2:4, :], m3[:], gb[:, 3], MAX)
+        interleave_z(2)
         ci_planes = ci.rearrange("p (v t) -> p v t", t=PACK)
 
         def interleave_cen(t0, lo, hi):

@@ -1,6 +1,7 @@
 from contextlib import ExitStack
 
 import concourse.mybir as mybir
+from concourse.masks import make_identity
 
 K, T, S, V, H, N = 512, 2048, 1024, 512, 512, 128
 FLOPS = 2 * K * H * S + 2 * 2 * H * N * V
@@ -34,8 +35,9 @@ def tile_picked_sagecat_maxrelu_p_kernel(
     with ExitStack() as ctx:
         lists = ctx.enter_context(tc.tile_pool(name="lists", bufs=1))
         keep = ctx.enter_context(tc.tile_pool(name="keep", bufs=1))
-        psum_h = ctx.enter_context(tc.psum_pool(name="psum_h", bufs=4))
-        psum_o = ctx.enter_context(tc.psum_pool(name="psum_o", bufs=1))
+        psum = ctx.enter_context(tc.psum_pool(name="psum", bufs=4))
+        psum_turn = ctx.enter_context(tc.psum_pool(name="psum_turn", bufs=2))
+        psum_z = ctx.enter_context(tc.psum_pool(name="psum_z", bufs=1))
 
         offs_sb = lists.tile([P, S // 16], U16, name="offs_sb")
         cen_sb = lists.tile([P, V // 16], U16, name="cen_sb")
@@ -50,6 +52,9 @@ def tile_picked_sagecat_maxrelu_p_kernel(
 
         nc.vector.memset(xs[:].bitcast(I32), 0)
         nc.vector.memset(ws[:].bitcast(I32), 0)
+
+        ident = keep.tile([P, P], F32, name="ident", align_bytes=64)
+        make_identity(nc, ident[:])
 
         w1_rows = w1.rearrange("(p j) c -> p j c", j=PACK)
         nc.sync.dma_start(offs_sb[:], offs)
@@ -79,7 +84,8 @@ def tile_picked_sagecat_maxrelu_p_kernel(
 
         w1g0 = keep.tile([P, PACK * P], BF16, name="w1g0", tag="shared", align_bytes=64)
         w1g = keep.tile([P, (PACK - 1) * PACK * P], BF16, name="w1g", align_bytes=64)
-        w1c = keep.tile([P, H], U32, name="w1c", align_bytes=64)
+        w1c = keep.tile([P, 2 * P], U32, name="w1c", align_bytes=64)
+        w1c_late = keep.tile([P, 2 * P], U32, name="w1c_late", align_bytes=64)
         w1s = keep.tile([P, H], U8, name="w1s", align_bytes=64)
         for a in range(2):
             js = slice(2 * a, 2 * a + 2)
@@ -92,16 +98,16 @@ def tile_picked_sagecat_maxrelu_p_kernel(
         xg_late = keep.tile([P, S - LATE], U32, name="xg_late", tag="shared", align_bytes=64)
         fetch_words(xg_late[:], LATE, S)
         nc.vector.quantize_mx(out=w1c[:, P:2 * P].bitcast(FP8X4), scales=w1s[:, P:2 * P], in_=w1g[:, 0:PACK * P])
-        nc.vector.quantize_mx(out=w1c[:, 2 * P:H].bitcast(FP8X4), scales=w1s[:, 2 * P:H], in_=w1g[:, PACK * P:3 * PACK * P])
+        nc.vector.quantize_mx(out=w1c_late[:].bitcast(FP8X4), scales=w1s[:, 2 * P:H], in_=w1g[:, PACK * P:3 * PACK * P])
 
         h = [keep.tile([P, S], F32, name=f"h{t}", align_bytes=64) for t in range(PACK)]
         pieces = ((0, BANK, xg[:, 0:BANK]), (BANK, LATE, xg[:, BANK:LATE]), (LATE, S, xg_late[:]))
         for t in range(PACK):
             for lo, hi, words in pieces:
-                acc = psum_h.tile([P, hi - lo], F32, name="acc")
+                acc = psum.tile([P, hi - lo], F32, name="acc", tag="bank")
                 nc.tensor.matmul_mx(
                     out=acc[:],
-                    lhsT=w1c[:, t * P:(t + 1) * P].bitcast(FP8X4),
+                    lhsT=(w1c, w1c_late)[t // 2][:, t % 2 * P:(t % 2 + 1) * P].bitcast(FP8X4),
                     lhsT_scale=w1s[:, t * P:(t + 1) * P],
                     rhs=words.bitcast(FP8X4),
                     rhs_scale=sg[:, lo:hi],
@@ -113,98 +119,125 @@ def tile_picked_sagecat_maxrelu_p_kernel(
                 else:
                     nc.scalar.activation(h[t][:, lo:hi], acc[:], RELU)
 
-        ga = keep.tile([P, PACK, 2, V], BF16, name="ga", align_bytes=64)
-        gb = keep.tile([P, PACK, 2, V], BF16, name="gb", align_bytes=64)
-        g = gb[:, :, 0, :]
-        m2 = keep.tile([P, 2, V], BF16, name="m2", align_bytes=64)
-        m3 = keep.tile([P, 2, V], BF16, name="m3", align_bytes=64)
-        z = keep.tile([P, PACK, V], BF16, name="z", align_bytes=64)
-
-        def fetch_pos(t, d):
-            nc.vector.tensor_copy((ga, gb)[t // 2][:, d, t % 2, :], h[t][:].indirect(pos_sb[d][:]))
-
-        def fetch_cen(t, lo, hi):
-            nc.vector.tensor_copy(g[:, t, lo:hi], h[t][:].indirect(cen_sb[:, lo // 16:hi // 16]))
-
-        def side_max(dst, a, b, name, diff=None):
-            rise = keep.tile([P, V], F32, name=f"rise{name}", align_bytes=64)
-            if diff is None:
-                diff = keep.tile([P, V], F32, name=f"diff{name}", align_bytes=64)[:]
-            nc.gpsimd.tensor_tensor(diff, b, a, SUB)
-            nc.scalar.activation(rise[:], diff, RELU)
-            nc.gpsimd.tensor_tensor(dst, rise[:], a, ADD)
-
-        stage = keep.tile([P, (EARLY + V) * PACK], BF16, name="stage", align_bytes=64)
-        ci = stage[:, 0:V * PACK]
-        zi = stage[:, EARLY * PACK:(EARLY + V) * PACK]
-        last_diff = stage[:, EARLY * PACK - V:EARLY * PACK + V].bitcast(F32)
+        zi = keep.tile([P, V * PACK], BF16, name="zi", align_bytes=64)
         zc = keep.tile([P, V], U32, name="zc", align_bytes=64)
         zs = keep.tile([P, V], U8, name="zs", align_bytes=64)
         cc = keep.tile([P, V], U32, name="cc", align_bytes=64)
         cs = keep.tile([P, V], U8, name="cs", align_bytes=64)
+        zi_planes = zi[:].rearrange("p (v t) -> p v t", t=PACK)
 
-        def interleave_z(t0):
-            nc.scalar.copy(
-                zi.rearrange("p (v t) -> p v t", t=PACK)[:, :, t0:t0 + 2],
-                z[:, t0:t0 + 2, :].rearrange("p t v -> p v t"),
-            )
+        def fetch(dst, t, offsets):
+            nc.vector.tensor_copy(dst, h[t][:].indirect(offsets))
 
+        def wide_tile(name, tag=None):
+            return keep.tile([P, V], F32, name=name, tag=tag or name, align_bytes=64)[:]
+
+        def excess(a, b, name, tag=None, rise=None):
+            diff = wide_tile(f"diff{name}", tag)
+            if rise is None:
+                rise = wide_tile(f"rise{name}")
+            nc.gpsimd.tensor_tensor(diff, b, a, SUB)
+            nc.scalar.activation(rise, diff, RELU)
+            return rise
+
+        def add_turned(dst, first, second, blocks):
+            terms = [(src, b) for src in (first, second) for b in blocks]
+            for i, (src, b) in enumerate(terms):
+                col = (b - blocks[0]) * P
+                nc.tensor.matmul(
+                    dst[:, col:col + P], src[:, b * P:(b + 1) * P], ident[:],
+                    start=i == 0, stop=i == len(terms) - 1, is_transpose=True,
+                )
+
+        def larger_turned(a, b, name):
+            rise = excess(a, b, name)
+            bank = psum_turn.tile([P, V], F32, name=f"turn{name}", tag="turn")
+            add_turned(bank[:], a, rise, (0, 1, 2, 3))
+            turned = wide_tile(f"turned{name}")
+            nc.scalar.copy(turned, bank[:])
+            return turned
+
+        def weave(planes, t0, src, lo, hi):
+            nc.scalar.copy(planes[:, lo:hi, t0:t0 + 2], src.rearrange("p t v -> p v t"))
+
+        nb = [[wide_tile(f"nb{t}{d}") for d in range(4)] for t in range(3)]
+        halves = []
         for t in range(2):
             for d in range(4):
-                fetch_pos(t, d)
-            pair = keep.tile([P, 2, V], BF16, name=f"pair{t}", align_bytes=64)
-            side_max(pair[:, 0, :], ga[:, 0, t, :], ga[:, 1, t, :], f"{t}a")
-            side_max(pair[:, 1, :], ga[:, 2, t, :], ga[:, 3, t, :], f"{t}b")
-            side_max(z[:, t, :], pair[:, 0, :], pair[:, 1, :], f"{t}c", last_diff if t == 1 else None)
-        interleave_z(0)
+                fetch(nb[t][d], t, pos_sb[d][:])
+            halves.append([larger_turned(nb[t][2 * e], nb[t][2 * e + 1], f"{t}{e}") for e in range(2)])
         for d in range(4):
-            fetch_pos(2, d)
-        for d in range(3):
-            fetch_pos(3, d)
-        nc.vector.tensor_tensor(m2[:], gb[:, 0], gb[:, 1], MAX)
-        fetch_pos(3, 3)
-        nc.vector.tensor_tensor(m3[:], m2[:], gb[:, 2], MAX)
-        fetch_cen(0, 0, V)
-        nc.vector.tensor_tensor(z[:, 2:4, :], m3[:], gb[:, 3], MAX)
-        interleave_z(2)
+            fetch(nb[2][d], 2, pos_sb[d][:])
+
+        stage = keep.tile([P, 13 * V], BF16, name="stage", tag="nb11", align_bytes=64)
+        ci = stage[:, 0:PACK * V]
         ci_planes = ci.rearrange("p (v t) -> p v t", t=PACK)
+        cen23 = stage[:, 4 * V:6 * V].rearrange("p (t v) -> p t v", t=2)
+        cen01 = stage[:, 6 * V:8 * V].rearrange("p (t v) -> p t v", t=2)
+        g3 = stage[:, 8 * V:11 * V].rearrange("p (d v) -> p d v", d=3)
+        right = stage[:, 11 * V:13 * V].rearrange("p (t v) -> p t v", t=2)
+        last_rise = stage[:, 4 * V - V // 2:6 * V - V // 2].bitcast(F32)
+        left = keep.tile([P, 2, V], BF16, name="left", align_bytes=64)
+        m2 = keep.tile([P, V], BF16, name="m2", align_bytes=64)
+        z23 = keep.tile([P, 2, V], BF16, name="z23", align_bytes=64)
+        z01 = [psum_z.tile([P, 2, V // 2], F32, name=f"z01_{half}") for half in range(2)]
 
-        def interleave_cen(t0, lo, hi):
-            nc.scalar.copy(ci_planes[:, lo:hi, t0:t0 + 2], g[:, t0:t0 + 2, lo:hi].rearrange("p t v -> p v t"))
+        def turn_back(t):
+            rise = excess(halves[t][0], halves[t][1], f"{t}z")
+            for half in range(2):
+                add_turned(z01[half][:, t, :], halves[t][0], rise, (2 * half, 2 * half + 1))
 
-        fetch_cen(1, 0, V)
-        interleave_cen(0, 0, EARLY)
-        fetch_cen(2, 0, EARLY)
-        fetch_cen(3, 0, EARLY)
-        interleave_cen(2, 0, EARLY)
-        nc.vector.quantize_mx(out=zc[:].bitcast(FP8X4), scales=zs[:], in_=zi)
-        interleave_cen(0, EARLY, V)
-        for t in range(2, PACK):
-            nc.vector.tensor_copy(ci_planes[:, EARLY:V, t], h[t][:].indirect(cen_sb[:, EARLY // 16:V // 16]))
+        turn_back(0)
+        rise_ab = excess(nb[2][0], nb[2][1], "20", tag="turned01")
+        rise_cd = excess(nb[2][2], nb[2][3], "21", tag="nb21", rise=last_rise)
+        nc.gpsimd.tensor_tensor(left[:, 0, :], rise_ab, nb[2][0], ADD)
+        turn_back(1)
+        nc.gpsimd.tensor_tensor(right[:, 0, :], rise_cd, nb[2][2], ADD)
+        for half in range(2):
+            weave(zi_planes, 0, z01[half][:], half * V // 2, (half + 1) * V // 2)
+
+        for t in range(2):
+            fetch(cen01[:, t, :], t, cen_sb[:])
+        weave(ci_planes, 0, cen01, 0, V)
+        for d in range(3):
+            fetch(g3[:, d, :], 3, pos_sb[d][:])
+        nc.vector.tensor_tensor(m2[:], g3[:, 0, :], g3[:, 1, :], MAX)
+        fetch(right[:, 1, :], 3, pos_sb[3][:])
+        nc.vector.tensor_tensor(left[:, 1, :], m2[:], g3[:, 2, :], MAX)
+        fetch(ci_planes[:, EARLY:V, 3], 3, cen_sb[:, EARLY // 16:V // 16])
+        nc.vector.tensor_tensor(z23[:], left[:], right, MAX)
         for half in range(2):
             cols = slice(half * V // 2, (half + 1) * V // 2)
-            nc.vector.quantize_mx(
-                out=cc[:, cols].bitcast(FP8X4), scales=cs[:, cols],
-                in_=ci[:, half * V // 2 * PACK:(half + 1) * V // 2 * PACK],
-            )
+            weave(zi_planes, 2, z23[:, :, cols], cols.start, cols.stop)
+        for t in (3, 2):
+            fetch(cen23[:, t - 2, 0:EARLY], t, cen_sb[:, 0:EARLY // 16])
+        weave(ci_planes, 2, cen23[:, :, 0:V // 2], 0, V // 2)
+        weave(ci_planes, 2, cen23[:, :, V // 2:EARLY], V // 2, EARLY)
+        fetch(ci_planes[:, EARLY:V, 2], 2, cen_sb[:, EARLY // 16:V // 16])
+        for half in range(2):
+            cols = slice(half * V // 2, (half + 1) * V // 2)
+            wide = slice(half * V // 2 * PACK, (half + 1) * V // 2 * PACK)
+            nc.vector.quantize_mx(out=zc[:, cols].bitcast(FP8X4), scales=zs[:, cols], in_=zi[:, wide])
+            nc.vector.quantize_mx(out=cc[:, cols].bitcast(FP8X4), scales=cs[:, cols], in_=ci[:, wide])
 
         res = [keep.tile([P, 2 * GROUP], F32, name=f"res{q}", align_bytes=64) for q in range(2)]
-        acc_o = [psum_o.tile([P, GROUP], F32, name=f"acc_o{q}") for q in range(V // GROUP)]
-        for q in range(V // GROUP):
-            cols = slice(q * GROUP, (q + 1) * GROUP)
-            nc.tensor.matmul_mx(
-                out=acc_o[q][:], lhsT=w3w[:].bitcast(FP4X4), lhsT_scale=ws[:, N:2 * N],
-                rhs=zc[:, cols].bitcast(FP8X4), rhs_scale=zs[:, cols], start=True, stop=False,
-            )
-        for q in range(V // GROUP):
-            cols = slice(q * GROUP, (q + 1) * GROUP)
-            nc.tensor.matmul_mx(
-                out=acc_o[q][:], lhsT=w2w[:].bitcast(FP4X4), lhsT_scale=ws[:, 0:N],
-                rhs=cc[:, cols].bitcast(FP8X4), rhs_scale=cs[:, cols], start=False, stop=True,
-            )
-            dst = res[q // 2][:, (q % 2) * GROUP:(q % 2 + 1) * GROUP]
-            if q % 2 == 0:
-                nc.scalar.activation(dst, acc_o[q][:], RELU)
-            else:
-                nc.vector.tensor_scalar_max(dst, acc_o[q][:], 0.0)
-                nc.sync.dma_start(out[:, (q - 1) * GROUP:(q + 1) * GROUP], res[q // 2][:])
+        acc_o = [psum.tile([P, GROUP], F32, name=f"acc_o{q}", tag="bank") for q in range(V // GROUP)]
+        for half in range(2):
+            for q in (2 * half, 2 * half + 1):
+                cols = slice(q * GROUP, (q + 1) * GROUP)
+                nc.tensor.matmul_mx(
+                    out=acc_o[q][:], lhsT=w3w[:].bitcast(FP4X4), lhsT_scale=ws[:, N:2 * N],
+                    rhs=zc[:, cols].bitcast(FP8X4), rhs_scale=zs[:, cols], start=True, stop=False,
+                )
+            for q in (2 * half, 2 * half + 1):
+                cols = slice(q * GROUP, (q + 1) * GROUP)
+                nc.tensor.matmul_mx(
+                    out=acc_o[q][:], lhsT=w2w[:].bitcast(FP4X4), lhsT_scale=ws[:, 0:N],
+                    rhs=cc[:, cols].bitcast(FP8X4), rhs_scale=cs[:, cols], start=False, stop=True,
+                )
+                dst = res[half][:, (q % 2) * GROUP:(q % 2 + 1) * GROUP]
+                if q % 2 == 0:
+                    nc.scalar.activation(dst, acc_o[q][:], RELU)
+                else:
+                    nc.vector.tensor_scalar_max(dst, acc_o[q][:], 0.0)
+                    nc.sync.dma_start(out[:, (q - 1) * GROUP:(q + 1) * GROUP], res[half][:])

@@ -54,7 +54,8 @@ def tile_picked_sagecat_maxrelu_p_kernel(
         nc.vector.memset(ws[:].bitcast(I32), 0)
 
         ident = keep.tile([P, P], F32, name="ident", align_bytes=64)
-        make_identity(nc, ident[:])
+        nc.vector.memset(ident[:], 0.0)
+        make_identity(nc, ident[:], nomemset=True)
 
         w1_rows = w1.rearrange("(p j) c -> p j c", j=PACK)
         nc.sync.dma_start(offs_sb[:], offs)
@@ -122,7 +123,7 @@ def tile_picked_sagecat_maxrelu_p_kernel(
         zi = keep.tile([P, V * PACK], BF16, name="zi", align_bytes=64)
         zc = keep.tile([P, V], U32, name="zc", align_bytes=64)
         zs = keep.tile([P, V], U8, name="zs", align_bytes=64)
-        cc = keep.tile([P, V], U32, name="cc", align_bytes=64)
+        cc = keep.tile([P, EARLY], U32, name="cc", align_bytes=64)
         cs = keep.tile([P, V], U8, name="cs", align_bytes=64)
         zi_planes = zi[:].rearrange("p (v t) -> p v t", t=PACK)
 
@@ -132,10 +133,9 @@ def tile_picked_sagecat_maxrelu_p_kernel(
         def wide_tile(name, tag=None):
             return keep.tile([P, V], F32, name=name, tag=tag or name, align_bytes=64)[:]
 
-        def excess(a, b, name, tag=None, rise=None):
+        def excess(a, b, name, tag=None):
             diff = wide_tile(f"diff{name}", tag)
-            if rise is None:
-                rise = wide_tile(f"rise{name}")
+            rise = wide_tile(f"rise{name}")
             nc.gpsimd.tensor_tensor(diff, b, a, SUB)
             nc.scalar.activation(rise, diff, RELU)
             return rise
@@ -169,14 +169,10 @@ def tile_picked_sagecat_maxrelu_p_kernel(
         for d in range(4):
             fetch(nb[2][d], 2, pos_sb[d][:])
 
-        stage = keep.tile([P, 13 * V], BF16, name="stage", tag="nb11", align_bytes=64)
-        ci = stage[:, 0:PACK * V]
-        ci_planes = ci.rearrange("p (v t) -> p v t", t=PACK)
-        cen23 = stage[:, 4 * V:6 * V].rearrange("p (t v) -> p t v", t=2)
-        cen01 = stage[:, 6 * V:8 * V].rearrange("p (t v) -> p t v", t=2)
-        g3 = stage[:, 8 * V:11 * V].rearrange("p (d v) -> p d v", d=3)
-        right = stage[:, 11 * V:13 * V].rearrange("p (t v) -> p t v", t=2)
-        last_rise = stage[:, 4 * V - V // 2:6 * V - V // 2].bitcast(F32)
+        stage = keep.tile([P, 7 * V], BF16, name="stage", tag="nb11", align_bytes=64)
+        cen01 = stage[:, 0:2 * V].rearrange("p (t v) -> p t v", t=2)
+        g3 = stage[:, 2 * V:5 * V].rearrange("p (d v) -> p d v", d=3)
+        right = stage[:, 5 * V:7 * V].rearrange("p (t v) -> p t v", t=2)
         left = keep.tile([P, 2, V], BF16, name="left", align_bytes=64)
         m2 = keep.tile([P, V], BF16, name="m2", align_bytes=64)
         z23 = keep.tile([P, 2, V], BF16, name="z23", align_bytes=64)
@@ -189,13 +185,16 @@ def tile_picked_sagecat_maxrelu_p_kernel(
 
         turn_back(0)
         rise_ab = excess(nb[2][0], nb[2][1], "20", tag="turned01")
-        rise_cd = excess(nb[2][2], nb[2][3], "21", tag="nb21", rise=last_rise)
+        rise_cd = excess(nb[2][2], nb[2][3], "21", tag="nb21")
         nc.gpsimd.tensor_tensor(left[:, 0, :], rise_ab, nb[2][0], ADD)
         turn_back(1)
         nc.gpsimd.tensor_tensor(right[:, 0, :], rise_cd, nb[2][2], ADD)
         for half in range(2):
             weave(zi_planes, 0, z01[half][:], half * V // 2, (half + 1) * V // 2)
 
+        ci = keep.tile([P, PACK * V], BF16, name="ci", tag="nb22", align_bytes=64)[:]
+        ci_planes = ci.rearrange("p (v t) -> p v t", t=PACK)
+        cen23 = keep.tile([P, 2, V], BF16, name="cen23", tag="rise21", align_bytes=64)
         for t in range(2):
             fetch(cen01[:, t, :], t, cen_sb[:])
         weave(ci_planes, 0, cen01, 0, V)
@@ -214,30 +213,37 @@ def tile_picked_sagecat_maxrelu_p_kernel(
         weave(ci_planes, 2, cen23[:, :, 0:V // 2], 0, V // 2)
         weave(ci_planes, 2, cen23[:, :, V // 2:EARLY], V // 2, EARLY)
         fetch(ci_planes[:, EARLY:V, 2], 2, cen_sb[:, EARLY // 16:V // 16])
-        for half in range(2):
-            cols = slice(half * V // 2, (half + 1) * V // 2)
-            wide = slice(half * V // 2 * PACK, (half + 1) * V // 2 * PACK)
-            nc.vector.quantize_mx(out=zc[:, cols].bitcast(FP8X4), scales=zs[:, cols], in_=zi[:, wide])
-            nc.vector.quantize_mx(out=cc[:, cols].bitcast(FP8X4), scales=cs[:, cols], in_=ci[:, wide])
+        cc_late = keep.tile([P, V - EARLY], U32, name="cc_late", tag="rise21", align_bytes=64)
+
+        def quantise(codes, scales, values, lo, hi):
+            nc.vector.quantize_mx(out=codes.bitcast(FP8X4), scales=scales[:, lo:hi], in_=values[:, lo * PACK:hi * PACK])
+
+        for lo, hi in ((0, V // 2), (V // 2, V)):
+            quantise(zc[:, lo:hi], zs, zi[:], lo, hi)
+        for lo, hi in ((0, V // 2), (V // 2, EARLY)):
+            quantise(cc[:, lo:hi], cs, ci, lo, hi)
+        quantise(cc_late[:], cs, ci, EARLY, V)
 
         res = [keep.tile([P, 2 * GROUP], F32, name=f"res{q}", align_bytes=64) for q in range(2)]
         acc_o = [psum.tile([P, GROUP], F32, name=f"acc_o{q}", tag="bank") for q in range(V // GROUP)]
-        for half in range(2):
-            for q in (2 * half, 2 * half + 1):
-                cols = slice(q * GROUP, (q + 1) * GROUP)
-                nc.tensor.matmul_mx(
-                    out=acc_o[q][:], lhsT=w3w[:].bitcast(FP4X4), lhsT_scale=ws[:, N:2 * N],
-                    rhs=zc[:, cols].bitcast(FP8X4), rhs_scale=zs[:, cols], start=True, stop=False,
-                )
-            for q in (2 * half, 2 * half + 1):
-                cols = slice(q * GROUP, (q + 1) * GROUP)
-                nc.tensor.matmul_mx(
-                    out=acc_o[q][:], lhsT=w2w[:].bitcast(FP4X4), lhsT_scale=ws[:, 0:N],
-                    rhs=cc[:, cols].bitcast(FP8X4), rhs_scale=cs[:, cols], start=False, stop=True,
-                )
-                dst = res[half][:, (q % 2) * GROUP:(q % 2 + 1) * GROUP]
-                if q % 2 == 0:
-                    nc.scalar.activation(dst, acc_o[q][:], RELU)
-                else:
-                    nc.vector.tensor_scalar_max(dst, acc_o[q][:], 0.0)
-                    nc.sync.dma_start(out[:, (q - 1) * GROUP:(q + 1) * GROUP], res[half][:])
+        for q in range(V // GROUP):
+            cols = slice(q * GROUP, (q + 1) * GROUP)
+            nc.tensor.matmul_mx(
+                out=acc_o[q][:], lhsT=w3w[:].bitcast(FP4X4), lhsT_scale=ws[:, N:2 * N],
+                rhs=zc[:, cols].bitcast(FP8X4), rhs_scale=zs[:, cols], start=True, stop=False,
+            )
+        for q in range(V // GROUP):
+            cols = slice(q * GROUP, (q + 1) * GROUP)
+            nc.tensor.matmul_mx(
+                out=acc_o[q][:], lhsT=w2w[:].bitcast(FP4X4), lhsT_scale=ws[:, 0:N],
+                rhs=(cc[:, cols] if cols.stop <= EARLY else cc_late[:]).bitcast(FP8X4), rhs_scale=cs[:, cols], start=False, stop=True,
+            )
+            dst = res[q // 2][:, (q % 2) * GROUP:(q % 2 + 1) * GROUP]
+            if q < 3:
+                nc.scalar.activation(dst, acc_o[q][:], RELU)
+            else:
+                nc.vector.tensor_scalar_max(dst, acc_o[q][:], 0.0)
+            if q == 1:
+                nc.sync.dma_start(out[:, 0:2 * GROUP], res[0][:])
+            if q >= 2:
+                nc.sync.dma_start(out[:, cols], dst)

@@ -160,7 +160,11 @@ def tile_picked_sagecat_maxrelu_p_kernel(
         def weave(planes, t0, src, lo, hi):
             nc.scalar.copy(planes[:, lo:hi, t0:t0 + 2], src.rearrange("p t v -> p v t"))
 
-        nb = [[wide_tile(f"nb{t}{d}") for d in range(4)] for t in range(3)]
+        nb = [
+            [keep.tile([P, V], F32 if t < 2 and d % 2 == 0 else BF16, name=f"nb{t}{d}", tag=f"nb{t}{d}", align_bytes=64)[:]
+             for d in range(4)]
+            for t in range(3)
+        ]
         halves = []
         for t in range(2):
             for d in range(4):
@@ -169,12 +173,9 @@ def tile_picked_sagecat_maxrelu_p_kernel(
         for d in range(4):
             fetch(nb[2][d], 2, pos_sb[d][:])
 
-        stage = keep.tile([P, 7 * V], BF16, name="stage", tag="nb11", align_bytes=64)
+        stage = keep.tile([P, 6 * V], BF16, name="stage", tag="nb11", align_bytes=64)
         cen01 = stage[:, 0:2 * V].rearrange("p (t v) -> p t v", t=2)
-        g3 = stage[:, 2 * V:5 * V].rearrange("p (d v) -> p d v", d=3)
-        right = stage[:, 5 * V:7 * V].rearrange("p (t v) -> p t v", t=2)
-        left = keep.tile([P, 2, V], BF16, name="left", align_bytes=64)
-        m2 = keep.tile([P, V], BF16, name="m2", align_bytes=64)
+        g3 = stage[:, 2 * V:6 * V].rearrange("p (d v) -> p d v", d=4)
         z23 = keep.tile([P, 2, V], BF16, name="z23", align_bytes=64)
         z01 = [psum_z.tile([P, 2, V // 2], F32, name=f"z01_{half}") for half in range(2)]
 
@@ -186,25 +187,30 @@ def tile_picked_sagecat_maxrelu_p_kernel(
         turn_back(0)
         rise_ab = excess(nb[2][0], nb[2][1], "20", tag="turned01")
         rise_cd = excess(nb[2][2], nb[2][3], "21", tag="nb21")
-        nc.gpsimd.tensor_tensor(left[:, 0, :], rise_ab, nb[2][0], ADD)
         turn_back(1)
-        nc.gpsimd.tensor_tensor(right[:, 0, :], rise_cd, nb[2][2], ADD)
+        pair2 = keep.tile([P, 2, V], BF16, name="pair2", tag="turned11", align_bytes=64)
+        nc.gpsimd.tensor_tensor(pair2[:, 0, :], rise_ab, nb[2][0], ADD)
+        nc.gpsimd.tensor_tensor(pair2[:, 1, :], rise_cd, nb[2][2], ADD)
         for half in range(2):
             weave(zi_planes, 0, z01[half][:], half * V // 2, (half + 1) * V // 2)
 
-        ci = keep.tile([P, PACK * V], BF16, name="ci", tag="nb22", align_bytes=64)[:]
+        ci = keep.tile([P, PACK * EARLY], BF16, name="ci", tag="nb21", align_bytes=64)[:]
         ci_planes = ci.rearrange("p (v t) -> p v t", t=PACK)
+        tail = keep.tile([P, PACK * (V - EARLY) + 2 * V], BF16, name="tail", tag="nb22", align_bytes=64)
+        ci_late = tail[:, 0:PACK * (V - EARLY)]
+        pair3 = tail[:, PACK * (V - EARLY):].rearrange("p (e v) -> p e v", e=2)
+        late_planes = ci_late.rearrange("p (v t) -> p v t", t=PACK)
         cen23 = keep.tile([P, 2, V], BF16, name="cen23", tag="rise21", align_bytes=64)
         for t in range(2):
             fetch(cen01[:, t, :], t, cen_sb[:])
-        weave(ci_planes, 0, cen01, 0, V)
-        for d in range(3):
+        weave(ci_planes, 0, cen01[:, :, 0:EARLY], 0, EARLY)
+        weave(late_planes, 0, cen01[:, :, EARLY:V], 0, V - EARLY)
+        for d in range(4):
             fetch(g3[:, d, :], 3, pos_sb[d][:])
-        nc.vector.tensor_tensor(m2[:], g3[:, 0, :], g3[:, 1, :], MAX)
-        fetch(right[:, 1, :], 3, pos_sb[3][:])
-        nc.vector.tensor_tensor(left[:, 1, :], m2[:], g3[:, 2, :], MAX)
-        fetch(ci_planes[:, EARLY:V, 3], 3, cen_sb[:, EARLY // 16:V // 16])
-        nc.vector.tensor_tensor(z23[:], left[:], right, MAX)
+        fetch(late_planes[:, :, 3], 3, cen_sb[:, EARLY // 16:V // 16])
+        nc.vector.tensor_tensor(pair3, g3[:, 0:2, :], g3[:, 2:4, :], MAX)
+        nc.vector.tensor_tensor(z23[:, 0, :], pair2[:, 0, :], pair2[:, 1, :], MAX)
+        nc.vector.tensor_tensor(z23[:, 1, :], pair3[:, 0, :], pair3[:, 1, :], MAX)
         for half in range(2):
             cols = slice(half * V // 2, (half + 1) * V // 2)
             weave(zi_planes, 2, z23[:, :, cols], cols.start, cols.stop)
@@ -212,17 +218,17 @@ def tile_picked_sagecat_maxrelu_p_kernel(
             fetch(cen23[:, t - 2, 0:EARLY], t, cen_sb[:, 0:EARLY // 16])
         weave(ci_planes, 2, cen23[:, :, 0:V // 2], 0, V // 2)
         weave(ci_planes, 2, cen23[:, :, V // 2:EARLY], V // 2, EARLY)
-        fetch(ci_planes[:, EARLY:V, 2], 2, cen_sb[:, EARLY // 16:V // 16])
+        fetch(late_planes[:, :, 2], 2, cen_sb[:, EARLY // 16:V // 16])
         cc_late = keep.tile([P, V - EARLY], U32, name="cc_late", tag="rise21", align_bytes=64)
 
-        def quantise(codes, scales, values, lo, hi):
-            nc.vector.quantize_mx(out=codes.bitcast(FP8X4), scales=scales[:, lo:hi], in_=values[:, lo * PACK:hi * PACK])
+        def quantise(codes, scales, values):
+            nc.vector.quantize_mx(out=codes.bitcast(FP8X4), scales=scales, in_=values)
 
         for lo, hi in ((0, V // 2), (V // 2, V)):
-            quantise(zc[:, lo:hi], zs, zi[:], lo, hi)
+            quantise(zc[:, lo:hi], zs[:, lo:hi], zi[:, lo * PACK:hi * PACK])
         for lo, hi in ((0, V // 2), (V // 2, EARLY)):
-            quantise(cc[:, lo:hi], cs, ci, lo, hi)
-        quantise(cc_late[:], cs, ci, EARLY, V)
+            quantise(cc[:, lo:hi], cs[:, lo:hi], ci[:, lo * PACK:hi * PACK])
+        quantise(cc_late[:], cs[:, EARLY:V], ci_late)
 
         res = [keep.tile([P, 2 * GROUP], F32, name=f"res{q}", align_bytes=64) for q in range(2)]
         acc_o = [psum.tile([P, GROUP], F32, name=f"acc_o{q}", tag="bank") for q in range(V // GROUP)]

@@ -176,7 +176,8 @@ def tile_picked_sagecat_maxrelu_p_kernel(
         stage = keep.tile([P, 6 * V], BF16, name="stage", tag="nb11", align_bytes=64)
         cen01 = stage[:, 0:2 * V].rearrange("p (t v) -> p t v", t=2)
         g3 = stage[:, 2 * V:6 * V].rearrange("p (d v) -> p d v", d=4)
-        z23 = keep.tile([P, 2, V], BF16, name="z23", align_bytes=64)
+        first3 = keep.tile([P, V], BF16, name="first3", align_bytes=64)
+        second3 = keep.tile([P, V], BF16, name="second3", align_bytes=64)
         z01 = [psum_z.tile([P, 2, V // 2], F32, name=f"z01_{half}") for half in range(2)]
 
         def turn_back(t):
@@ -198,19 +199,20 @@ def tile_picked_sagecat_maxrelu_p_kernel(
         ci_planes = ci.rearrange("p (v t) -> p v t", t=PACK)
         tail = keep.tile([P, PACK * (V - EARLY) + 2 * V], BF16, name="tail", tag="nb22", align_bytes=64)
         ci_late = tail[:, 0:PACK * (V - EARLY)]
-        pair3 = tail[:, PACK * (V - EARLY):].rearrange("p (e v) -> p e v", e=2)
+        z23 = tail[:, PACK * (V - EARLY):].rearrange("p (e v) -> p e v", e=2)
         late_planes = ci_late.rearrange("p (v t) -> p v t", t=PACK)
         cen23 = keep.tile([P, 2, V], BF16, name="cen23", tag="rise21", align_bytes=64)
         for t in range(2):
             fetch(cen01[:, t, :], t, cen_sb[:])
         weave(ci_planes, 0, cen01[:, :, 0:EARLY], 0, EARLY)
         weave(late_planes, 0, cen01[:, :, EARLY:V], 0, V - EARLY)
-        for d in range(4):
+        for d in range(3):
             fetch(g3[:, d, :], 3, pos_sb[d][:])
-        fetch(late_planes[:, :, 3], 3, cen_sb[:, EARLY // 16:V // 16])
-        nc.vector.tensor_tensor(pair3, g3[:, 0:2, :], g3[:, 2:4, :], MAX)
+        nc.vector.tensor_tensor(first3[:], g3[:, 0, :], g3[:, 1, :], MAX)
+        fetch(g3[:, 3, :], 3, pos_sb[3][:])
+        nc.vector.tensor_tensor(second3[:], first3[:], g3[:, 2, :], MAX)
         nc.vector.tensor_tensor(z23[:, 0, :], pair2[:, 0, :], pair2[:, 1, :], MAX)
-        nc.vector.tensor_tensor(z23[:, 1, :], pair3[:, 0, :], pair3[:, 1, :], MAX)
+        nc.vector.tensor_tensor(z23[:, 1, :], second3[:], g3[:, 3, :], MAX)
         for half in range(2):
             cols = slice(half * V // 2, (half + 1) * V // 2)
             weave(zi_planes, 2, z23[:, :, cols], cols.start, cols.stop)
@@ -218,7 +220,8 @@ def tile_picked_sagecat_maxrelu_p_kernel(
             fetch(cen23[:, t - 2, 0:EARLY], t, cen_sb[:, 0:EARLY // 16])
         weave(ci_planes, 2, cen23[:, :, 0:V // 2], 0, V // 2)
         weave(ci_planes, 2, cen23[:, :, V // 2:EARLY], V // 2, EARLY)
-        fetch(late_planes[:, :, 2], 2, cen_sb[:, EARLY // 16:V // 16])
+        for t in (2, 3):
+            fetch(late_planes[:, :, t], t, cen_sb[:, EARLY // 16:V // 16])
         cc_late = keep.tile([P, V - EARLY], U32, name="cc_late", tag="rise21", align_bytes=64)
 
         def quantise(codes, scales, values):

@@ -123,7 +123,7 @@ def tile_picked_sagecat_maxrelu_p_kernel(
         zi = keep.tile([P, V * PACK], BF16, name="zi", align_bytes=64)
         zc = keep.tile([P, V], U32, name="zc", align_bytes=64)
         zs = keep.tile([P, V], U8, name="zs", align_bytes=64)
-        cc = keep.tile([P, EARLY], U32, name="cc", align_bytes=64)
+        cc = keep.tile([P, V], U32, name="cc", align_bytes=64)
         cs = keep.tile([P, V], U8, name="cs", align_bytes=64)
         zi_planes = zi[:].rearrange("p (v t) -> p v t", t=PACK)
 
@@ -195,17 +195,13 @@ def tile_picked_sagecat_maxrelu_p_kernel(
         for half in range(2):
             weave(zi_planes, 0, z01[half][:], half * V // 2, (half + 1) * V // 2)
 
-        ci = keep.tile([P, PACK * EARLY], BF16, name="ci", tag="nb21", align_bytes=64)[:]
+        ci = keep.tile([P, PACK * V], BF16, name="ci", tag="diff1z", align_bytes=64)[:]
         ci_planes = ci.rearrange("p (v t) -> p v t", t=PACK)
-        tail = keep.tile([P, PACK * (V - EARLY) + 2 * V], BF16, name="tail", tag="nb22", align_bytes=64)
-        ci_late = tail[:, 0:PACK * (V - EARLY)]
-        z23 = tail[:, PACK * (V - EARLY):].rearrange("p (e v) -> p e v", e=2)
-        late_planes = ci_late.rearrange("p (v t) -> p v t", t=PACK)
+        z23 = keep.tile([P, 2, V], BF16, name="z23", tag="nb22", align_bytes=64)
         cen23 = keep.tile([P, 2, V], BF16, name="cen23", tag="rise21", align_bytes=64)
         for t in range(2):
             fetch(cen01[:, t, :], t, cen_sb[:])
-        weave(ci_planes, 0, cen01[:, :, 0:EARLY], 0, EARLY)
-        weave(late_planes, 0, cen01[:, :, EARLY:V], 0, V - EARLY)
+        weave(ci_planes, 0, cen01, 0, V)
         for d in range(3):
             fetch(g3[:, d, :], 3, pos_sb[d][:])
         nc.vector.tensor_tensor(first3[:], g3[:, 0, :], g3[:, 1, :], MAX)
@@ -216,22 +212,22 @@ def tile_picked_sagecat_maxrelu_p_kernel(
         for half in range(2):
             cols = slice(half * V // 2, (half + 1) * V // 2)
             weave(zi_planes, 2, z23[:, :, cols], cols.start, cols.stop)
-        for t in (3, 2):
-            fetch(cen23[:, t - 2, 0:EARLY], t, cen_sb[:, 0:EARLY // 16])
-        weave(ci_planes, 2, cen23[:, :, 0:V // 2], 0, V // 2)
-        weave(ci_planes, 2, cen23[:, :, V // 2:EARLY], V // 2, EARLY)
-        for t in (2, 3):
-            fetch(late_planes[:, :, t], t, cen_sb[:, EARLY // 16:V // 16])
-        cc_late = keep.tile([P, V - EARLY], U32, name="cc_late", tag="rise21", align_bytes=64)
+        for lo, hi in ((0, V // 2), (V // 2, V)):
+            for t in (2, 3):
+                fetch(cen23[:, t - 2, lo:hi], t, cen_sb[:, lo // 16:hi // 16])
+        cuts = ((0, V // 2), (V // 2, EARLY), (EARLY, V))
+        for lo, hi in cuts:
+            weave(ci_planes, 2, cen23[:, :, lo:hi], lo, hi)
 
-        def quantise(codes, scales, values):
-            nc.vector.quantize_mx(out=codes.bitcast(FP8X4), scales=scales, in_=values)
+        def quantise(codes, scales, values, lo, hi):
+            nc.vector.quantize_mx(
+                out=codes[:, lo:hi].bitcast(FP8X4), scales=scales[:, lo:hi], in_=values[:, lo * PACK:hi * PACK]
+            )
 
         for lo, hi in ((0, V // 2), (V // 2, V)):
-            quantise(zc[:, lo:hi], zs[:, lo:hi], zi[:, lo * PACK:hi * PACK])
-        for lo, hi in ((0, V // 2), (V // 2, EARLY)):
-            quantise(cc[:, lo:hi], cs[:, lo:hi], ci[:, lo * PACK:hi * PACK])
-        quantise(cc_late[:], cs[:, EARLY:V], ci_late)
+            quantise(zc, zs, zi, lo, hi)
+        for lo, hi in cuts:
+            quantise(cc, cs, ci, lo, hi)
 
         res = [keep.tile([P, 2 * GROUP], F32, name=f"res{q}", align_bytes=64) for q in range(2)]
         acc_o = [psum.tile([P, GROUP], F32, name=f"acc_o{q}", tag="bank") for q in range(V // GROUP)]
@@ -245,7 +241,7 @@ def tile_picked_sagecat_maxrelu_p_kernel(
             cols = slice(q * GROUP, (q + 1) * GROUP)
             nc.tensor.matmul_mx(
                 out=acc_o[q][:], lhsT=w2w[:].bitcast(FP4X4), lhsT_scale=ws[:, 0:N],
-                rhs=(cc[:, cols] if cols.stop <= EARLY else cc_late[:]).bitcast(FP8X4), rhs_scale=cs[:, cols], start=False, stop=True,
+                rhs=cc[:, cols].bitcast(FP8X4), rhs_scale=cs[:, cols], start=False, stop=True,
             )
             dst = res[q // 2][:, (q % 2) * GROUP:(q % 2 + 1) * GROUP]
             if q < 3:

@@ -25,7 +25,7 @@ PACK = 4
 BANK = 512
 GROUP = 128
 EARLY = 384
-LATE = 768
+ROWS0 = 112
 
 
 def tile_picked_sagecat_maxrelu_p_kernel(
@@ -44,14 +44,12 @@ def tile_picked_sagecat_maxrelu_p_kernel(
         pos_sb = [lists.tile([P, V // 16], U16, name=f"pos_sb{d}") for d in range(4)]
 
         xw = keep.tile([P, T], I32, name="xw", align_bytes=64)
-        xs = keep.tile([P, T], U8, name="xs", align_bytes=64)
-        ws = keep.tile([P, 2 * N], U8, name="ws", align_bytes=64)
-        w2w = keep.tile([P, 2 * N], U8, name="w2w", align_bytes=64)
-        w3w = keep.tile([P, 2 * N], U8, name="w3w", align_bytes=64)
-        w1_raw = [keep.tile([P, 2, H], F32, name=f"w1_raw{a}", align_bytes=64) for a in range(2)]
+        xs = keep.tile([P, T], U8, name="xs", tag="xs", align_bytes=64)
+        sgm = keep.tile([P, S], U8, name="sgm", align_bytes=64)
+        w1_raw = [keep.tile([P, PACK, H // 2], F32, name=f"w1_raw{a}", tag=f"raw{a}", align_bytes=64) for a in range(2)]
 
-        nc.vector.memset(xs[:].bitcast(I32), 0)
-        nc.vector.memset(ws[:].bitcast(I32), 0)
+        nc.vector.memset(xs[0:ROWS0, :].bitcast(I32), 0)
+        nc.vector.memset(sgm[:].bitcast(I32), 0)
 
         ident = keep.tile([P, P], F32, name="ident", align_bytes=64)
         nc.vector.memset(ident[:], 0.0)
@@ -59,14 +57,52 @@ def tile_picked_sagecat_maxrelu_p_kernel(
 
         w1_rows = w1.rearrange("(p j) c -> p j c", j=PACK)
         nc.sync.dma_start(offs_sb[:], offs)
-        nc.sync.dma_start(w1_raw[0][:], w1_rows[:, 0:2, :])
-        for r in range(4):
-            nc.sync.dma_start(xs[r:P:32, :].bitcast(I32), x_scales[0, r:16:4, :].bitcast(I32))
+        nc.sync.dma_start(xs[ROWS0:P, :].bitcast(I32), x_scales[0].bitcast(I32))
         nc.sync.dma_start(xw[:], x_words[0].rearrange("p n r -> p (n r)").bitcast(I32))
-        nc.sync.dma_start(w1_raw[1][:], w1_rows[:, 2:PACK, :])
-        for d, pos in enumerate((pos1, pos2, pos3, pos4)):
-            nc.sync.dma_start(pos_sb[d][:], pos)
+        nc.sync.dma_start(pos_sb[0][:], pos1)
+        nc.sync.dma_start(pos_sb[1][:], pos2)
+        nc.sync.dma_start(pos_sb[2][:], pos3)
+        nc.sync.dma_start(w1_raw[0][:], w1_rows[:, :, 0:H // 2])
+        nc.sync.dma_start(w1_raw[1][:], w1_rows[:, :, H // 2:H])
+        nc.sync.dma_start(pos_sb[3][:], pos4)
         nc.sync.dma_start(cen_sb[:], cen)
+
+        sg = keep.tile([P, S], U8, name="sg", align_bytes=64)
+        nc.vector.tensor_copy(sg[:], xs[:].indirect(offs_sb[:]))
+        for q in range(4):
+            nc.sync.dma_start(
+                sgm[32 * q:32 * q + 4, :].bitcast(I32), sg[ROWS0 + 4 * q:ROWS0 + 4 * q + 4, :].bitcast(I32)
+            )
+
+        xg = keep.tile([P, S], U32, name="xg", align_bytes=64)
+        nc.vector.tensor_copy(xg[:], xw[:].bitcast(U32).indirect(offs_sb[:]))
+
+        w1g = keep.tile([P, PACK * PACK * P], BF16, name="w1g", align_bytes=64)
+        w1c = [keep.tile([P, P], U32, name=f"w1c{t}", align_bytes=64) for t in range(2)]
+        w1c_late = keep.tile([P, 2 * P], U32, name="w1c_late", align_bytes=64)
+        w1s = keep.tile([P, H], U8, name="w1s", align_bytes=64)
+        dealt = w1g[:].rearrange("p (t m j) -> p m t j", t=PACK, j=PACK)
+
+        def views(a, t_lo, t_hi):
+            raw = w1_raw[a][:].rearrange("p j (m t) -> p m t j", t=PACK)
+            return dealt[:, a * P // 2:(a + 1) * P // 2, t_lo:t_hi, :], raw[:, :, t_lo:t_hi, :]
+
+        def deal(a, t_lo, t_hi):
+            nc.scalar.activation(*views(a, t_lo, t_hi), COPY)
+
+        deal(0, 0, 2)
+        nc.vector.tensor_copy(*views(0, 2, PACK))
+        deal(1, 0, 1)
+        nc.vector.quantize_mx(out=w1c[0][:].bitcast(FP8X4), scales=w1s[:, 0:P], in_=w1g[:, 0:H])
+        deal(1, 1, PACK)
+        nc.vector.quantize_mx(out=w1c[1][:].bitcast(FP8X4), scales=w1s[:, P:2 * P], in_=w1g[:, H:2 * H])
+        nc.vector.quantize_mx(out=w1c_late[:].bitcast(FP8X4), scales=w1s[:, 2 * P:H], in_=w1g[:, 2 * H:4 * H])
+        w1_codes = [w1c[0][:], w1c[1][:], w1c_late[:, 0:P], w1c_late[:, P:2 * P]]
+
+        ws = keep.tile([P, 2 * N], U8, name="ws", tag="xs", align_bytes=64)
+        w3w = keep.tile([P, 2 * N], U8, name="w3w", tag="raw0", align_bytes=64)
+        w2w = keep.tile([P, 2 * N], U8, name="w2w", tag="raw1", align_bytes=64)
+        nc.gpsimd.memset(ws[:].bitcast(I32), 0)
         nc.sync.dma_start(w3w[:].bitcast(I32), w3_words[0].bitcast(I32))
         nc.sync.dma_start(w2w[:].bitcast(I32), w2_words[0].bitcast(I32))
         for r in range(4):
@@ -74,48 +110,22 @@ def tile_picked_sagecat_maxrelu_p_kernel(
         for r in range(4):
             nc.sync.dma_start(ws[r:P:32, 0:N].bitcast(I32), w2_scales[0, r:16:4, :].bitcast(I32))
 
-        sg = keep.tile([P, S], U8, name="sg", align_bytes=64)
-        nc.vector.tensor_copy(sg[:], xs[:].indirect(offs_sb[:]))
-
-        def fetch_words(tile, lo, hi):
-            nc.vector.tensor_copy(tile, xw[:].bitcast(U32).indirect(offs_sb[:, lo // 16:hi // 16]))
-
-        xg = keep.tile([P, LATE], U32, name="xg", align_bytes=64)
-        fetch_words(xg[:], 0, LATE)
-
-        w1g0 = keep.tile([P, PACK * P], BF16, name="w1g0", tag="shared", align_bytes=64)
-        w1g = keep.tile([P, (PACK - 1) * PACK * P], BF16, name="w1g", align_bytes=64)
-        w1c = keep.tile([P, 2 * P], U32, name="w1c", align_bytes=64)
-        w1c_late = keep.tile([P, 2 * P], U32, name="w1c_late", align_bytes=64)
-        w1s = keep.tile([P, H], U8, name="w1s", align_bytes=64)
-        for a in range(2):
-            js = slice(2 * a, 2 * a + 2)
-            raw = w1_raw[a][:].rearrange("p j (m t) -> p m t j", t=PACK)
-            nc.scalar.activation(w1g0[:].rearrange("p (m j) -> p m j", j=PACK)[:, :, js], raw[:, :, 0, :], COPY)
-            nc.scalar.activation(
-                w1g[:].rearrange("p (t m j) -> p m t j", t=PACK - 1, j=PACK)[:, :, :, js], raw[:, :, 1:PACK, :], COPY
-            )
-        nc.vector.quantize_mx(out=w1c[:, 0:P].bitcast(FP8X4), scales=w1s[:, 0:P], in_=w1g0[:])
-        xg_late = keep.tile([P, S - LATE], U32, name="xg_late", tag="shared", align_bytes=64)
-        fetch_words(xg_late[:], LATE, S)
-        nc.vector.quantize_mx(out=w1c[:, P:2 * P].bitcast(FP8X4), scales=w1s[:, P:2 * P], in_=w1g[:, 0:PACK * P])
-        nc.vector.quantize_mx(out=w1c_late[:].bitcast(FP8X4), scales=w1s[:, 2 * P:H], in_=w1g[:, PACK * P:3 * PACK * P])
-
         h = [keep.tile([P, S], F32, name=f"h{t}", align_bytes=64) for t in range(PACK)]
-        pieces = ((0, BANK, xg[:, 0:BANK]), (BANK, LATE, xg[:, BANK:LATE]), (LATE, S, xg_late[:]))
         for t in range(PACK):
-            for lo, hi, words in pieces:
-                acc = psum.tile([P, hi - lo], F32, name="acc", tag="bank")
+            width = BANK // 2 if t == 0 else BANK
+            for lo in range(0, S, width):
+                hi = lo + width
+                acc = psum.tile([P, width], F32, name="acc", tag="bank")
                 nc.tensor.matmul_mx(
                     out=acc[:],
-                    lhsT=(w1c, w1c_late)[t // 2][:, t % 2 * P:(t % 2 + 1) * P].bitcast(FP8X4),
+                    lhsT=w1_codes[t].bitcast(FP8X4),
                     lhsT_scale=w1s[:, t * P:(t + 1) * P],
-                    rhs=words.bitcast(FP8X4),
-                    rhs_scale=sg[:, lo:hi],
+                    rhs=xg[:, lo:hi].bitcast(FP8X4),
+                    rhs_scale=sgm[:, lo:hi],
                     start=True,
                     stop=True,
                 )
-                if t == 0 and lo == BANK:
+                if t == 0 and lo in (0, S - width):
                     nc.vector.tensor_scalar_max(h[t][:, lo:hi], acc[:], 0.0)
                 else:
                     nc.scalar.activation(h[t][:, lo:hi], acc[:], RELU)

@@ -17,6 +17,7 @@ FP4X4 = mybir.dt.float4_e2m1fn_x4
 MAX = mybir.AluOpType.max
 SUB = mybir.AluOpType.subtract
 ADD = mybir.AluOpType.add
+MULT = mybir.AluOpType.mult
 RELU = mybir.ActivationFunctionType.Relu
 COPY = mybir.ActivationFunctionType.Copy
 
@@ -46,7 +47,7 @@ def tile_picked_sagecat_maxrelu_p_kernel(
         xw = keep.tile([P, T], I32, name="xw", align_bytes=64)
         xs = keep.tile([P, T], U8, name="xs", tag="xs", align_bytes=64)
         sgm = keep.tile([P, S], U8, name="sgm", align_bytes=64)
-        w1_raw = [keep.tile([P, PACK, H // 2], F32, name=f"w1_raw{a}", tag=f"raw{a}", align_bytes=64) for a in range(2)]
+        w1_raw = [keep.tile([P, 2, H], F32, name=f"w1_raw{a}", tag=f"raw{a}", align_bytes=64) for a in range(2)]
 
         nc.vector.memset(xs[0:ROWS0, :].bitcast(I32), 0)
         nc.vector.memset(sgm[:].bitcast(I32), 0)
@@ -61,9 +62,9 @@ def tile_picked_sagecat_maxrelu_p_kernel(
         nc.sync.dma_start(xw[:], x_words[0].rearrange("p n r -> p (n r)").bitcast(I32))
         nc.sync.dma_start(pos_sb[0][:], pos1)
         nc.sync.dma_start(pos_sb[1][:], pos2)
+        nc.sync.dma_start(w1_raw[0][:], w1_rows[:, 0:2, :])
+        nc.sync.dma_start(w1_raw[1][:], w1_rows[:, 2:PACK, :])
         nc.sync.dma_start(pos_sb[2][:], pos3)
-        nc.sync.dma_start(w1_raw[0][:], w1_rows[:, :, 0:H // 2])
-        nc.sync.dma_start(w1_raw[1][:], w1_rows[:, :, H // 2:H])
         nc.sync.dma_start(pos_sb[3][:], pos4)
         nc.sync.dma_start(cen_sb[:], cen)
 
@@ -85,14 +86,14 @@ def tile_picked_sagecat_maxrelu_p_kernel(
 
         def views(a, t_lo, t_hi):
             raw = w1_raw[a][:].rearrange("p j (m t) -> p m t j", t=PACK)
-            return dealt[:, a * P // 2:(a + 1) * P // 2, t_lo:t_hi, :], raw[:, :, t_lo:t_hi, :]
+            return dealt[:, :, t_lo:t_hi, 2 * a:2 * a + 2], raw[:, :, t_lo:t_hi, :]
 
         def deal(a, t_lo, t_hi):
             nc.scalar.activation(*views(a, t_lo, t_hi), COPY)
 
-        deal(0, 0, 2)
-        nc.vector.tensor_copy(*views(0, 2, PACK))
-        deal(1, 0, 1)
+        deal(0, 0, 1)
+        nc.gpsimd.tensor_scalar(*views(0, 1, PACK), 1.0, 0.0, MULT, ADD)
+        nc.vector.tensor_copy(*views(1, 0, 1))
         nc.vector.quantize_mx(out=w1c[0][:].bitcast(FP8X4), scales=w1s[:, 0:P], in_=w1g[:, 0:H])
         deal(1, 1, PACK)
         nc.vector.quantize_mx(out=w1c[1][:].bitcast(FP8X4), scales=w1s[:, P:2 * P], in_=w1g[:, H:2 * H])
@@ -125,7 +126,7 @@ def tile_picked_sagecat_maxrelu_p_kernel(
                     start=True,
                     stop=True,
                 )
-                if t == 0 and lo in (0, S - width):
+                if t == 0 and lo == S - width:
                     nc.vector.tensor_scalar_max(h[t][:, lo:hi], acc[:], 0.0)
                 else:
                     nc.scalar.activation(h[t][:, lo:hi], acc[:], RELU)

@@ -62,9 +62,9 @@ def tile_picked_sagecat_maxrelu_p_kernel(
         nc.sync.dma_start(xw[:], x_words[0].rearrange("p n r -> p (n r)").bitcast(I32))
         nc.sync.dma_start(pos_sb[0][:], pos1)
         nc.sync.dma_start(pos_sb[1][:], pos2)
+        nc.sync.dma_start(pos_sb[2][:], pos3)
         nc.sync.dma_start(w1_raw[0][:], w1_rows[:, 0:2, :])
         nc.sync.dma_start(w1_raw[1][:], w1_rows[:, 2:PACK, :])
-        nc.sync.dma_start(pos_sb[2][:], pos3)
         nc.sync.dma_start(pos_sb[3][:], pos4)
         nc.sync.dma_start(cen_sb[:], cen)
 

@@ -92,7 +92,8 @@ def tile_picked_sagecat_maxrelu_p_kernel(
             nc.scalar.activation(*views(a, t_lo, t_hi), COPY)
 
         deal(0, 0, 1)
-        nc.gpsimd.tensor_scalar(*views(0, 1, PACK), 1.0, 0.0, MULT, ADD)
+        deal(0, 1, 2)
+        nc.gpsimd.tensor_scalar(*views(0, 2, PACK), 1.0, 0.0, MULT, ADD)
         nc.vector.tensor_copy(*views(1, 0, 1))
         nc.vector.quantize_mx(out=w1c[0][:].bitcast(FP8X4), scales=w1s[:, 0:P], in_=w1g[:, 0:H])
         deal(1, 1, PACK)

@@ -27,6 +27,8 @@ BANK = 512
 GROUP = 128
 EARLY = 384
 ROWS0 = 112
+FIRST = 256
+WARM = 5
 
 
 def tile_picked_sagecat_maxrelu_p_kernel(
@@ -76,7 +78,14 @@ def tile_picked_sagecat_maxrelu_p_kernel(
             )
 
         xg = keep.tile([P, S], U32, name="xg", align_bytes=64)
-        nc.vector.tensor_copy(xg[:], xw[:].bitcast(U32).indirect(offs_sb[:]))
+        for lo, hi in ((0, FIRST), (FIRST, S)):
+            nc.vector.tensor_copy(xg[:, lo:hi], xw[:].bitcast(U32).indirect(offs_sb[:, lo // 16:hi // 16]))
+        idle = psum_turn.tile([P, FIRST], F32, name="idle", tag="turn")
+        for i in range(WARM):
+            nc.tensor.matmul_mx(
+                out=idle[:], lhsT=xg[:, 0:P].bitcast(FP8X4), lhsT_scale=sg[:, 0:P],
+                rhs=xg[:, 0:FIRST].bitcast(FP8X4), rhs_scale=sg[:, 0:FIRST], start=True, stop=True,
+            )
 
         w1g = keep.tile([P, PACK * PACK * P], BF16, name="w1g", align_bytes=64)
         w1c = [keep.tile([P, P], U32, name=f"w1c{t}", align_bytes=64) for t in range(2)]

@@ -1,7 +1,6 @@
 from contextlib import ExitStack
 
 import concourse.mybir as mybir
-from concourse.masks import make_identity
 
 K, T, S, V, H, N = 512, 2048, 1024, 512, 512, 128
 FLOPS = 2 * K * H * S + 2 * 2 * H * N * V
@@ -15,7 +14,6 @@ U8 = mybir.dt.uint8
 FP8X4 = mybir.dt.float8_e4m3fn_x4
 FP4X4 = mybir.dt.float4_e2m1fn_x4
 MAX = mybir.AluOpType.max
-SUB = mybir.AluOpType.subtract
 ADD = mybir.AluOpType.add
 MULT = mybir.AluOpType.mult
 RELU = mybir.ActivationFunctionType.Relu
@@ -24,7 +22,6 @@ COPY = mybir.ActivationFunctionType.Copy
 P = 128
 PACK = 4
 BANK = 512
-GROUP = 128
 EARLY = 384
 ROWS0 = 112
 FIRST = 256
@@ -39,8 +36,7 @@ def tile_picked_sagecat_maxrelu_p_kernel(
         lists = ctx.enter_context(tc.tile_pool(name="lists", bufs=1))
         keep = ctx.enter_context(tc.tile_pool(name="keep", bufs=1))
         psum = ctx.enter_context(tc.psum_pool(name="psum", bufs=4))
-        psum_turn = ctx.enter_context(tc.psum_pool(name="psum_turn", bufs=2))
-        psum_z = ctx.enter_context(tc.psum_pool(name="psum_z", bufs=1))
+        psum_out = ctx.enter_context(tc.psum_pool(name="psum_out", bufs=1))
 
         offs_sb = lists.tile([P, S // 16], U16, name="offs_sb")
         cen_sb = lists.tile([P, V // 16], U16, name="cen_sb")
@@ -53,10 +49,6 @@ def tile_picked_sagecat_maxrelu_p_kernel(
 
         nc.vector.memset(xs[0:ROWS0, :].bitcast(I32), 0)
         nc.vector.memset(sgm[:].bitcast(I32), 0)
-
-        ident = keep.tile([P, P], F32, name="ident", align_bytes=64)
-        nc.vector.memset(ident[:], 0.0)
-        make_identity(nc, ident[:], nomemset=True)
 
         w1_rows = w1.rearrange("(p j) c -> p j c", j=PACK)
         nc.sync.dma_start(offs_sb[:], offs)
@@ -80,7 +72,7 @@ def tile_picked_sagecat_maxrelu_p_kernel(
         xg = keep.tile([P, S], U32, name="xg", align_bytes=64)
         for lo, hi in ((0, FIRST), (FIRST, S)):
             nc.vector.tensor_copy(xg[:, lo:hi], xw[:].bitcast(U32).indirect(offs_sb[:, lo // 16:hi // 16]))
-        idle = psum_turn.tile([P, FIRST], F32, name="idle", tag="turn")
+        idle = psum_out.tile([P, FIRST], F32, name="idle")
         for i in range(WARM):
             nc.tensor.matmul_mx(
                 out=idle[:], lhsT=xg[:, 0:P].bitcast(FP8X4), lhsT_scale=sg[:, 0:P],
@@ -141,135 +133,85 @@ def tile_picked_sagecat_maxrelu_p_kernel(
                 else:
                     nc.scalar.activation(h[t][:, lo:hi], acc[:], RELU)
 
+        def fetch(engine, dst, t, offsets):
+            if engine == "vector":
+                nc.vector.tensor_copy(dst, h[t][:].indirect(offsets))
+            else:
+                nc.scalar.activation(dst, h[t][:].indirect(offsets), COPY)
+
+        nb = [keep.tile([P, 4 * V], BF16, name=f"nb{t}", align_bytes=64) for t in range(PACK)]
+        pairs = [keep.tile([P, 2 * V], BF16, name=f"pairs{t}", align_bytes=64) for t in range(PACK)]
+        zp = keep.tile([P, PACK * V], BF16, name="zp", align_bytes=64)
+        cuts = ((0, V // 2), (V // 2, EARLY), (EARLY, V))
+        cp = [keep.tile([P, PACK * (hi - lo)], BF16, name=f"cp{lo}", align_bytes=64) for lo, hi in cuts]
+
+        def neighbours(engine, t):
+            for d in range(4):
+                fetch(engine, nb[t][:, d * V:(d + 1) * V], t, pos_sb[d][:])
+
+        def first_max(t):
+            nc.vector.tensor_tensor(pairs[t][:], nb[t][:, 0:2 * V], nb[t][:, 2 * V:4 * V], MAX)
+
+        def last_max(t):
+            nc.vector.tensor_tensor(zp[:, t * V:(t + 1) * V], pairs[t][:, 0:V], pairs[t][:, V:2 * V], MAX)
+
+        def centre(engine, t, i):
+            lo, hi = cuts[i]
+            n = hi - lo
+            fetch(engine, cp[i][:, t * n:(t + 1) * n], t, cen_sb[:, lo // 16:hi // 16])
+
+        neighbours("vector", 0)
+        neighbours("vector", 1)
+        neighbours("scalar", 2)
+        neighbours("scalar", 3)
+        first_max(0)
+        centre("vector", 0, 0)
+        first_max(1)
+        centre("vector", 1, 0)
+        last_max(0)
+        centre("vector", 0, 1)
+        last_max(1)
+        centre("vector", 0, 2)
+        first_max(2)
+        first_max(3)
+        last_max(2)
+        last_max(3)
+        for t in (2, 3):
+            centre("scalar", t, 0)
+        for i in (1, 2):
+            for t in (1, 2, 3):
+                centre("scalar", t, i)
+
         zi = keep.tile([P, V * PACK], BF16, name="zi", align_bytes=64)
         zc = keep.tile([P, V], U32, name="zc", align_bytes=64)
         zs = keep.tile([P, V], U8, name="zs", align_bytes=64)
-        cc = keep.tile([P, V], U32, name="cc", align_bytes=64)
-        cs = keep.tile([P, V], U8, name="cs", align_bytes=64)
-        zi_planes = zi[:].rearrange("p (v t) -> p v t", t=PACK)
+        ci = [keep.tile([P, PACK * (hi - lo)], BF16, name=f"ci{lo}", align_bytes=64) for lo, hi in cuts]
+        cc = [keep.tile([P, hi - lo], U32, name=f"cc{lo}", align_bytes=64) for lo, hi in cuts]
+        cs = [keep.tile([P, hi - lo], U8, name=f"cs{lo}", align_bytes=64) for lo, hi in cuts]
 
-        def fetch(dst, t, offsets):
-            nc.vector.tensor_copy(dst, h[t][:].indirect(offsets))
+        def weave(dst, src):
+            nc.vector.tensor_copy(dst.rearrange("p (v t) -> p v t", t=PACK), src.rearrange("p (t v) -> p v t", t=PACK))
 
-        def wide_tile(name, tag=None):
-            return keep.tile([P, V], F32, name=name, tag=tag or name, align_bytes=64)[:]
+        weave(zi[:], zp[:])
+        weave(ci[0][:], cp[0][:])
+        nc.vector.quantize_mx(out=zc[:].bitcast(FP8X4), scales=zs[:], in_=zi[:])
+        nc.vector.quantize_mx(out=cc[0][:].bitcast(FP8X4), scales=cs[0][:], in_=ci[0][:])
+        for i in (1, 2):
+            weave(ci[i][:], cp[i][:])
+        for i in (1, 2):
+            nc.vector.quantize_mx(out=cc[i][:].bitcast(FP8X4), scales=cs[i][:], in_=ci[i][:])
 
-        def excess(a, b, name, tag=None):
-            diff = wide_tile(f"diff{name}", tag)
-            rise = wide_tile(f"rise{name}")
-            nc.gpsimd.tensor_tensor(diff, b, a, SUB)
-            nc.scalar.activation(rise, diff, RELU)
-            return rise
-
-        def add_turned(dst, first, second, blocks):
-            terms = [(src, b) for src in (first, second) for b in blocks]
-            for i, (src, b) in enumerate(terms):
-                col = (b - blocks[0]) * P
-                nc.tensor.matmul(
-                    dst[:, col:col + P], src[:, b * P:(b + 1) * P], ident[:],
-                    start=i == 0, stop=i == len(terms) - 1, is_transpose=True,
-                )
-
-        def larger_turned(a, b, name):
-            rise = excess(a, b, name)
-            bank = psum_turn.tile([P, V], F32, name=f"turn{name}", tag="turn")
-            add_turned(bank[:], a, rise, (0, 1, 2, 3))
-            turned = wide_tile(f"turned{name}")
-            nc.scalar.copy(turned, bank[:])
-            return turned
-
-        def weave(planes, t0, src, lo, hi):
-            nc.scalar.copy(planes[:, lo:hi, t0:t0 + 2], src.rearrange("p t v -> p v t"))
-
-        nb = [
-            [keep.tile([P, V], F32 if t < 2 and d % 2 == 0 else BF16, name=f"nb{t}{d}", tag=f"nb{t}{d}", align_bytes=64)[:]
-             for d in range(4)]
-            for t in range(3)
-        ]
-        halves = []
-        for t in range(2):
-            for d in range(4):
-                fetch(nb[t][d], t, pos_sb[d][:])
-            halves.append([larger_turned(nb[t][2 * e], nb[t][2 * e + 1], f"{t}{e}") for e in range(2)])
-        for d in range(4):
-            fetch(nb[2][d], 2, pos_sb[d][:])
-
-        stage = keep.tile([P, 6 * V], BF16, name="stage", tag="nb11", align_bytes=64)
-        cen01 = stage[:, 0:2 * V].rearrange("p (t v) -> p t v", t=2)
-        g3 = stage[:, 2 * V:6 * V].rearrange("p (d v) -> p d v", d=4)
-        first3 = keep.tile([P, V], BF16, name="first3", align_bytes=64)
-        second3 = keep.tile([P, V], BF16, name="second3", align_bytes=64)
-        z01 = [psum_z.tile([P, 2, V // 2], F32, name=f"z01_{half}") for half in range(2)]
-
-        def turn_back(t):
-            rise = excess(halves[t][0], halves[t][1], f"{t}z")
-            for half in range(2):
-                add_turned(z01[half][:, t, :], halves[t][0], rise, (2 * half, 2 * half + 1))
-
-        turn_back(0)
-        rise_ab = excess(nb[2][0], nb[2][1], "20", tag="turned01")
-        rise_cd = excess(nb[2][2], nb[2][3], "21", tag="nb21")
-        turn_back(1)
-        pair2 = keep.tile([P, 2, V], BF16, name="pair2", tag="turned11", align_bytes=64)
-        nc.gpsimd.tensor_tensor(pair2[:, 0, :], rise_ab, nb[2][0], ADD)
-        nc.gpsimd.tensor_tensor(pair2[:, 1, :], rise_cd, nb[2][2], ADD)
-        for half in range(2):
-            weave(zi_planes, 0, z01[half][:], half * V // 2, (half + 1) * V // 2)
-
-        ci = keep.tile([P, PACK * V], BF16, name="ci", tag="diff1z", align_bytes=64)[:]
-        ci_planes = ci.rearrange("p (v t) -> p v t", t=PACK)
-        z23 = keep.tile([P, 2, V], BF16, name="z23", tag="nb22", align_bytes=64)
-        cen23 = keep.tile([P, 2, V], BF16, name="cen23", tag="rise21", align_bytes=64)
-        for t in range(2):
-            fetch(cen01[:, t, :], t, cen_sb[:])
-        weave(ci_planes, 0, cen01, 0, V)
-        for d in range(3):
-            fetch(g3[:, d, :], 3, pos_sb[d][:])
-        nc.vector.tensor_tensor(first3[:], g3[:, 0, :], g3[:, 1, :], MAX)
-        fetch(g3[:, 3, :], 3, pos_sb[3][:])
-        nc.vector.tensor_tensor(second3[:], first3[:], g3[:, 2, :], MAX)
-        nc.vector.tensor_tensor(z23[:, 0, :], pair2[:, 0, :], pair2[:, 1, :], MAX)
-        nc.vector.tensor_tensor(z23[:, 1, :], second3[:], g3[:, 3, :], MAX)
-        for half in range(2):
-            cols = slice(half * V // 2, (half + 1) * V // 2)
-            weave(zi_planes, 2, z23[:, :, cols], cols.start, cols.stop)
-        for lo, hi in ((0, V // 2), (V // 2, V)):
-            for t in (2, 3):
-                fetch(cen23[:, t - 2, lo:hi], t, cen_sb[:, lo // 16:hi // 16])
-        cuts = ((0, V // 2), (V // 2, EARLY), (EARLY, V))
-        for lo, hi in cuts:
-            weave(ci_planes, 2, cen23[:, :, lo:hi], lo, hi)
-
-        def quantise(codes, scales, values, lo, hi):
-            nc.vector.quantize_mx(
-                out=codes[:, lo:hi].bitcast(FP8X4), scales=scales[:, lo:hi], in_=values[:, lo * PACK:hi * PACK]
-            )
-
-        for lo, hi in ((0, V // 2), (V // 2, V)):
-            quantise(zc, zs, zi, lo, hi)
-        for lo, hi in cuts:
-            quantise(cc, cs, ci, lo, hi)
-
-        res = [keep.tile([P, 2 * GROUP], F32, name=f"res{q}", align_bytes=64) for q in range(2)]
-        acc_o = [psum.tile([P, GROUP], F32, name=f"acc_o{q}", tag="bank") for q in range(V // GROUP)]
-        for q in range(V // GROUP):
-            cols = slice(q * GROUP, (q + 1) * GROUP)
+        res = [keep.tile([P, hi - lo], F32, name=f"res{lo}", align_bytes=64) for lo, hi in cuts]
+        acc_o = [psum_out.tile([P, hi - lo], F32, name=f"acc_o{lo}") for lo, hi in cuts]
+        for i, (lo, hi) in enumerate(cuts):
             nc.tensor.matmul_mx(
-                out=acc_o[q][:], lhsT=w3w[:].bitcast(FP4X4), lhsT_scale=ws[:, N:2 * N],
-                rhs=zc[:, cols].bitcast(FP8X4), rhs_scale=zs[:, cols], start=True, stop=False,
+                out=acc_o[i][:], lhsT=w3w[:].bitcast(FP4X4), lhsT_scale=ws[:, N:2 * N],
+                rhs=zc[:, lo:hi].bitcast(FP8X4), rhs_scale=zs[:, lo:hi], start=True, stop=False,
             )
-        for q in range(V // GROUP):
-            cols = slice(q * GROUP, (q + 1) * GROUP)
+        for i, (lo, hi) in enumerate(cuts):
             nc.tensor.matmul_mx(
-                out=acc_o[q][:], lhsT=w2w[:].bitcast(FP4X4), lhsT_scale=ws[:, 0:N],
-                rhs=cc[:, cols].bitcast(FP8X4), rhs_scale=cs[:, cols], start=False, stop=True,
+                out=acc_o[i][:], lhsT=w2w[:].bitcast(FP4X4), lhsT_scale=ws[:, 0:N],
+                rhs=cc[i][:].bitcast(FP8X4), rhs_scale=cs[i][:], start=False, stop=True,
             )
-            dst = res[q // 2][:, (q % 2) * GROUP:(q % 2 + 1) * GROUP]
-            if q < 3:
-                nc.scalar.activation(dst, acc_o[q][:], RELU)
-            else:
-                nc.vector.tensor_scalar_max(dst, acc_o[q][:], 0.0)
-            if q == 1:
-                nc.sync.dma_start(out[:, 0:2 * GROUP], res[0][:])
-            if q >= 2:
-                nc.sync.dma_start(out[:, cols], dst)
+            nc.scalar.activation(res[i][:], acc_o[i][:], RELU)
+            nc.sync.dma_start(out[:, lo:hi], res[i][:])

@@ -35,8 +35,7 @@ def tile_picked_sagecat_maxrelu_p_kernel(
     with ExitStack() as ctx:
         lists = ctx.enter_context(tc.tile_pool(name="lists", bufs=1))
         keep = ctx.enter_context(tc.tile_pool(name="keep", bufs=1))
-        psum = ctx.enter_context(tc.psum_pool(name="psum", bufs=4))
-        psum_out = ctx.enter_context(tc.psum_pool(name="psum_out", bufs=1))
+        psum = ctx.enter_context(tc.psum_pool(name="psum", bufs=8))
 
         offs_sb = lists.tile([P, S // 16], U16, name="offs_sb")
         cen_sb = lists.tile([P, V // 16], U16, name="cen_sb")
@@ -72,7 +71,7 @@ def tile_picked_sagecat_maxrelu_p_kernel(
         xg = keep.tile([P, S], U32, name="xg", align_bytes=64)
         for lo, hi in ((0, FIRST), (FIRST, S)):
             nc.vector.tensor_copy(xg[:, lo:hi], xw[:].bitcast(U32).indirect(offs_sb[:, lo // 16:hi // 16]))
-        idle = psum_out.tile([P, FIRST], F32, name="idle")
+        idle = psum.tile([P, FIRST], F32, name="idle", tag="bank")
         for i in range(WARM):
             nc.tensor.matmul_mx(
                 out=idle[:], lhsT=xg[:, 0:P].bitcast(FP8X4), lhsT_scale=sg[:, 0:P],
@@ -96,8 +95,9 @@ def tile_picked_sagecat_maxrelu_p_kernel(
         deal(0, 1, 2)
         nc.gpsimd.tensor_scalar(*views(0, 2, PACK), 1.0, 0.0, MULT, ADD)
         nc.vector.tensor_copy(*views(1, 0, 1))
+        nc.vector.tensor_copy(*views(1, 1, 2))
         nc.vector.quantize_mx(out=w1c[0][:].bitcast(FP8X4), scales=w1s[:, 0:P], in_=w1g[:, 0:H])
-        deal(1, 1, PACK)
+        deal(1, 2, PACK)
         nc.vector.quantize_mx(out=w1c[1][:].bitcast(FP8X4), scales=w1s[:, P:2 * P], in_=w1g[:, H:2 * H])
         nc.vector.quantize_mx(out=w1c_late[:].bitcast(FP8X4), scales=w1s[:, 2 * P:H], in_=w1g[:, 2 * H:4 * H])
         w1_codes = [w1c[0][:], w1c[1][:], w1c_late[:, 0:P], w1c_late[:, P:2 * P]]
@@ -128,7 +128,7 @@ def tile_picked_sagecat_maxrelu_p_kernel(
                     start=True,
                     stop=True,
                 )
-                if t == 0 and lo == S - width:
+                if t == 0 and (lo // width) % 2 == 1:
                     nc.vector.tensor_scalar_max(h[t][:, lo:hi], acc[:], 0.0)
                 else:
                     nc.scalar.activation(h[t][:, lo:hi], acc[:], RELU)
@@ -139,79 +139,100 @@ def tile_picked_sagecat_maxrelu_p_kernel(
             else:
                 nc.scalar.activation(dst, h[t][:].indirect(offsets), COPY)
 
-        nb = [keep.tile([P, 4 * V], BF16, name=f"nb{t}", align_bytes=64) for t in range(PACK)]
-        pairs = [keep.tile([P, 2 * V], BF16, name=f"pairs{t}", align_bytes=64) for t in range(PACK)]
-        zp = keep.tile([P, PACK * V], BF16, name="zp", align_bytes=64)
         cuts = ((0, V // 2), (V // 2, EARLY), (EARLY, V))
-        cp = [keep.tile([P, PACK * (hi - lo)], BF16, name=f"cp{lo}", align_bytes=64) for lo, hi in cuts]
+        cp = keep.tile([P, PACK * V], BF16, name="cp", align_bytes=64)
+        nb01 = keep.tile([P, 8 * V], BF16, name="nb01", align_bytes=64)
+        pairs01 = keep.tile([P, 4 * V], BF16, name="pairs01", align_bytes=64)
+        nb2 = keep.tile([P, 4 * V], BF16, name="nb2", align_bytes=64)
+        pairs2 = keep.tile([P, 2 * V], BF16, name="pairs2", align_bytes=64)
+        nb3 = [keep.tile([P, 4 * (hi - lo)], BF16, name=f"nb3_{lo}", align_bytes=64) for lo, hi in cuts]
+        pairs3 = [keep.tile([P, 2 * (hi - lo)], BF16, name=f"pairs3_{lo}", align_bytes=64) for lo, hi in cuts]
+        zp = keep.tile([P, PACK * V], BF16, name="zp", align_bytes=64)
 
-        def neighbours(engine, t):
-            for d in range(4):
-                fetch(engine, nb[t][:, d * V:(d + 1) * V], t, pos_sb[d][:])
+        def centre(engine, t, lo, hi):
+            fetch(engine, cp[:, t * V + lo:t * V + hi], t, cen_sb[:, lo // 16:hi // 16])
 
-        def first_max(t):
-            nc.vector.tensor_tensor(pairs[t][:], nb[t][:, 0:2 * V], nb[t][:, 2 * V:4 * V], MAX)
-
-        def last_max(t):
-            nc.vector.tensor_tensor(zp[:, t * V:(t + 1) * V], pairs[t][:, 0:V], pairs[t][:, V:2 * V], MAX)
-
-        def centre(engine, t, i):
-            lo, hi = cuts[i]
+        def neighbours(engine, dst, t, lo, hi):
             n = hi - lo
-            fetch(engine, cp[i][:, t * n:(t + 1) * n], t, cen_sb[:, lo // 16:hi // 16])
+            for d in range(4):
+                fetch(engine, dst[:, d * n:(d + 1) * n], t, pos_sb[d][:, lo // 16:hi // 16])
 
-        neighbours("vector", 0)
-        neighbours("vector", 1)
-        neighbours("scalar", 2)
-        neighbours("scalar", 3)
-        first_max(0)
-        centre("vector", 0, 0)
-        first_max(1)
-        centre("vector", 1, 0)
-        last_max(0)
-        centre("vector", 0, 1)
-        last_max(1)
-        centre("vector", 0, 2)
-        first_max(2)
-        first_max(3)
-        last_max(2)
-        last_max(3)
-        for t in (2, 3):
-            centre("scalar", t, 0)
-        for i in (1, 2):
-            for t in (1, 2, 3):
-                centre("scalar", t, i)
+        def larger(dst, src, n):
+            nc.vector.tensor_tensor(dst, src[:, 0:n], src[:, n:2 * n], MAX)
 
-        zi = keep.tile([P, V * PACK], BF16, name="zi", align_bytes=64)
-        zc = keep.tile([P, V], U32, name="zc", align_bytes=64)
-        zs = keep.tile([P, V], U8, name="zs", align_bytes=64)
-        ci = [keep.tile([P, PACK * (hi - lo)], BF16, name=f"ci{lo}", align_bytes=64) for lo, hi in cuts]
-        cc = [keep.tile([P, hi - lo], U32, name=f"cc{lo}", align_bytes=64) for lo, hi in cuts]
-        cs = [keep.tile([P, hi - lo], U8, name=f"cs{lo}", align_bytes=64) for lo, hi in cuts]
-
-        def weave(dst, src):
-            nc.vector.tensor_copy(dst.rearrange("p (v t) -> p v t", t=PACK), src.rearrange("p (t v) -> p v t", t=PACK))
-
-        weave(zi[:], zp[:])
-        weave(ci[0][:], cp[0][:])
-        nc.vector.quantize_mx(out=zc[:].bitcast(FP8X4), scales=zs[:], in_=zi[:])
-        nc.vector.quantize_mx(out=cc[0][:].bitcast(FP8X4), scales=cs[0][:], in_=ci[0][:])
-        for i in (1, 2):
-            weave(ci[i][:], cp[i][:])
-        for i in (1, 2):
-            nc.vector.quantize_mx(out=cc[i][:].bitcast(FP8X4), scales=cs[i][:], in_=ci[i][:])
-
-        res = [keep.tile([P, hi - lo], F32, name=f"res{lo}", align_bytes=64) for lo, hi in cuts]
-        acc_o = [psum_out.tile([P, hi - lo], F32, name=f"acc_o{lo}") for lo, hi in cuts]
+        centre("vector", 0, 0, V)
+        for t in range(2):
+            for d in range(4):
+                fetch("vector", nb01[:, (2 * d + t) * V:(2 * d + t + 1) * V], t, pos_sb[d][:])
+        for t in (1, 2, 3):
+            centre("scalar", t, 0, V)
+        neighbours("scalar", nb2, 2, 0, V)
         for i, (lo, hi) in enumerate(cuts):
-            nc.tensor.matmul_mx(
-                out=acc_o[i][:], lhsT=w3w[:].bitcast(FP4X4), lhsT_scale=ws[:, N:2 * N],
-                rhs=zc[:, lo:hi].bitcast(FP8X4), rhs_scale=zs[:, lo:hi], start=True, stop=False,
-            )
+            neighbours("scalar", nb3[i], 3, lo, hi)
+
+        ci = keep.tile([P, PACK * V], BF16, name="ci", align_bytes=64)
+        cc = keep.tile([P, V], U32, name="cc", align_bytes=64)
+        cs = keep.tile([P, V], U8, name="cs", align_bytes=64)
+        nc.gpsimd.tensor_scalar(
+            ci[:].rearrange("p (v t) -> p v t", t=PACK), cp[:].rearrange("p (t v) -> p v t", t=PACK), 1.0, 0.0, MULT, ADD
+        )
+        larger(pairs01[:], nb01, 4 * V)
+        larger(pairs2[:], nb2, 2 * V)
+        larger(zp[:, 0:2 * V], pairs01, 2 * V)
+        nc.vector.quantize_mx(out=cc[:].bitcast(FP8X4), scales=cs[:], in_=ci[:])
+
+        acc_o = [psum.tile([P, hi - lo], F32, name=f"acc_o{lo}", tag="bank") for lo, hi in cuts]
         for i, (lo, hi) in enumerate(cuts):
             nc.tensor.matmul_mx(
                 out=acc_o[i][:], lhsT=w2w[:].bitcast(FP4X4), lhsT_scale=ws[:, 0:N],
-                rhs=cc[i][:].bitcast(FP8X4), rhs_scale=cs[i][:], start=False, stop=True,
+                rhs=cc[:, lo:hi].bitcast(FP8X4), rhs_scale=cs[:, lo:hi], start=True, stop=False,
             )
-            nc.scalar.activation(res[i][:], acc_o[i][:], RELU)
+
+        zi = [keep.tile([P, PACK * (hi - lo)], BF16, name=f"zi{lo}", align_bytes=64) for lo, hi in cuts]
+        zc = [keep.tile([P, hi - lo], U32, name=f"zc{lo}", align_bytes=64) for lo, hi in cuts]
+        zs = [keep.tile([P, hi - lo], U8, name=f"zs{lo}", align_bytes=64) for lo, hi in cuts]
+        res = [keep.tile([P, hi - lo], F32, name=f"res{lo}", align_bytes=64) for lo, hi in cuts]
+        z_planes = zp[:].rearrange("p (t v) -> p v t", t=PACK)
+
+        def first_max(i):
+            lo, hi = cuts[i]
+            larger(pairs3[i][:], nb3[i], 2 * (hi - lo))
+
+        def last_max(i):
+            lo, hi = cuts[i]
+            larger(zp[:, 3 * V + lo:3 * V + hi], pairs3[i], hi - lo)
+
+        def weave(i):
+            lo, hi = cuts[i]
+            woven = zi[i][:].rearrange("p (v t) -> p v t", t=PACK)
+            if i == 1:
+                nc.scalar.copy(woven, z_planes[:, lo:hi, :])
+            else:
+                nc.vector.tensor_copy(woven, z_planes[:, lo:hi, :])
+
+        def finish(i):
+            lo, hi = cuts[i]
+            nc.vector.quantize_mx(out=zc[i][:].bitcast(FP8X4), scales=zs[i][:], in_=zi[i][:])
+            nc.tensor.matmul_mx(
+                out=acc_o[i][:], lhsT=w3w[:].bitcast(FP4X4), lhsT_scale=ws[:, N:2 * N],
+                rhs=zc[i][:].bitcast(FP8X4), rhs_scale=zs[i][:], start=False, stop=True,
+            )
+            if i < 2:
+                nc.scalar.activation(res[i][:], acc_o[i][:], RELU)
+            else:
+                nc.vector.tensor_scalar_max(res[i][:], acc_o[i][:], 0.0)
             nc.sync.dma_start(out[:, lo:hi], res[i][:])
+
+        first_max(0)
+        larger(zp[:, 2 * V:3 * V], pairs2, V)
+        last_max(0)
+        first_max(1)
+        weave(0)
+        last_max(1)
+        weave(1)
+        first_max(2)
+        finish(0)
+        last_max(2)
+        weave(2)
+        finish(1)
+        finish(2)

@@ -152,9 +152,9 @@ def tile_picked_sagecat_maxrelu_p_kernel(
         def centre(engine, t, lo, hi):
             fetch(engine, cp[:, t * V + lo:t * V + hi], t, cen_sb[:, lo // 16:hi // 16])
 
-        def neighbours(engine, dst, t, lo, hi):
+        def neighbours(engine, dst, t, lo, hi, first=0, last=4):
             n = hi - lo
-            for d in range(4):
+            for d in range(first, last):
                 fetch(engine, dst[:, d * n:(d + 1) * n], t, pos_sb[d][:, lo // 16:hi // 16])
 
         def larger(dst, src, n):
@@ -164,11 +164,12 @@ def tile_picked_sagecat_maxrelu_p_kernel(
         for t in range(2):
             for d in range(4):
                 fetch("vector", nb01[:, (2 * d + t) * V:(2 * d + t + 1) * V], t, pos_sb[d][:])
+        neighbours("vector", nb3[0], 3, 0, V // 2, 0, 1)
         for t in (1, 2, 3):
             centre("scalar", t, 0, V)
         neighbours("scalar", nb2, 2, 0, V)
         for i, (lo, hi) in enumerate(cuts):
-            neighbours("scalar", nb3[i], 3, lo, hi)
+            neighbours("scalar", nb3[i], 3, lo, hi, 1 if i == 0 else 0)
 
         ci = keep.tile([P, PACK * V], BF16, name="ci", align_bytes=64)
         cc = keep.tile([P, V], U32, name="cc", align_bytes=64)
@@ -202,13 +203,10 @@ def tile_picked_sagecat_maxrelu_p_kernel(
             lo, hi = cuts[i]
             larger(zp[:, 3 * V + lo:3 * V + hi], pairs3[i], hi - lo)
 
-        def weave(i):
-            lo, hi = cuts[i]
+        def weave(copy, i, lo, hi):
+            first = cuts[i][0]
             woven = zi[i][:].rearrange("p (v t) -> p v t", t=PACK)
-            if i == 1:
-                nc.scalar.copy(woven, z_planes[:, lo:hi, :])
-            else:
-                nc.vector.tensor_copy(woven, z_planes[:, lo:hi, :])
+            copy(woven[:, lo - first:hi - first, :], z_planes[:, lo:hi, :])
 
         def finish(i):
             lo, hi = cuts[i]
@@ -227,12 +225,13 @@ def tile_picked_sagecat_maxrelu_p_kernel(
         larger(zp[:, 2 * V:3 * V], pairs2, V)
         last_max(0)
         first_max(1)
-        weave(0)
+        weave(nc.scalar.copy, 0, 0, V // 4)
+        weave(nc.vector.tensor_copy, 0, V // 4, V // 2)
         last_max(1)
-        weave(1)
+        weave(nc.scalar.copy, 1, *cuts[1])
         first_max(2)
         finish(0)
         last_max(2)
-        weave(2)
+        weave(nc.vector.tensor_copy, 2, *cuts[2])
         finish(1)
         finish(2)

@@ -24,8 +24,6 @@ PACK = 4
 BANK = 512
 EARLY = 384
 ROWS0 = 112
-FIRST = 256
-WARM = 5
 
 
 def tile_picked_sagecat_maxrelu_p_kernel(
@@ -69,14 +67,7 @@ def tile_picked_sagecat_maxrelu_p_kernel(
             )
 
         xg = keep.tile([P, S], U32, name="xg", align_bytes=64)
-        for lo, hi in ((0, FIRST), (FIRST, S)):
-            nc.vector.tensor_copy(xg[:, lo:hi], xw[:].bitcast(U32).indirect(offs_sb[:, lo // 16:hi // 16]))
-        idle = psum.tile([P, FIRST], F32, name="idle", tag="bank")
-        for i in range(WARM):
-            nc.tensor.matmul_mx(
-                out=idle[:], lhsT=xg[:, 0:P].bitcast(FP8X4), lhsT_scale=sg[:, 0:P],
-                rhs=xg[:, 0:FIRST].bitcast(FP8X4), rhs_scale=sg[:, 0:FIRST], start=True, stop=True,
-            )
+        nc.vector.tensor_copy(xg[:], xw[:].bitcast(U32).indirect(offs_sb[:]))
 
         w1g = keep.tile([P, PACK * PACK * P], BF16, name="w1g", align_bytes=64)
         w1c = [keep.tile([P, P], U32, name=f"w1c{t}", align_bytes=64) for t in range(2)]
@@ -84,9 +75,9 @@ def tile_picked_sagecat_maxrelu_p_kernel(
         w1s = keep.tile([P, H], U8, name="w1s", align_bytes=64)
         dealt = w1g[:].rearrange("p (t m j) -> p m t j", t=PACK, j=PACK)
 
-        def views(a, t_lo, t_hi):
+        def views(a, t_lo, t_hi, m_lo=0, m_hi=P):
             raw = w1_raw[a][:].rearrange("p j (m t) -> p m t j", t=PACK)
-            return dealt[:, :, t_lo:t_hi, 2 * a:2 * a + 2], raw[:, :, t_lo:t_hi, :]
+            return dealt[:, m_lo:m_hi, t_lo:t_hi, 2 * a:2 * a + 2], raw[:, m_lo:m_hi, t_lo:t_hi, :]
 
         def deal(a, t_lo, t_hi):
             nc.scalar.activation(*views(a, t_lo, t_hi), COPY)
@@ -94,12 +85,12 @@ def tile_picked_sagecat_maxrelu_p_kernel(
         deal(0, 0, 1)
         deal(0, 1, 2)
         nc.gpsimd.tensor_scalar(*views(0, 2, PACK), 1.0, 0.0, MULT, ADD)
-        nc.vector.tensor_copy(*views(1, 0, 1))
-        nc.vector.tensor_copy(*views(1, 1, 2))
+        nc.scalar.activation(*views(1, 0, 1, 0, P // 2), COPY)
+        nc.vector.tensor_copy(*views(1, 0, 1, P // 2, P))
         nc.vector.quantize_mx(out=w1c[0][:].bitcast(FP8X4), scales=w1s[:, 0:P], in_=w1g[:, 0:H])
-        deal(1, 2, PACK)
+        deal(1, 1, 2)
         nc.vector.quantize_mx(out=w1c[1][:].bitcast(FP8X4), scales=w1s[:, P:2 * P], in_=w1g[:, H:2 * H])
-        nc.vector.quantize_mx(out=w1c_late[:].bitcast(FP8X4), scales=w1s[:, 2 * P:H], in_=w1g[:, 2 * H:4 * H])
+        deal(1, 2, PACK)
         w1_codes = [w1c[0][:], w1c[1][:], w1c_late[:, 0:P], w1c_late[:, P:2 * P]]
 
         ws = keep.tile([P, 2 * N], U8, name="ws", tag="xs", align_bytes=64)
@@ -114,11 +105,12 @@ def tile_picked_sagecat_maxrelu_p_kernel(
             nc.sync.dma_start(ws[r:P:32, 0:N].bitcast(I32), w2_scales[0, r:16:4, :].bitcast(I32))
 
         h = [keep.tile([P, S], F32, name=f"h{t}", align_bytes=64) for t in range(PACK)]
+        pieces = [(0, 256, 512, 768, S), (0, 256, 512, S), (0, 512, S), (0, 512, S)]
         for t in range(PACK):
-            width = BANK // 2 if t == 0 else BANK
-            for lo in range(0, S, width):
-                hi = lo + width
-                acc = psum.tile([P, width], F32, name="acc", tag="bank")
+            for lo, hi in zip(pieces[t], pieces[t][1:]):
+                if t == 0 and lo == 512:
+                    nc.vector.quantize_mx(out=w1c_late[:].bitcast(FP8X4), scales=w1s[:, 2 * P:H], in_=w1g[:, 2 * H:4 * H])
+                acc = psum.tile([P, hi - lo], F32, name="acc", tag="bank")
                 nc.tensor.matmul_mx(
                     out=acc[:],
                     lhsT=w1_codes[t].bitcast(FP8X4),
@@ -128,7 +120,7 @@ def tile_picked_sagecat_maxrelu_p_kernel(
                     start=True,
                     stop=True,
                 )
-                if t == 0 and (lo // width) % 2 == 1:
+                if t == 0 and lo != 512:
                     nc.vector.tensor_scalar_max(h[t][:, lo:hi], acc[:], 0.0)
                 else:
                     nc.scalar.activation(h[t][:, lo:hi], acc[:], RELU)
@@ -164,12 +156,13 @@ def tile_picked_sagecat_maxrelu_p_kernel(
         for t in range(2):
             for d in range(4):
                 fetch("vector", nb01[:, (2 * d + t) * V:(2 * d + t + 1) * V], t, pos_sb[d][:])
-        neighbours("vector", nb3[0], 3, 0, V // 2, 0, 1)
+        for i in range(2):
+            neighbours("vector", nb3[i], 3, *cuts[i], 0, 1)
         for t in (1, 2, 3):
             centre("scalar", t, 0, V)
         neighbours("scalar", nb2, 2, 0, V)
         for i, (lo, hi) in enumerate(cuts):
-            neighbours("scalar", nb3[i], 3, lo, hi, 1 if i == 0 else 0)
+            neighbours("scalar", nb3[i], 3, lo, hi, 1 if i < 2 else 0)
 
         ci = keep.tile([P, PACK * V], BF16, name="ci", align_bytes=64)
         cc = keep.tile([P, V], U32, name="cc", align_bytes=64)

@@ -24,6 +24,7 @@ PACK = 4
 BANK = 512
 EARLY = 384
 ROWS0 = 112
+SHARE = 40
 
 
 def tile_picked_sagecat_maxrelu_p_kernel(
@@ -42,7 +43,7 @@ def tile_picked_sagecat_maxrelu_p_kernel(
         xw = keep.tile([P, T], I32, name="xw", align_bytes=64)
         xs = keep.tile([P, T], U8, name="xs", tag="xs", align_bytes=64)
         sgm = keep.tile([P, S], U8, name="sgm", align_bytes=64)
-        w1_raw = [keep.tile([P, 2, H], F32, name=f"w1_raw{a}", tag=f"raw{a}", align_bytes=64) for a in range(2)]
+        w1_raw = keep.tile([P, PACK, H], F32, name="w1_raw", tag="raw", align_bytes=64)
 
         nc.vector.memset(xs[0:ROWS0, :].bitcast(I32), 0)
         nc.vector.memset(sgm[:].bitcast(I32), 0)
@@ -53,9 +54,8 @@ def tile_picked_sagecat_maxrelu_p_kernel(
         nc.sync.dma_start(xw[:], x_words[0].rearrange("p n r -> p (n r)").bitcast(I32))
         nc.sync.dma_start(pos_sb[0][:], pos1)
         nc.sync.dma_start(pos_sb[1][:], pos2)
+        nc.sync.dma_start(w1_raw[:], w1_rows)
         nc.sync.dma_start(pos_sb[2][:], pos3)
-        nc.sync.dma_start(w1_raw[0][:], w1_rows[:, 0:2, :])
-        nc.sync.dma_start(w1_raw[1][:], w1_rows[:, 2:PACK, :])
         nc.sync.dma_start(pos_sb[3][:], pos4)
         nc.sync.dma_start(cen_sb[:], cen)
 
@@ -69,36 +69,32 @@ def tile_picked_sagecat_maxrelu_p_kernel(
         xg = keep.tile([P, S], U32, name="xg", align_bytes=64)
         nc.vector.tensor_copy(xg[:], xw[:].bitcast(U32).indirect(offs_sb[:]))
 
-        w1g = keep.tile([P, PACK * PACK * P], BF16, name="w1g", align_bytes=64)
         w1c = [keep.tile([P, P], U32, name=f"w1c{t}", align_bytes=64) for t in range(2)]
         w1c_late = keep.tile([P, 2 * P], U32, name="w1c_late", align_bytes=64)
         w1s = keep.tile([P, H], U8, name="w1s", align_bytes=64)
-        dealt = w1g[:].rearrange("p (t m j) -> p m t j", t=PACK, j=PACK)
+        raw = w1_raw[:].rearrange("p j (m t) -> p m t j", t=PACK)
 
-        def views(a, t_lo, t_hi, m_lo=0, m_hi=P):
-            raw = w1_raw[a][:].rearrange("p j (m t) -> p m t j", t=PACK)
-            return dealt[:, m_lo:m_hi, t_lo:t_hi, 2 * a:2 * a + 2], raw[:, m_lo:m_hi, t_lo:t_hi, :]
+        def dealt(tile, planes):
+            return tile[:].rearrange("p (t m j) -> p m t j", t=planes, j=PACK)
 
-        def deal(a, t_lo, t_hi):
-            nc.scalar.activation(*views(a, t_lo, t_hi), COPY)
-
-        deal(0, 0, 1)
-        deal(0, 1, 2)
-        nc.gpsimd.tensor_scalar(*views(0, 2, PACK), 1.0, 0.0, MULT, ADD)
-        nc.scalar.activation(*views(1, 0, 1, 0, P // 2), COPY)
-        nc.vector.tensor_copy(*views(1, 0, 1, P // 2, P))
-        nc.vector.quantize_mx(out=w1c[0][:].bitcast(FP8X4), scales=w1s[:, 0:P], in_=w1g[:, 0:H])
-        deal(1, 1, 2)
-        nc.vector.quantize_mx(out=w1c[1][:].bitcast(FP8X4), scales=w1s[:, P:2 * P], in_=w1g[:, H:2 * H])
-        deal(1, 2, PACK)
+        first = keep.tile([P, H], BF16, name="w1g0", tag="w1g", align_bytes=64)
+        late = keep.tile([P, 2 * H], BF16, name="w1g23", align_bytes=64)
+        nc.scalar.activation(dealt(first, 1)[:, 0:SHARE], raw[:, 0:SHARE, 0:1, :], COPY)
+        nc.vector.tensor_copy(dealt(first, 1)[:, SHARE:P], raw[:, SHARE:P, 0:1, :])
+        nc.vector.quantize_mx(out=w1c[0][:].bitcast(FP8X4), scales=w1s[:, 0:P], in_=first[:])
+        nc.scalar.activation(dealt(late, 2), raw[:, :, 2:PACK, :], COPY)
+        second = keep.tile([P, H], BF16, name="w1g1", tag="w1g", align_bytes=64)
+        nc.vector.tensor_copy(dealt(second, 1), raw[:, :, 1:2, :])
+        nc.vector.quantize_mx(out=w1c[1][:].bitcast(FP8X4), scales=w1s[:, P:2 * P], in_=second[:])
+        nc.vector.quantize_mx(out=w1c_late[:].bitcast(FP8X4), scales=w1s[:, 2 * P:H], in_=late[:])
         w1_codes = [w1c[0][:], w1c[1][:], w1c_late[:, 0:P], w1c_late[:, P:2 * P]]
 
         ws = keep.tile([P, 2 * N], U8, name="ws", tag="xs", align_bytes=64)
-        w3w = keep.tile([P, 2 * N], U8, name="w3w", tag="raw0", align_bytes=64)
-        w2w = keep.tile([P, 2 * N], U8, name="w2w", tag="raw1", align_bytes=64)
+        ww = keep.tile([P, 4 * N], U8, name="ww", tag="raw", align_bytes=64)
+        w3w, w2w = ww[:, 0:2 * N], ww[:, 2 * N:4 * N]
         nc.gpsimd.memset(ws[:].bitcast(I32), 0)
-        nc.sync.dma_start(w3w[:].bitcast(I32), w3_words[0].bitcast(I32))
-        nc.sync.dma_start(w2w[:].bitcast(I32), w2_words[0].bitcast(I32))
+        nc.sync.dma_start(w3w.bitcast(I32), w3_words[0].bitcast(I32))
+        nc.sync.dma_start(w2w.bitcast(I32), w2_words[0].bitcast(I32))
         for r in range(4):
             nc.sync.dma_start(ws[r:P:32, N:2 * N].bitcast(I32), w3_scales[0, r:16:4, :].bitcast(I32))
         for r in range(4):
@@ -108,8 +104,6 @@ def tile_picked_sagecat_maxrelu_p_kernel(
         pieces = [(0, 256, 512, 768, S), (0, 256, 512, S), (0, 512, S), (0, 512, S)]
         for t in range(PACK):
             for lo, hi in zip(pieces[t], pieces[t][1:]):
-                if t == 0 and lo == 512:
-                    nc.vector.quantize_mx(out=w1c_late[:].bitcast(FP8X4), scales=w1s[:, 2 * P:H], in_=w1g[:, 2 * H:4 * H])
                 acc = psum.tile([P, hi - lo], F32, name="acc", tag="bank")
                 nc.tensor.matmul_mx(
                     out=acc[:],
@@ -120,7 +114,7 @@ def tile_picked_sagecat_maxrelu_p_kernel(
                     start=True,
                     stop=True,
                 )
-                if t == 0 and lo != 512:
+                if t == 0 and hi == S:
                     nc.vector.tensor_scalar_max(h[t][:, lo:hi], acc[:], 0.0)
                 else:
                     nc.scalar.activation(h[t][:, lo:hi], acc[:], RELU)
@@ -137,16 +131,16 @@ def tile_picked_sagecat_maxrelu_p_kernel(
         pairs01 = keep.tile([P, 4 * V], BF16, name="pairs01", align_bytes=64)
         nb2 = keep.tile([P, 4 * V], BF16, name="nb2", align_bytes=64)
         pairs2 = keep.tile([P, 2 * V], BF16, name="pairs2", align_bytes=64)
-        nb3 = [keep.tile([P, 4 * (hi - lo)], BF16, name=f"nb3_{lo}", align_bytes=64) for lo, hi in cuts]
+        nb3 = keep.tile([P, 4 * V], BF16, name="nb3", align_bytes=64)
         pairs3 = [keep.tile([P, 2 * (hi - lo)], BF16, name=f"pairs3_{lo}", align_bytes=64) for lo, hi in cuts]
         zp = keep.tile([P, PACK * V], BF16, name="zp", align_bytes=64)
 
         def centre(engine, t, lo, hi):
             fetch(engine, cp[:, t * V + lo:t * V + hi], t, cen_sb[:, lo // 16:hi // 16])
 
-        def neighbours(engine, dst, t, lo, hi, first=0, last=4):
+        def neighbours(engine, dst, t, lo, hi):
             n = hi - lo
-            for d in range(first, last):
+            for d in range(4):
                 fetch(engine, dst[:, d * n:(d + 1) * n], t, pos_sb[d][:, lo // 16:hi // 16])
 
         def larger(dst, src, n):
@@ -156,13 +150,13 @@ def tile_picked_sagecat_maxrelu_p_kernel(
         for t in range(2):
             for d in range(4):
                 fetch("vector", nb01[:, (2 * d + t) * V:(2 * d + t + 1) * V], t, pos_sb[d][:])
-        for i in range(2):
-            neighbours("vector", nb3[i], 3, *cuts[i], 0, 1)
+        fetch("vector", nb3[:, 0:V], 3, pos_sb[0][:])
         for t in (1, 2, 3):
             centre("scalar", t, 0, V)
         neighbours("scalar", nb2, 2, 0, V)
-        for i, (lo, hi) in enumerate(cuts):
-            neighbours("scalar", nb3[i], 3, lo, hi, 1 if i < 2 else 0)
+        for lo, hi in cuts:
+            for d in range(1, 4):
+                fetch("scalar", nb3[:, d * V + lo:d * V + hi], 3, pos_sb[d][:, lo // 16:hi // 16])
 
         ci = keep.tile([P, PACK * V], BF16, name="ci", align_bytes=64)
         cc = keep.tile([P, V], U32, name="cc", align_bytes=64)
@@ -178,7 +172,7 @@ def tile_picked_sagecat_maxrelu_p_kernel(
         acc_o = [psum.tile([P, hi - lo], F32, name=f"acc_o{lo}", tag="bank") for lo, hi in cuts]
         for i, (lo, hi) in enumerate(cuts):
             nc.tensor.matmul_mx(
-                out=acc_o[i][:], lhsT=w2w[:].bitcast(FP4X4), lhsT_scale=ws[:, 0:N],
+                out=acc_o[i][:], lhsT=w2w.bitcast(FP4X4), lhsT_scale=ws[:, 0:N],
                 rhs=cc[:, lo:hi].bitcast(FP8X4), rhs_scale=cs[:, lo:hi], start=True, stop=False,
             )
 
@@ -190,7 +184,8 @@ def tile_picked_sagecat_maxrelu_p_kernel(
 
         def first_max(i):
             lo, hi = cuts[i]
-            larger(pairs3[i][:], nb3[i], 2 * (hi - lo))
+            both = nb3[:].rearrange("p (f e v) -> p f e v", f=2, e=2)[:, :, :, lo:hi]
+            nc.vector.tensor_tensor(pairs3[i][:].rearrange("p (e v) -> p e v", e=2), both[:, 0], both[:, 1], MAX)
 
         def last_max(i):
             lo, hi = cuts[i]
@@ -205,7 +200,7 @@ def tile_picked_sagecat_maxrelu_p_kernel(
             lo, hi = cuts[i]
             nc.vector.quantize_mx(out=zc[i][:].bitcast(FP8X4), scales=zs[i][:], in_=zi[i][:])
             nc.tensor.matmul_mx(
-                out=acc_o[i][:], lhsT=w3w[:].bitcast(FP4X4), lhsT_scale=ws[:, N:2 * N],
+                out=acc_o[i][:], lhsT=w3w.bitcast(FP4X4), lhsT_scale=ws[:, N:2 * N],
                 rhs=zc[i][:].bitcast(FP8X4), rhs_scale=zs[i][:], start=False, stop=True,
             )
             if i < 2:

@@ -21,10 +21,17 @@ COPY = mybir.ActivationFunctionType.Copy
 
 P = 128
 PACK = 4
+NEIGHBOURS = 4
+GROUP = 16
+QUADRANT = 32
+SCALE_ROWS = 16
+SCALE_FIRST = P - SCALE_ROWS
 BANK = 512
-EARLY = 384
-ROWS0 = 112
-SHARE = 40
+BANKS = 8
+HALF = V // 2
+QUARTER = V // 4
+SCALAR_COLUMNS = 40
+RUN = 4
 
 
 def tile_picked_sagecat_maxrelu_p_kernel(
@@ -34,192 +41,193 @@ def tile_picked_sagecat_maxrelu_p_kernel(
     with ExitStack() as ctx:
         lists = ctx.enter_context(tc.tile_pool(name="lists", bufs=1))
         keep = ctx.enter_context(tc.tile_pool(name="keep", bufs=1))
-        psum = ctx.enter_context(tc.psum_pool(name="psum", bufs=8))
+        psum = ctx.enter_context(tc.psum_pool(name="psum", bufs=BANKS))
 
-        offs_sb = lists.tile([P, S // 16], U16, name="offs_sb")
-        cen_sb = lists.tile([P, V // 16], U16, name="cen_sb")
-        pos_sb = [lists.tile([P, V // 16], U16, name=f"pos_sb{d}") for d in range(4)]
+        offs_sb = lists.tile([P, S // GROUP], U16, name="offs_sb")
+        cen_sb = lists.tile([P, V // GROUP], U16, name="cen_sb")
+        pos_sb = [lists.tile([P, V // GROUP], U16, name=f"pos_sb{d}") for d in range(NEIGHBOURS)]
 
-        xw = keep.tile([P, T], I32, name="xw", align_bytes=64)
-        xs = keep.tile([P, T], U8, name="xs", tag="xs", align_bytes=64)
-        sgm = keep.tile([P, S], U8, name="sgm", align_bytes=64)
-        w1_raw = keep.tile([P, PACK, H], F32, name="w1_raw", tag="raw", align_bytes=64)
+        x_table = keep.tile([P, T], I32, name="x_table", align_bytes=64)
+        scale_table = keep.tile([P, T], U8, name="scale_table", tag="scale_table", align_bytes=64)
+        x_plane = keep.tile([P, S], U8, name="x_plane", align_bytes=64)
+        w1_raw = keep.tile([P, PACK, H], F32, name="w1_raw", tag="w1_raw", align_bytes=64)
 
-        nc.vector.memset(xs[0:ROWS0, :].bitcast(I32), 0)
-        nc.vector.memset(sgm[:].bitcast(I32), 0)
+        nc.vector.memset(scale_table[0:SCALE_FIRST, :].bitcast(I32), 0)
+        nc.vector.memset(x_plane[:].bitcast(I32), 0)
 
-        w1_rows = w1.rearrange("(p j) c -> p j c", j=PACK)
         nc.sync.dma_start(offs_sb[:], offs)
-        nc.sync.dma_start(xs[ROWS0:P, :].bitcast(I32), x_scales[0].bitcast(I32))
-        nc.sync.dma_start(xw[:], x_words[0].rearrange("p n r -> p (n r)").bitcast(I32))
+        nc.sync.dma_start(scale_table[SCALE_FIRST:P, :].bitcast(I32), x_scales[0].bitcast(I32))
+        nc.sync.dma_start(x_table[:], x_words[0].rearrange("p n r -> p (n r)").bitcast(I32))
         nc.sync.dma_start(pos_sb[0][:], pos1)
         nc.sync.dma_start(pos_sb[1][:], pos2)
-        nc.sync.dma_start(w1_raw[:], w1_rows)
+        nc.sync.dma_start(w1_raw[:], w1.rearrange("(p j) c -> p j c", j=PACK))
         nc.sync.dma_start(pos_sb[2][:], pos3)
         nc.sync.dma_start(pos_sb[3][:], pos4)
         nc.sync.dma_start(cen_sb[:], cen)
 
-        sg = keep.tile([P, S], U8, name="sg", align_bytes=64)
-        nc.vector.tensor_copy(sg[:], xs[:].indirect(offs_sb[:]))
-        for q in range(4):
+        picked_scales = keep.tile([P, S], U8, name="picked_scales", align_bytes=64)
+        nc.vector.tensor_copy(picked_scales[:], scale_table[:].indirect(offs_sb[:]))
+        for q in range(P // QUADRANT):
+            row = SCALE_FIRST + PACK * q
             nc.sync.dma_start(
-                sgm[32 * q:32 * q + 4, :].bitcast(I32), sg[ROWS0 + 4 * q:ROWS0 + 4 * q + 4, :].bitcast(I32)
+                x_plane[QUADRANT * q:QUADRANT * q + PACK, :].bitcast(I32), picked_scales[row:row + PACK, :].bitcast(I32)
             )
 
-        xg = keep.tile([P, S], U32, name="xg", align_bytes=64)
-        nc.vector.tensor_copy(xg[:], xw[:].bitcast(U32).indirect(offs_sb[:]))
+        picked_words = keep.tile([P, S], U32, name="picked_words", align_bytes=64)
+        nc.vector.tensor_copy(picked_words[:], x_table[:].bitcast(U32).indirect(offs_sb[:]))
 
-        w1c = [keep.tile([P, P], U32, name=f"w1c{t}", align_bytes=64) for t in range(2)]
-        w1c_late = keep.tile([P, 2 * P], U32, name="w1c_late", align_bytes=64)
-        w1s = keep.tile([P, H], U8, name="w1s", align_bytes=64)
+        codes = [keep.tile([P, P], U32, name=f"w1_codes{t}", align_bytes=64) for t in range(2)]
+        codes23 = keep.tile([P, 2 * P], U32, name="w1_codes23", align_bytes=64)
+        w1_plane = keep.tile([P, H], U8, name="w1_plane", align_bytes=64)
         raw = w1_raw[:].rearrange("p j (m t) -> p m t j", t=PACK)
 
         def dealt(tile, planes):
             return tile[:].rearrange("p (t m j) -> p m t j", t=planes, j=PACK)
 
-        first = keep.tile([P, H], BF16, name="w1g0", tag="w1g", align_bytes=64)
-        late = keep.tile([P, 2 * H], BF16, name="w1g23", align_bytes=64)
-        nc.scalar.activation(dealt(first, 1)[:, 0:SHARE], raw[:, 0:SHARE, 0:1, :], COPY)
-        nc.vector.tensor_copy(dealt(first, 1)[:, SHARE:P], raw[:, SHARE:P, 0:1, :])
-        nc.vector.quantize_mx(out=w1c[0][:].bitcast(FP8X4), scales=w1s[:, 0:P], in_=first[:])
-        nc.scalar.activation(dealt(late, 2), raw[:, :, 2:PACK, :], COPY)
-        second = keep.tile([P, H], BF16, name="w1g1", tag="w1g", align_bytes=64)
-        nc.vector.tensor_copy(dealt(second, 1), raw[:, :, 1:2, :])
-        nc.vector.quantize_mx(out=w1c[1][:].bitcast(FP8X4), scales=w1s[:, P:2 * P], in_=second[:])
-        nc.vector.quantize_mx(out=w1c_late[:].bitcast(FP8X4), scales=w1s[:, 2 * P:H], in_=late[:])
-        w1_codes = [w1c[0][:], w1c[1][:], w1c_late[:, 0:P], w1c_late[:, P:2 * P]]
+        stage0 = keep.tile([P, H], BF16, name="stage0", tag="stage", align_bytes=64)
+        stage23 = keep.tile([P, 2 * H], BF16, name="stage23", align_bytes=64)
+        nc.scalar.activation(dealt(stage0, 1)[:, 0:SCALAR_COLUMNS], raw[:, 0:SCALAR_COLUMNS, 0:1, :], COPY)
+        nc.vector.tensor_copy(dealt(stage0, 1)[:, SCALAR_COLUMNS:P], raw[:, SCALAR_COLUMNS:P, 0:1, :])
+        nc.vector.quantize_mx(out=codes[0][:].bitcast(FP8X4), scales=w1_plane[:, 0:P], in_=stage0[:])
+        nc.scalar.activation(dealt(stage23, 2), raw[:, :, 2:PACK, :], COPY)
+        stage1 = keep.tile([P, H], BF16, name="stage1", tag="stage", align_bytes=64)
+        nc.vector.tensor_copy(dealt(stage1, 1), raw[:, :, 1:2, :])
+        nc.vector.quantize_mx(out=codes[1][:].bitcast(FP8X4), scales=w1_plane[:, P:2 * P], in_=stage1[:])
+        nc.vector.quantize_mx(out=codes23[:].bitcast(FP8X4), scales=w1_plane[:, 2 * P:H], in_=stage23[:])
+        w1_codes = [codes[0][:], codes[1][:], codes23[:, 0:P], codes23[:, P:2 * P]]
 
-        ws = keep.tile([P, 2 * N], U8, name="ws", tag="xs", align_bytes=64)
-        ww = keep.tile([P, 4 * N], U8, name="ww", tag="raw", align_bytes=64)
-        w3w, w2w = ww[:, 0:2 * N], ww[:, 2 * N:4 * N]
-        nc.gpsimd.memset(ws[:].bitcast(I32), 0)
-        nc.sync.dma_start(w3w.bitcast(I32), w3_words[0].bitcast(I32))
-        nc.sync.dma_start(w2w.bitcast(I32), w2_words[0].bitcast(I32))
-        for r in range(4):
-            nc.sync.dma_start(ws[r:P:32, N:2 * N].bitcast(I32), w3_scales[0, r:16:4, :].bitcast(I32))
-        for r in range(4):
-            nc.sync.dma_start(ws[r:P:32, 0:N].bitcast(I32), w2_scales[0, r:16:4, :].bitcast(I32))
+        out_plane = keep.tile([P, 2 * N], U8, name="out_plane", tag="scale_table", align_bytes=64)
+        out_words = keep.tile([P, 4 * N], U8, name="out_words", tag="w1_raw", align_bytes=64)
+        w3_sb, w2_sb = out_words[:, 0:2 * N], out_words[:, 2 * N:4 * N]
+        w2_plane, w3_plane = out_plane[:, 0:N], out_plane[:, N:2 * N]
+        nc.gpsimd.memset(out_plane[:].bitcast(I32), 0)
+        nc.sync.dma_start(w3_sb.bitcast(I32), w3_words[0].bitcast(I32))
+        nc.sync.dma_start(w2_sb.bitcast(I32), w2_words[0].bitcast(I32))
+        for scales, first in ((w3_scales, N), (w2_scales, 0)):
+            for r in range(PACK):
+                nc.sync.dma_start(
+                    out_plane[r:P:QUADRANT, first:first + N].bitcast(I32), scales[0, r:SCALE_ROWS:PACK, :].bitcast(I32)
+                )
 
         h = [keep.tile([P, S], F32, name=f"h{t}", align_bytes=64) for t in range(PACK)]
-        pieces = [(0, 256, 512, 768, S), (0, 256, 512, S), (0, 512, S), (0, 512, S)]
         for t in range(PACK):
-            for lo, hi in zip(pieces[t], pieces[t][1:]):
-                acc = psum.tile([P, hi - lo], F32, name="acc", tag="bank")
-                nc.tensor.matmul_mx(
-                    out=acc[:],
-                    lhsT=w1_codes[t].bitcast(FP8X4),
-                    lhsT_scale=w1s[:, t * P:(t + 1) * P],
-                    rhs=xg[:, lo:hi].bitcast(FP8X4),
-                    rhs_scale=sgm[:, lo:hi],
-                    start=True,
-                    stop=True,
-                )
-                if t == 0 and hi == S:
-                    nc.vector.tensor_scalar_max(h[t][:, lo:hi], acc[:], 0.0)
-                else:
-                    nc.scalar.activation(h[t][:, lo:hi], acc[:], RELU)
+            for bank in range(0, S, BANK):
+                width = BANK // 2 if t * S + bank < 3 * BANK else BANK
+                for lo in range(bank, bank + BANK, width):
+                    hi = lo + width
+                    acc = psum.tile([P, width], F32, name="acc", tag="bank")
+                    nc.tensor.matmul_mx(
+                        out=acc[:],
+                        lhsT=w1_codes[t].bitcast(FP8X4),
+                        lhsT_scale=w1_plane[:, t * P:(t + 1) * P],
+                        rhs=picked_words[:, lo:hi].bitcast(FP8X4),
+                        rhs_scale=x_plane[:, lo:hi],
+                        start=True,
+                        stop=True,
+                    )
+                    if t == 0 and hi == S:
+                        nc.vector.tensor_scalar_max(h[t][:, lo:hi], acc[:], 0.0)
+                    else:
+                        nc.scalar.activation(h[t][:, lo:hi], acc[:], RELU)
 
-        def fetch(engine, dst, t, offsets):
-            if engine == "vector":
-                nc.vector.tensor_copy(dst, h[t][:].indirect(offsets))
-            else:
-                nc.scalar.activation(dst, h[t][:].indirect(offsets), COPY)
+        def fetch_vector(dst, t, offsets):
+            nc.vector.tensor_copy(dst, h[t][:].indirect(offsets))
 
-        cuts = ((0, V // 2), (V // 2, EARLY), (EARLY, V))
-        cp = keep.tile([P, PACK * V], BF16, name="cp", align_bytes=64)
-        nb01 = keep.tile([P, 8 * V], BF16, name="nb01", align_bytes=64)
-        pairs01 = keep.tile([P, 4 * V], BF16, name="pairs01", align_bytes=64)
-        nb2 = keep.tile([P, 4 * V], BF16, name="nb2", align_bytes=64)
+        def fetch_scalar(dst, t, offsets):
+            nc.scalar.activation(dst, h[t][:].indirect(offsets), COPY)
+
+        def run(tile, index, width=V):
+            return tile[:, index * width:(index + 1) * width]
+
+        halves = ((0, HALF), (HALF, V))
+        cuts = ((0, HALF), (HALF, HALF + QUARTER), (HALF + QUARTER, V))
+        centres = keep.tile([P, PACK * V], BF16, name="centres", align_bytes=64)
+        near01 = keep.tile([P, 2 * NEIGHBOURS * V], BF16, name="near01", align_bytes=64)
+        pairs01 = keep.tile([P, NEIGHBOURS * V], BF16, name="pairs01", align_bytes=64)
+        near2 = keep.tile([P, NEIGHBOURS * V], BF16, name="near2", align_bytes=64)
         pairs2 = keep.tile([P, 2 * V], BF16, name="pairs2", align_bytes=64)
-        nb3 = keep.tile([P, 4 * V], BF16, name="nb3", align_bytes=64)
-        pairs3 = [keep.tile([P, 2 * (hi - lo)], BF16, name=f"pairs3_{lo}", align_bytes=64) for lo, hi in cuts]
-        zp = keep.tile([P, PACK * V], BF16, name="zp", align_bytes=64)
+        near3 = keep.tile([P, NEIGHBOURS * V], BF16, name="near3", align_bytes=64)
+        pairs3 = [keep.tile([P, 2 * HALF], BF16, name=f"pairs3_{lo}", align_bytes=64) for lo, hi in halves]
+        z = keep.tile([P, PACK * V], BF16, name="z", align_bytes=64)
 
-        def centre(engine, t, lo, hi):
-            fetch(engine, cp[:, t * V + lo:t * V + hi], t, cen_sb[:, lo // 16:hi // 16])
+        def larger_half(dst, tile):
+            width = tile.shape[1] // 2
+            nc.vector.tensor_tensor(dst, run(tile, 0, width), run(tile, 1, width), MAX)
 
-        def neighbours(engine, dst, t, lo, hi):
-            n = hi - lo
-            for d in range(4):
-                fetch(engine, dst[:, d * n:(d + 1) * n], t, pos_sb[d][:, lo // 16:hi // 16])
-
-        def larger(dst, src, n):
-            nc.vector.tensor_tensor(dst, src[:, 0:n], src[:, n:2 * n], MAX)
-
-        centre("vector", 0, 0, V)
+        fetch_vector(run(centres, 0), 0, cen_sb[:])
         for t in range(2):
-            for d in range(4):
-                fetch("vector", nb01[:, (2 * d + t) * V:(2 * d + t + 1) * V], t, pos_sb[d][:])
-        fetch("vector", nb3[:, 0:V], 3, pos_sb[0][:])
-        for t in (1, 2, 3):
-            centre("scalar", t, 0, V)
-        neighbours("scalar", nb2, 2, 0, V)
-        for lo, hi in cuts:
-            for d in range(1, 4):
-                fetch("scalar", nb3[:, d * V + lo:d * V + hi], 3, pos_sb[d][:, lo // 16:hi // 16])
+            for d in range(NEIGHBOURS):
+                fetch_vector(run(near01, 2 * d + t), t, pos_sb[d][:])
+        fetch_vector(run(near3, 0), 3, pos_sb[0][:])
+        for t in range(1, PACK):
+            fetch_scalar(run(centres, t), t, cen_sb[:])
+        for d in range(NEIGHBOURS):
+            fetch_scalar(run(near2, d), 2, pos_sb[d][:])
+        for lo, hi in halves:
+            for d in range(1, NEIGHBOURS):
+                fetch_scalar(near3[:, d * V + lo:d * V + hi], 3, pos_sb[d][:, lo // GROUP:hi // GROUP])
 
-        ci = keep.tile([P, PACK * V], BF16, name="ci", align_bytes=64)
-        cc = keep.tile([P, V], U32, name="cc", align_bytes=64)
-        cs = keep.tile([P, V], U8, name="cs", align_bytes=64)
+        centres_woven = keep.tile([P, PACK * V], BF16, name="centres_woven", align_bytes=64)
+        centre_codes = keep.tile([P, V], U32, name="centre_codes", align_bytes=64)
+        centre_plane = keep.tile([P, V], U8, name="centre_plane", align_bytes=64)
         nc.gpsimd.tensor_scalar(
-            ci[:].rearrange("p (v t) -> p v t", t=PACK), cp[:].rearrange("p (t v) -> p v t", t=PACK), 1.0, 0.0, MULT, ADD
+            centres_woven[:].rearrange("p (v t) -> p v t", t=PACK), centres[:].rearrange("p (t v) -> p v t", t=PACK),
+            1.0, 0.0, MULT, ADD,
         )
-        larger(pairs01[:], nb01, 4 * V)
-        larger(pairs2[:], nb2, 2 * V)
-        larger(zp[:, 0:2 * V], pairs01, 2 * V)
-        nc.vector.quantize_mx(out=cc[:].bitcast(FP8X4), scales=cs[:], in_=ci[:])
+        larger_half(pairs01[:], near01)
+        larger_half(pairs2[:], near2)
+        larger_half(z[:, 0:2 * V], pairs01)
+        nc.vector.quantize_mx(out=centre_codes[:].bitcast(FP8X4), scales=centre_plane[:], in_=centres_woven[:])
 
-        acc_o = [psum.tile([P, hi - lo], F32, name=f"acc_o{lo}", tag="bank") for lo, hi in cuts]
+        sums = [psum.tile([P, hi - lo], F32, name=f"sums{lo}", tag="bank") for lo, hi in cuts]
         for i, (lo, hi) in enumerate(cuts):
             nc.tensor.matmul_mx(
-                out=acc_o[i][:], lhsT=w2w.bitcast(FP4X4), lhsT_scale=ws[:, 0:N],
-                rhs=cc[:, lo:hi].bitcast(FP8X4), rhs_scale=cs[:, lo:hi], start=True, stop=False,
+                out=sums[i][:], lhsT=w2_sb.bitcast(FP4X4), lhsT_scale=w2_plane,
+                rhs=centre_codes[:, lo:hi].bitcast(FP8X4), rhs_scale=centre_plane[:, lo:hi], start=True, stop=False,
             )
 
-        zi = [keep.tile([P, PACK * (hi - lo)], BF16, name=f"zi{lo}", align_bytes=64) for lo, hi in cuts]
-        zc = [keep.tile([P, hi - lo], U32, name=f"zc{lo}", align_bytes=64) for lo, hi in cuts]
-        zs = [keep.tile([P, hi - lo], U8, name=f"zs{lo}", align_bytes=64) for lo, hi in cuts]
-        res = [keep.tile([P, hi - lo], F32, name=f"res{lo}", align_bytes=64) for lo, hi in cuts]
-        z_planes = zp[:].rearrange("p (t v) -> p v t", t=PACK)
+        z_woven = [keep.tile([P, PACK * (hi - lo)], BF16, name=f"z_woven{lo}", align_bytes=64) for lo, hi in cuts]
+        z_codes = [keep.tile([P, hi - lo], U32, name=f"z_codes{lo}", align_bytes=64) for lo, hi in cuts]
+        z_plane = [keep.tile([P, hi - lo], U8, name=f"z_plane{lo}", align_bytes=64) for lo, hi in cuts]
+        result = [keep.tile([P, hi - lo], F32, name=f"result{lo}", align_bytes=64) for lo, hi in cuts]
+        z_runs = z[:].rearrange("p (t c r) -> p c t r", t=PACK, r=RUN)
 
-        def first_max(i):
-            lo, hi = cuts[i]
-            both = nb3[:].rearrange("p (f e v) -> p f e v", f=2, e=2)[:, :, :, lo:hi]
+        def plane3_pairs(i):
+            lo, hi = halves[i]
+            both = near3[:].rearrange("p (f e v) -> p f e v", f=2, e=2)[:, :, :, lo:hi]
             nc.vector.tensor_tensor(pairs3[i][:].rearrange("p (e v) -> p e v", e=2), both[:, 0], both[:, 1], MAX)
 
-        def last_max(i):
-            lo, hi = cuts[i]
-            larger(zp[:, 3 * V + lo:3 * V + hi], pairs3[i], hi - lo)
+        def plane3_largest(i):
+            lo, hi = halves[i]
+            larger_half(z[:, 3 * V + lo:3 * V + hi], pairs3[i])
 
         def weave(copy, i, lo, hi):
-            first = cuts[i][0]
-            woven = zi[i][:].rearrange("p (v t) -> p v t", t=PACK)
-            copy(woven[:, lo - first:hi - first, :], z_planes[:, lo:hi, :])
+            start = cuts[i][0]
+            woven = z_woven[i][:].rearrange("p (c r t) -> p c t r", t=PACK, r=RUN)
+            copy(woven[:, (lo - start) // RUN:(hi - start) // RUN], z_runs[:, lo // RUN:hi // RUN])
 
         def finish(i):
             lo, hi = cuts[i]
-            nc.vector.quantize_mx(out=zc[i][:].bitcast(FP8X4), scales=zs[i][:], in_=zi[i][:])
+            nc.vector.quantize_mx(out=z_codes[i][:].bitcast(FP8X4), scales=z_plane[i][:], in_=z_woven[i][:])
             nc.tensor.matmul_mx(
-                out=acc_o[i][:], lhsT=w3w.bitcast(FP4X4), lhsT_scale=ws[:, N:2 * N],
-                rhs=zc[i][:].bitcast(FP8X4), rhs_scale=zs[i][:], start=False, stop=True,
+                out=sums[i][:], lhsT=w3_sb.bitcast(FP4X4), lhsT_scale=w3_plane,
+                rhs=z_codes[i][:].bitcast(FP8X4), rhs_scale=z_plane[i][:], start=False, stop=True,
             )
-            if i < 2:
-                nc.scalar.activation(res[i][:], acc_o[i][:], RELU)
+            if hi < V:
+                nc.scalar.activation(result[i][:], sums[i][:], RELU)
             else:
-                nc.vector.tensor_scalar_max(res[i][:], acc_o[i][:], 0.0)
-            nc.sync.dma_start(out[:, lo:hi], res[i][:])
+                nc.vector.tensor_scalar_max(result[i][:], sums[i][:], 0.0)
+            nc.sync.dma_start(out[:, lo:hi], result[i][:])
 
-        first_max(0)
-        larger(zp[:, 2 * V:3 * V], pairs2, V)
-        last_max(0)
-        first_max(1)
-        weave(nc.scalar.copy, 0, 0, V // 4)
-        weave(nc.vector.tensor_copy, 0, V // 4, V // 2)
-        last_max(1)
+        plane3_pairs(0)
+        larger_half(run(z, 2), pairs2)
+        plane3_largest(0)
+        weave(nc.scalar.copy, 0, 0, QUARTER)
+        plane3_pairs(1)
+        weave(nc.vector.tensor_copy, 0, QUARTER, HALF)
+        plane3_largest(1)
         weave(nc.scalar.copy, 1, *cuts[1])
-        first_max(2)
         finish(0)
-        last_max(2)
         weave(nc.vector.tensor_copy, 2, *cuts[2])
         finish(1)
         finish(2)

@@ -32,6 +32,7 @@ HALF = V // 2
 QUARTER = V // 4
 SCALAR_COLUMNS = 40
 RUN = 4
+VECTOR_TARGETS = HALF
 
 
 def tile_picked_sagecat_maxrelu_p_kernel(
@@ -139,15 +140,18 @@ def tile_picked_sagecat_maxrelu_p_kernel(
         def run(tile, index, width=V):
             return tile[:, index * width:(index + 1) * width]
 
-        halves = ((0, HALF), (HALF, V))
+        def entries(tile, lo, hi):
+            return tile[:, lo // GROUP:hi // GROUP]
+
         cuts = ((0, HALF), (HALF, HALF + QUARTER), (HALF + QUARTER, V))
         centres = keep.tile([P, PACK * V], BF16, name="centres", align_bytes=64)
         near01 = keep.tile([P, 2 * NEIGHBOURS * V], BF16, name="near01", align_bytes=64)
         pairs01 = keep.tile([P, NEIGHBOURS * V], BF16, name="pairs01", align_bytes=64)
         near2 = keep.tile([P, NEIGHBOURS * V], BF16, name="near2", align_bytes=64)
         pairs2 = keep.tile([P, 2 * V], BF16, name="pairs2", align_bytes=64)
-        near3 = keep.tile([P, NEIGHBOURS * V], BF16, name="near3", align_bytes=64)
-        pairs3 = [keep.tile([P, 2 * HALF], BF16, name=f"pairs3_{lo}", align_bytes=64) for lo, hi in halves]
+        near3 = [keep.tile([P, V], BF16, name=f"near3_{d}", align_bytes=64) for d in range(NEIGHBOURS)]
+        two3 = keep.tile([P, V], BF16, name="two3", align_bytes=64)
+        three3 = keep.tile([P, V], BF16, name="three3", align_bytes=64)
         z = keep.tile([P, PACK * V], BF16, name="z", align_bytes=64)
 
         def larger_half(dst, tile):
@@ -158,14 +162,19 @@ def tile_picked_sagecat_maxrelu_p_kernel(
         for t in range(2):
             for d in range(NEIGHBOURS):
                 fetch_vector(run(near01, 2 * d + t), t, pos_sb[d][:])
-        fetch_vector(run(near3, 0), 3, pos_sb[0][:])
+        fetch_vector(near3[0][:, 0:VECTOR_TARGETS], 3, entries(pos_sb[0], 0, VECTOR_TARGETS))
         for t in range(1, PACK):
             fetch_scalar(run(centres, t), t, cen_sb[:])
         for d in range(NEIGHBOURS):
             fetch_scalar(run(near2, d), 2, pos_sb[d][:])
-        for lo, hi in halves:
-            for d in range(1, NEIGHBOURS):
-                fetch_scalar(near3[:, d * V + lo:d * V + hi], 3, pos_sb[d][:, lo // GROUP:hi // GROUP])
+        for d in range(1, NEIGHBOURS):
+            fetch_scalar(near3[d][:, 0:HALF], 3, entries(pos_sb[d], 0, HALF))
+        for d in range(NEIGHBOURS - 1):
+            lo = VECTOR_TARGETS if d == 0 else HALF
+            if lo < V:
+                fetch_scalar(near3[d][:, lo:V], 3, entries(pos_sb[d], lo, V))
+        for lo, hi in cuts[1:]:
+            fetch_scalar(near3[3][:, lo:hi], 3, entries(pos_sb[3], lo, hi))
 
         centres_woven = keep.tile([P, PACK * V], BF16, name="centres_woven", align_bytes=64)
         centre_codes = keep.tile([P, V], U32, name="centre_codes", align_bytes=64)
@@ -177,6 +186,13 @@ def tile_picked_sagecat_maxrelu_p_kernel(
         larger_half(pairs01[:], near01)
         larger_half(pairs2[:], near2)
         larger_half(z[:, 0:2 * V], pairs01)
+
+        def larger(dst, a, b, lo, hi):
+            nc.vector.tensor_tensor(dst[:, lo:hi], a[:, lo:hi], b[:, lo:hi], MAX)
+
+        larger(two3, near3[0], near3[1], 0, HALF)
+        larger_half(run(z, 2), pairs2)
+        larger(three3, two3, near3[2], 0, HALF)
         nc.vector.quantize_mx(out=centre_codes[:].bitcast(FP8X4), scales=centre_plane[:], in_=centres_woven[:])
 
         sums = [psum.tile([P, hi - lo], F32, name=f"sums{lo}", tag="bank") for lo, hi in cuts]
@@ -192,14 +208,8 @@ def tile_picked_sagecat_maxrelu_p_kernel(
         result = [keep.tile([P, hi - lo], F32, name=f"result{lo}", align_bytes=64) for lo, hi in cuts]
         z_runs = z[:].rearrange("p (t c r) -> p c t r", t=PACK, r=RUN)
 
-        def plane3_pairs(i):
-            lo, hi = halves[i]
-            both = near3[:].rearrange("p (f e v) -> p f e v", f=2, e=2)[:, :, :, lo:hi]
-            nc.vector.tensor_tensor(pairs3[i][:].rearrange("p (e v) -> p e v", e=2), both[:, 0], both[:, 1], MAX)
-
-        def plane3_largest(i):
-            lo, hi = halves[i]
-            larger_half(z[:, 3 * V + lo:3 * V + hi], pairs3[i])
+        def largest3(lo, hi):
+            nc.vector.tensor_tensor(z[:, 3 * V + lo:3 * V + hi], three3[:, lo:hi], near3[3][:, lo:hi], MAX)
 
         def weave(copy, i, lo, hi):
             start = cuts[i][0]
@@ -213,21 +223,20 @@ def tile_picked_sagecat_maxrelu_p_kernel(
                 out=sums[i][:], lhsT=w3_sb.bitcast(FP4X4), lhsT_scale=w3_plane,
                 rhs=z_codes[i][:].bitcast(FP8X4), rhs_scale=z_plane[i][:], start=False, stop=True,
             )
-            if hi < V:
+            if i != 1:
                 nc.scalar.activation(result[i][:], sums[i][:], RELU)
             else:
                 nc.vector.tensor_scalar_max(result[i][:], sums[i][:], 0.0)
             nc.sync.dma_start(out[:, lo:hi], result[i][:])
 
-        plane3_pairs(0)
-        larger_half(run(z, 2), pairs2)
-        plane3_largest(0)
-        weave(nc.scalar.copy, 0, 0, QUARTER)
-        plane3_pairs(1)
-        weave(nc.vector.tensor_copy, 0, QUARTER, HALF)
-        plane3_largest(1)
-        weave(nc.scalar.copy, 1, *cuts[1])
+        largest3(*cuts[0])
+        larger(two3, near3[0], near3[1], HALF, V)
+        weave(nc.vector.tensor_copy, 0, 0, HALF)
+        larger(three3, two3, near3[2], HALF, V)
         finish(0)
+        largest3(*cuts[1])
+        largest3(*cuts[2])
+        weave(nc.scalar.copy, 1, *cuts[1])
         weave(nc.vector.tensor_copy, 2, *cuts[2])
-        finish(1)
         finish(2)
+        finish(1)

@@ -32,7 +32,7 @@ HALF = V // 2
 QUARTER = V // 4
 SCALAR_COLUMNS = 40
 RUN = 4
-VECTOR_TARGETS = HALF
+VECTOR_TARGETS = 288
 
 
 def tile_picked_sagecat_maxrelu_p_kernel(
@@ -90,7 +90,11 @@ def tile_picked_sagecat_maxrelu_p_kernel(
         nc.scalar.activation(dealt(stage0, 1)[:, 0:SCALAR_COLUMNS], raw[:, 0:SCALAR_COLUMNS, 0:1, :], COPY)
         nc.vector.tensor_copy(dealt(stage0, 1)[:, SCALAR_COLUMNS:P], raw[:, SCALAR_COLUMNS:P, 0:1, :])
         nc.vector.quantize_mx(out=codes[0][:].bitcast(FP8X4), scales=w1_plane[:, 0:P], in_=stage0[:])
-        nc.scalar.activation(dealt(stage23, 2), raw[:, :, 2:PACK, :], COPY)
+        nc.scalar.activation(
+            stage23[:].rearrange("p (t m j) -> p m j t", t=2, j=PACK),
+            w1_raw[:].rearrange("p j (m t) -> p m j t", t=PACK)[:, :, :, 2:PACK],
+            COPY,
+        )
         stage1 = keep.tile([P, H], BF16, name="stage1", tag="stage", align_bytes=64)
         nc.vector.tensor_copy(dealt(stage1, 1), raw[:, :, 1:2, :])
         nc.vector.quantize_mx(out=codes[1][:].bitcast(FP8X4), scales=w1_plane[:, P:2 * P], in_=stage1[:])
@@ -145,13 +149,14 @@ def tile_picked_sagecat_maxrelu_p_kernel(
 
         cuts = ((0, HALF), (HALF, HALF + QUARTER), (HALF + QUARTER, V))
         centres = keep.tile([P, PACK * V], BF16, name="centres", align_bytes=64)
-        near01 = keep.tile([P, 2 * NEIGHBOURS * V], BF16, name="near01", align_bytes=64)
-        pairs01 = keep.tile([P, NEIGHBOURS * V], BF16, name="pairs01", align_bytes=64)
-        near2 = keep.tile([P, NEIGHBOURS * V], BF16, name="near2", align_bytes=64)
-        pairs2 = keep.tile([P, 2 * V], BF16, name="pairs2", align_bytes=64)
-        near3 = [keep.tile([P, V], BF16, name=f"near3_{d}", align_bytes=64) for d in range(NEIGHBOURS)]
-        two3 = keep.tile([P, V], BF16, name="two3", align_bytes=64)
-        three3 = keep.tile([P, V], BF16, name="three3", align_bytes=64)
+        near = keep.tile([P, 3 * NEIGHBOURS * V], BF16, name="near", align_bytes=64)
+        pairs = keep.tile([P, 3 * 2 * V], BF16, name="pairs", align_bytes=64)
+        early3 = keep.tile([P, (NEIGHBOURS + 1) * HALF], BF16, name="early3", align_bytes=64)
+        pairs3 = keep.tile([P, 2 * HALF], BF16, name="pairs3", align_bytes=64)
+        late3 = [early3[:, NEIGHBOURS * HALF:]]
+        late3 = late3 + [keep.tile([P, HALF], BF16, name=f"late3_{d}", align_bytes=64) for d in range(1, NEIGHBOURS)]
+        two3 = keep.tile([P, HALF], BF16, name="two3", align_bytes=64)
+        three3 = keep.tile([P, HALF], BF16, name="three3", align_bytes=64)
         z = keep.tile([P, PACK * V], BF16, name="z", align_bytes=64)
 
         def larger_half(dst, tile):
@@ -161,20 +166,19 @@ def tile_picked_sagecat_maxrelu_p_kernel(
         fetch_vector(run(centres, 0), 0, cen_sb[:])
         for t in range(2):
             for d in range(NEIGHBOURS):
-                fetch_vector(run(near01, 2 * d + t), t, pos_sb[d][:])
-        fetch_vector(near3[0][:, 0:VECTOR_TARGETS], 3, entries(pos_sb[0], 0, VECTOR_TARGETS))
+                fetch_vector(run(near, 3 * d + t), t, pos_sb[d][:])
+        fetch_vector(early3[:, 3 * HALF:3 * HALF + VECTOR_TARGETS], 3, entries(pos_sb[0], 0, VECTOR_TARGETS))
         for t in range(1, PACK):
             fetch_scalar(run(centres, t), t, cen_sb[:])
         for d in range(NEIGHBOURS):
-            fetch_scalar(run(near2, d), 2, pos_sb[d][:])
+            fetch_scalar(run(near, 3 * d + 2), 2, pos_sb[d][:])
         for d in range(1, NEIGHBOURS):
-            fetch_scalar(near3[d][:, 0:HALF], 3, entries(pos_sb[d], 0, HALF))
-        for d in range(NEIGHBOURS - 1):
-            lo = VECTOR_TARGETS if d == 0 else HALF
-            if lo < V:
-                fetch_scalar(near3[d][:, lo:V], 3, entries(pos_sb[d], lo, V))
+            fetch_scalar(run(early3, d - 1, HALF), 3, entries(pos_sb[d], 0, HALF))
+        fetch_scalar(early3[:, 3 * HALF + VECTOR_TARGETS:5 * HALF], 3, entries(pos_sb[0], VECTOR_TARGETS, V))
+        for d in range(1, NEIGHBOURS - 1):
+            fetch_scalar(late3[d][:], 3, entries(pos_sb[d], HALF, V))
         for lo, hi in cuts[1:]:
-            fetch_scalar(near3[3][:, lo:hi], 3, entries(pos_sb[3], lo, hi))
+            fetch_scalar(late3[3][:, lo - HALF:hi - HALF], 3, entries(pos_sb[3], lo, hi))
 
         centres_woven = keep.tile([P, PACK * V], BF16, name="centres_woven", align_bytes=64)
         centre_codes = keep.tile([P, V], U32, name="centre_codes", align_bytes=64)
@@ -183,17 +187,13 @@ def tile_picked_sagecat_maxrelu_p_kernel(
             centres_woven[:].rearrange("p (v t) -> p v t", t=PACK), centres[:].rearrange("p (t v) -> p v t", t=PACK),
             1.0, 0.0, MULT, ADD,
         )
-        larger_half(pairs01[:], near01)
-        larger_half(pairs2[:], near2)
-        larger_half(z[:, 0:2 * V], pairs01)
-
-        def larger(dst, a, b, lo, hi):
-            nc.vector.tensor_tensor(dst[:, lo:hi], a[:, lo:hi], b[:, lo:hi], MAX)
-
-        larger(two3, near3[0], near3[1], 0, HALF)
-        larger_half(run(z, 2), pairs2)
-        larger(three3, two3, near3[2], 0, HALF)
+        both = near[:].rearrange("p (f e w) -> p f e w", f=2, e=2)
+        paired = pairs[:].rearrange("p (e w) -> p e w", e=2)
+        for lo, hi in ((0, 2 * V), (2 * V, 3 * V)):
+            nc.vector.tensor_tensor(paired[:, :, lo:hi], both[:, 0, :, lo:hi], both[:, 1, :, lo:hi], MAX)
         nc.vector.quantize_mx(out=centre_codes[:].bitcast(FP8X4), scales=centre_plane[:], in_=centres_woven[:])
+        larger_half(z[:, 0:3 * V], pairs)
+        nc.vector.tensor_tensor(pairs3[:], run(early3, 0), run(early3, 1), MAX)
 
         sums = [psum.tile([P, hi - lo], F32, name=f"sums{lo}", tag="bank") for lo, hi in cuts]
         for i, (lo, hi) in enumerate(cuts):
@@ -209,7 +209,8 @@ def tile_picked_sagecat_maxrelu_p_kernel(
         z_runs = z[:].rearrange("p (t c r) -> p c t r", t=PACK, r=RUN)
 
         def largest3(lo, hi):
-            nc.vector.tensor_tensor(z[:, 3 * V + lo:3 * V + hi], three3[:, lo:hi], near3[3][:, lo:hi], MAX)
+            late = slice(lo - HALF, hi - HALF)
+            nc.vector.tensor_tensor(z[:, 3 * V + lo:3 * V + hi], three3[:, late], late3[3][:, late], MAX)
 
         def weave(copy, i, lo, hi):
             start = cuts[i][0]
@@ -229,10 +230,10 @@ def tile_picked_sagecat_maxrelu_p_kernel(
                 nc.vector.tensor_scalar_max(result[i][:], sums[i][:], 0.0)
             nc.sync.dma_start(out[:, lo:hi], result[i][:])
 
-        largest3(*cuts[0])
-        larger(two3, near3[0], near3[1], HALF, V)
+        nc.vector.tensor_tensor(two3[:], late3[0], late3[1][:], MAX)
+        larger_half(z[:, 3 * V:3 * V + HALF], pairs3)
+        nc.vector.tensor_tensor(three3[:], two3[:], late3[2][:], MAX)
         weave(nc.vector.tensor_copy, 0, 0, HALF)
-        larger(three3, two3, near3[2], HALF, V)
         finish(0)
         largest3(*cuts[1])
         largest3(*cuts[2])

@@ -56,8 +56,8 @@ def tile_picked_sagecat_maxrelu_p_kernel(
         nc.vector.memset(scale_table[0:SCALE_FIRST, :].bitcast(I32), 0)
         nc.vector.memset(x_plane[:].bitcast(I32), 0)
 
-        nc.sync.dma_start(offs_sb[:], offs)
         nc.sync.dma_start(scale_table[SCALE_FIRST:P, :].bitcast(I32), x_scales[0].bitcast(I32))
+        nc.sync.dma_start(offs_sb[:], offs)
         nc.sync.dma_start(x_table[:], x_words[0].rearrange("p n r -> p (n r)").bitcast(I32))
         nc.sync.dma_start(pos_sb[0][:], pos1)
         nc.sync.dma_start(pos_sb[1][:], pos2)
@@ -175,10 +175,8 @@ def tile_picked_sagecat_maxrelu_p_kernel(
         for d in range(1, NEIGHBOURS):
             fetch_scalar(run(early3, d - 1, HALF), 3, entries(pos_sb[d], 0, HALF))
         fetch_scalar(early3[:, 3 * HALF + VECTOR_TARGETS:5 * HALF], 3, entries(pos_sb[0], VECTOR_TARGETS, V))
-        for d in range(1, NEIGHBOURS - 1):
+        for d in range(1, NEIGHBOURS):
             fetch_scalar(late3[d][:], 3, entries(pos_sb[d], HALF, V))
-        for lo, hi in cuts[1:]:
-            fetch_scalar(late3[3][:, lo - HALF:hi - HALF], 3, entries(pos_sb[3], lo, hi))
 
         centres_woven = keep.tile([P, PACK * V], BF16, name="centres_woven", align_bytes=64)
         centre_codes = keep.tile([P, V], U32, name="centre_codes", align_bytes=64)
@@ -235,8 +233,7 @@ def tile_picked_sagecat_maxrelu_p_kernel(
         nc.vector.tensor_tensor(three3[:], two3[:], late3[2][:], MAX)
         weave(nc.vector.tensor_copy, 0, 0, HALF)
         finish(0)
-        largest3(*cuts[1])
-        largest3(*cuts[2])
+        largest3(HALF, V)
         weave(nc.scalar.copy, 1, *cuts[1])
         weave(nc.vector.tensor_copy, 2, *cuts[2])
         finish(2)

@@ -33,6 +33,7 @@ QUARTER = V // 4
 SCALAR_COLUMNS = 40
 RUN = 4
 VECTOR_TARGETS = 288
+PLANE0_EDGES = (0, 256, 512, 768, 896, 1024)
 
 
 def tile_picked_sagecat_maxrelu_p_kernel(
@@ -116,24 +117,22 @@ def tile_picked_sagecat_maxrelu_p_kernel(
 
         h = [keep.tile([P, S], F32, name=f"h{t}", align_bytes=64) for t in range(PACK)]
         for t in range(PACK):
-            for bank in range(0, S, BANK):
-                width = BANK // 2 if t * S + bank < 3 * BANK else BANK
-                for lo in range(bank, bank + BANK, width):
-                    hi = lo + width
-                    acc = psum.tile([P, width], F32, name="acc", tag="bank")
-                    nc.tensor.matmul_mx(
-                        out=acc[:],
-                        lhsT=w1_codes[t].bitcast(FP8X4),
-                        lhsT_scale=w1_plane[:, t * P:(t + 1) * P],
-                        rhs=picked_words[:, lo:hi].bitcast(FP8X4),
-                        rhs_scale=x_plane[:, lo:hi],
-                        start=True,
-                        stop=True,
-                    )
-                    if t == 0 and hi == S:
-                        nc.vector.tensor_scalar_max(h[t][:, lo:hi], acc[:], 0.0)
-                    else:
-                        nc.scalar.activation(h[t][:, lo:hi], acc[:], RELU)
+            edges = PLANE0_EDGES if t == 0 else range(0, S + 1, BANK // 2 if t == 1 else BANK)
+            for lo, hi in zip(edges, edges[1:]):
+                acc = psum.tile([P, hi - lo], F32, name="acc", tag="bank")
+                nc.tensor.matmul_mx(
+                    out=acc[:],
+                    lhsT=w1_codes[t].bitcast(FP8X4),
+                    lhsT_scale=w1_plane[:, t * P:(t + 1) * P],
+                    rhs=picked_words[:, lo:hi].bitcast(FP8X4),
+                    rhs_scale=x_plane[:, lo:hi],
+                    start=True,
+                    stop=True,
+                )
+                if t == 0 and hi == S:
+                    nc.vector.tensor_scalar_max(h[t][:, lo:hi], acc[:], 0.0)
+                else:
+                    nc.scalar.activation(h[t][:, lo:hi], acc[:], RELU)
 
         def fetch_vector(dst, t, offsets):
             nc.vector.tensor_copy(dst, h[t][:].indirect(offsets))

@@ -16,6 +16,8 @@ FP4X4 = mybir.dt.float4_e2m1fn_x4
 MAX = mybir.AluOpType.max
 ADD = mybir.AluOpType.add
 MULT = mybir.AluOpType.mult
+MIN = mybir.AluOpType.min
+SUBTRACT = mybir.AluOpType.subtract
 RELU = mybir.ActivationFunctionType.Relu
 COPY = mybir.ActivationFunctionType.Copy
 
@@ -32,7 +34,8 @@ HALF = V // 2
 QUARTER = V // 4
 SCALAR_COLUMNS = 40
 RUN = 4
-VECTOR_TARGETS = 288
+VECTOR_TARGETS = 352
+LARGEST = 3.4028234663852886e38
 PLANE0_EDGES = (0, 256, 512, 768, 896, 1024)
 
 
@@ -162,21 +165,31 @@ def tile_picked_sagecat_maxrelu_p_kernel(
             width = tile.shape[1] // 2
             nc.vector.tensor_tensor(dst, run(tile, 0, width), run(tile, 1, width), MAX)
 
+        def neighbours(t, d):
+            return run(near, 6 * (d % 2) + 2 * t + d // 2)
+
+        for d in range(2):
+            fetch_vector(neighbours(0, d), 0, pos_sb[d][:])
         fetch_vector(run(centres, 0), 0, cen_sb[:])
-        for t in range(2):
-            for d in range(NEIGHBOURS):
-                fetch_vector(run(near, 3 * d + t), t, pos_sb[d][:])
+        for t, first in ((0, 2), (1, 0)):
+            for d in range(first, NEIGHBOURS):
+                fetch_vector(neighbours(t, d), t, pos_sb[d][:])
         fetch_vector(early3[:, 3 * HALF:3 * HALF + VECTOR_TARGETS], 3, entries(pos_sb[0], 0, VECTOR_TARGETS))
         for t in range(1, PACK):
             fetch_scalar(run(centres, t), t, cen_sb[:])
         for d in range(NEIGHBOURS):
-            fetch_scalar(run(near, 3 * d + 2), 2, pos_sb[d][:])
+            fetch_scalar(neighbours(2, d), 2, pos_sb[d][:])
         for d in range(1, NEIGHBOURS):
             fetch_scalar(run(early3, d - 1, HALF), 3, entries(pos_sb[d], 0, HALF))
         fetch_scalar(early3[:, 3 * HALF + VECTOR_TARGETS:5 * HALF], 3, entries(pos_sb[0], VECTOR_TARGETS, V))
         for d in range(1, NEIGHBOURS):
             fetch_scalar(late3[d][:], 3, entries(pos_sb[d], HALF, V))
 
+        lead = keep.tile([P, V], F32, name="lead", align_bytes=64)
+        gain = keep.tile([P, V], F32, name="gain", align_bytes=64)
+        nc.gpsimd.tensor_tensor(lead[:], neighbours(0, 1), neighbours(0, 0), SUBTRACT)
+        nc.gpsimd.tensor_scalar(gain[:], lead[:], LARGEST, 0.0, MIN, MAX)
+        nc.gpsimd.tensor_tensor(run(pairs, 0), neighbours(0, 0), gain[:], ADD)
         centres_woven = keep.tile([P, PACK * V], BF16, name="centres_woven", align_bytes=64)
         centre_codes = keep.tile([P, V], U32, name="centre_codes", align_bytes=64)
         centre_plane = keep.tile([P, V], U8, name="centre_plane", align_bytes=64)
@@ -184,12 +197,11 @@ def tile_picked_sagecat_maxrelu_p_kernel(
             centres_woven[:].rearrange("p (v t) -> p v t", t=PACK), centres[:].rearrange("p (t v) -> p v t", t=PACK),
             1.0, 0.0, MULT, ADD,
         )
-        both = near[:].rearrange("p (f e w) -> p f e w", f=2, e=2)
-        paired = pairs[:].rearrange("p (e w) -> p e w", e=2)
-        for lo, hi in ((0, 2 * V), (2 * V, 3 * V)):
-            nc.vector.tensor_tensor(paired[:, :, lo:hi], both[:, 0, :, lo:hi], both[:, 1, :, lo:hi], MAX)
+        for lo, hi in ((V, 4 * V), (4 * V, 6 * V)):
+            nc.vector.tensor_tensor(pairs[:, lo:hi], near[:, lo:hi], near[:, 6 * V + lo:6 * V + hi], MAX)
         nc.vector.quantize_mx(out=centre_codes[:].bitcast(FP8X4), scales=centre_plane[:], in_=centres_woven[:])
-        larger_half(z[:, 0:3 * V], pairs)
+        paired = pairs[:].rearrange("p (t e v) -> p e t v", e=2, v=V)
+        nc.vector.tensor_tensor(z[:, 0:3 * V].rearrange("p (t v) -> p t v", v=V), paired[:, 0], paired[:, 1], MAX)
         nc.vector.tensor_tensor(pairs3[:], run(early3, 0), run(early3, 1), MAX)
 
         sums = [psum.tile([P, hi - lo], F32, name=f"sums{lo}", tag="bank") for lo, hi in cuts]

@@ -34,7 +34,8 @@ HALF = V // 2
 QUARTER = V // 4
 SCALAR_COLUMNS = 40
 RUN = 4
-VECTOR_TARGETS = 352
+VECTOR_TARGETS = 384
+GPSIMD_TARGETS = 320
 LARGEST = 3.4028234663852886e38
 PLANE0_EDGES = (0, 256, 512, 768, 896, 1024)
 
@@ -150,16 +151,12 @@ def tile_picked_sagecat_maxrelu_p_kernel(
             return tile[:, lo // GROUP:hi // GROUP]
 
         cuts = ((0, HALF), (HALF, HALF + QUARTER), (HALF + QUARTER, V))
-        centres = keep.tile([P, PACK * V], BF16, name="centres", align_bytes=64)
+        centres = keep.tile([P, PACK * V], BF16, name="centres", tag="planes", align_bytes=64)
         near = keep.tile([P, 3 * NEIGHBOURS * V], BF16, name="near", align_bytes=64)
         pairs = keep.tile([P, 3 * 2 * V], BF16, name="pairs", align_bytes=64)
-        early3 = keep.tile([P, (NEIGHBOURS + 1) * HALF], BF16, name="early3", align_bytes=64)
-        pairs3 = keep.tile([P, 2 * HALF], BF16, name="pairs3", align_bytes=64)
-        late3 = [early3[:, NEIGHBOURS * HALF:]]
-        late3 = late3 + [keep.tile([P, HALF], BF16, name=f"late3_{d}", align_bytes=64) for d in range(1, NEIGHBOURS)]
-        two3 = keep.tile([P, HALF], BF16, name="two3", align_bytes=64)
+        early3 = keep.tile([P, 6 * HALF], BF16, name="early3", align_bytes=64)
+        late3 = [keep.tile([P, HALF], BF16, name=f"late3_{d}", align_bytes=64) for d in range(2, NEIGHBOURS)]
         three3 = keep.tile([P, HALF], BF16, name="three3", align_bytes=64)
-        z = keep.tile([P, PACK * V], BF16, name="z", align_bytes=64)
 
         def larger_half(dst, tile):
             width = tile.shape[1] // 2
@@ -168,41 +165,45 @@ def tile_picked_sagecat_maxrelu_p_kernel(
         def neighbours(t, d):
             return run(near, 6 * (d % 2) + 2 * t + d // 2)
 
-        for d in range(2):
+        for d in range(NEIGHBOURS):
             fetch_vector(neighbours(0, d), 0, pos_sb[d][:])
         fetch_vector(run(centres, 0), 0, cen_sb[:])
-        for t, first in ((0, 2), (1, 0)):
-            for d in range(first, NEIGHBOURS):
-                fetch_vector(neighbours(t, d), t, pos_sb[d][:])
-        fetch_vector(early3[:, 3 * HALF:3 * HALF + VECTOR_TARGETS], 3, entries(pos_sb[0], 0, VECTOR_TARGETS))
+        for d in range(NEIGHBOURS):
+            fetch_vector(neighbours(1, d), 1, pos_sb[d][:])
+        fetch_vector(early3[:, 4 * HALF:4 * HALF + VECTOR_TARGETS], 3, entries(pos_sb[0], 0, VECTOR_TARGETS))
         for t in range(1, PACK):
             fetch_scalar(run(centres, t), t, cen_sb[:])
         for d in range(NEIGHBOURS):
             fetch_scalar(neighbours(2, d), 2, pos_sb[d][:])
-        for d in range(1, NEIGHBOURS):
-            fetch_scalar(run(early3, d - 1, HALF), 3, entries(pos_sb[d], 0, HALF))
-        fetch_scalar(early3[:, 3 * HALF + VECTOR_TARGETS:5 * HALF], 3, entries(pos_sb[0], VECTOR_TARGETS, V))
-        for d in range(1, NEIGHBOURS):
-            fetch_scalar(late3[d][:], 3, entries(pos_sb[d], HALF, V))
+        fetch_scalar(run(early3, 0, HALF), 3, entries(pos_sb[2], 0, HALF))
+        fetch_scalar(run(early3, 3, HALF), 3, entries(pos_sb[3], 0, HALF))
+        fetch_scalar(early3[:, HALF:3 * HALF], 3, pos_sb[1][:])
+        fetch_scalar(early3[:, 4 * HALF + VECTOR_TARGETS:6 * HALF], 3, entries(pos_sb[0], VECTOR_TARGETS, V))
+        for d in range(2, NEIGHBOURS):
+            fetch_scalar(late3[d - 2][:], 3, entries(pos_sb[d], HALF, V))
 
         lead = keep.tile([P, V], F32, name="lead", align_bytes=64)
         gain = keep.tile([P, V], F32, name="gain", align_bytes=64)
-        nc.gpsimd.tensor_tensor(lead[:], neighbours(0, 1), neighbours(0, 0), SUBTRACT)
-        nc.gpsimd.tensor_scalar(gain[:], lead[:], LARGEST, 0.0, MIN, MAX)
-        nc.gpsimd.tensor_tensor(run(pairs, 0), neighbours(0, 0), gain[:], ADD)
+        for e, width in enumerate((V, GPSIMD_TARGETS)):
+            a, b = neighbours(0, 2 * e)[:, 0:width], neighbours(0, 2 * e + 1)[:, 0:width]
+            nc.gpsimd.tensor_tensor(lead[:, 0:width], b, a, SUBTRACT)
+            nc.gpsimd.tensor_scalar(gain[:, 0:width], lead[:, 0:width], LARGEST, 0.0, MIN, MAX)
+            nc.gpsimd.tensor_tensor(run(pairs, e)[:, 0:width], a, gain[:, 0:width], ADD)
         centres_woven = keep.tile([P, PACK * V], BF16, name="centres_woven", align_bytes=64)
+        pairs3, two3 = centres_woven[:, 0:V], centres_woven[:, V:V + HALF]
         centre_codes = keep.tile([P, V], U32, name="centre_codes", align_bytes=64)
         centre_plane = keep.tile([P, V], U8, name="centre_plane", align_bytes=64)
         nc.gpsimd.tensor_scalar(
             centres_woven[:].rearrange("p (v t) -> p v t", t=PACK), centres[:].rearrange("p (t v) -> p v t", t=PACK),
             1.0, 0.0, MULT, ADD,
         )
-        for lo, hi in ((V, 4 * V), (4 * V, 6 * V)):
-            nc.vector.tensor_tensor(pairs[:, lo:hi], near[:, lo:hi], near[:, 6 * V + lo:6 * V + hi], MAX)
+        rest = V + GPSIMD_TARGETS
+        nc.vector.tensor_tensor(pairs[:, rest:6 * V], near[:, rest:6 * V], near[:, 6 * V + rest:12 * V], MAX)
         nc.vector.quantize_mx(out=centre_codes[:].bitcast(FP8X4), scales=centre_plane[:], in_=centres_woven[:])
+        z = keep.tile([P, PACK * V], BF16, name="z", tag="planes", align_bytes=64)
         paired = pairs[:].rearrange("p (t e v) -> p e t v", e=2, v=V)
         nc.vector.tensor_tensor(z[:, 0:3 * V].rearrange("p (t v) -> p t v", v=V), paired[:, 0], paired[:, 1], MAX)
-        nc.vector.tensor_tensor(pairs3[:], run(early3, 0), run(early3, 1), MAX)
+        nc.vector.tensor_tensor(pairs3, early3[:, 0:V], early3[:, 3 * HALF:5 * HALF], MAX)
 
         sums = [psum.tile([P, hi - lo], F32, name=f"sums{lo}", tag="bank") for lo, hi in cuts]
         for i, (lo, hi) in enumerate(cuts):
@@ -219,7 +220,7 @@ def tile_picked_sagecat_maxrelu_p_kernel(
 
         def largest3(lo, hi):
             late = slice(lo - HALF, hi - HALF)
-            nc.vector.tensor_tensor(z[:, 3 * V + lo:3 * V + hi], three3[:, late], late3[3][:, late], MAX)
+            nc.vector.tensor_tensor(z[:, 3 * V + lo:3 * V + hi], three3[:, late], late3[1][:, late], MAX)
 
         def weave(copy, i, lo, hi):
             start = cuts[i][0]
@@ -233,19 +234,19 @@ def tile_picked_sagecat_maxrelu_p_kernel(
                 out=sums[i][:], lhsT=w3_sb.bitcast(FP4X4), lhsT_scale=w3_plane,
                 rhs=z_codes[i][:].bitcast(FP8X4), rhs_scale=z_plane[i][:], start=False, stop=True,
             )
-            if i != 1:
+            if i != 2:
                 nc.scalar.activation(result[i][:], sums[i][:], RELU)
             else:
                 nc.vector.tensor_scalar_max(result[i][:], sums[i][:], 0.0)
             nc.sync.dma_start(out[:, lo:hi], result[i][:])
 
-        nc.vector.tensor_tensor(two3[:], late3[0], late3[1][:], MAX)
+        nc.vector.tensor_tensor(two3, run(early3, 2, HALF), run(early3, 5, HALF), MAX)
         larger_half(z[:, 3 * V:3 * V + HALF], pairs3)
-        nc.vector.tensor_tensor(three3[:], two3[:], late3[2][:], MAX)
+        nc.vector.tensor_tensor(three3[:], two3, late3[0][:], MAX)
         weave(nc.vector.tensor_copy, 0, 0, HALF)
         finish(0)
         largest3(HALF, V)
         weave(nc.scalar.copy, 1, *cuts[1])
         weave(nc.vector.tensor_copy, 2, *cuts[2])
-        finish(2)
         finish(1)
+        finish(2)

from contextlib import ExitStack

import concourse.mybir as mybir

K, T, S, V, H, N = 512, 2048, 1024, 512, 512, 128
FLOPS = 2 * K * H * S + 2 * 2 * H * N * V

F32 = mybir.dt.float32
BF16 = mybir.dt.bfloat16
I32 = mybir.dt.int32
U32 = mybir.dt.uint32
U16 = mybir.dt.uint16
U8 = mybir.dt.uint8
FP8X4 = mybir.dt.float8_e4m3fn_x4
FP4X4 = mybir.dt.float4_e2m1fn_x4
MAX = mybir.AluOpType.max
ADD = mybir.AluOpType.add
MULT = mybir.AluOpType.mult
MIN = mybir.AluOpType.min
SUBTRACT = mybir.AluOpType.subtract
RELU = mybir.ActivationFunctionType.Relu
COPY = mybir.ActivationFunctionType.Copy

P = 128
PACK = 4
NEIGHBOURS = 4
GROUP = 16
QUADRANT = 32
SCALE_ROWS = 16
SCALE_FIRST = P - SCALE_ROWS
BANK = 512
BANKS = 8
HALF = V // 2
QUARTER = V // 4
SCALAR_COLUMNS = 40
RUN = 4
VECTOR_TARGETS = 384
GPSIMD_TARGETS = 320
LARGEST = 3.4028234663852886e38
PLANE0_EDGES = (0, 256, 512, 768, 896, 1024)


def tile_picked_sagecat_maxrelu_p_kernel(
    tc, x_words, x_scales, w1, w2_words, w2_scales, w3_words, w3_scales, offs, cen, pos1, pos2, pos3, pos4, out
):
    nc = tc.nc
    with ExitStack() as ctx:
        lists = ctx.enter_context(tc.tile_pool(name="lists", bufs=1))
        keep = ctx.enter_context(tc.tile_pool(name="keep", bufs=1))
        psum = ctx.enter_context(tc.psum_pool(name="psum", bufs=BANKS))

        offs_sb = lists.tile([P, S // GROUP], U16, name="offs_sb")
        cen_sb = lists.tile([P, V // GROUP], U16, name="cen_sb")
        pos_sb = [lists.tile([P, V // GROUP], U16, name=f"pos_sb{d}") for d in range(NEIGHBOURS)]

        x_table = keep.tile([P, T], I32, name="x_table", align_bytes=64)
        scale_table = keep.tile([P, T], U8, name="scale_table", tag="scale_table", align_bytes=64)
        x_plane = keep.tile([P, S], U8, name="x_plane", align_bytes=64)
        w1_raw = keep.tile([P, PACK, H], F32, name="w1_raw", tag="w1_raw", align_bytes=64)

        nc.vector.memset(scale_table[0:SCALE_FIRST, :].bitcast(I32), 0)
        nc.vector.memset(x_plane[:].bitcast(I32), 0)

        nc.sync.dma_start(scale_table[SCALE_FIRST:P, :].bitcast(I32), x_scales[0].bitcast(I32))
        nc.sync.dma_start(offs_sb[:], offs)
        nc.sync.dma_start(x_table[:], x_words[0].rearrange("p n r -> p (n r)").bitcast(I32))
        nc.sync.dma_start(pos_sb[0][:], pos1)
        nc.sync.dma_start(pos_sb[1][:], pos2)
        nc.sync.dma_start(w1_raw[:], w1.rearrange("(p j) c -> p j c", j=PACK))
        nc.sync.dma_start(pos_sb[2][:], pos3)
        nc.sync.dma_start(pos_sb[3][:], pos4)
        nc.sync.dma_start(cen_sb[:], cen)

        picked_scales = keep.tile([P, S], U8, name="picked_scales", align_bytes=64)
        nc.vector.tensor_copy(picked_scales[:], scale_table[:].indirect(offs_sb[:]))
        for q in range(P // QUADRANT):
            row = SCALE_FIRST + PACK * q
            nc.sync.dma_start(
                x_plane[QUADRANT * q:QUADRANT * q + PACK, :].bitcast(I32), picked_scales[row:row + PACK, :].bitcast(I32)
            )

        picked_words = keep.tile([P, S], U32, name="picked_words", align_bytes=64)
        nc.vector.tensor_copy(picked_words[:], x_table[:].bitcast(U32).indirect(offs_sb[:]))

        codes = [keep.tile([P, P], U32, name=f"w1_codes{t}", align_bytes=64) for t in range(2)]
        codes23 = keep.tile([P, 2 * P], U32, name="w1_codes23", align_bytes=64)
        w1_plane = keep.tile([P, H], U8, name="w1_plane", align_bytes=64)
        raw = w1_raw[:].rearrange("p j (m t) -> p m t j", t=PACK)

        def dealt(tile, planes):
            return tile[:].rearrange("p (t m j) -> p m t j", t=planes, j=PACK)

        stage0 = keep.tile([P, H], BF16, name="stage0", tag="stage", align_bytes=64)
        stage23 = keep.tile([P, 2 * H], BF16, name="stage23", align_bytes=64)
        nc.scalar.activation(dealt(stage0, 1)[:, 0:SCALAR_COLUMNS], raw[:, 0:SCALAR_COLUMNS, 0:1, :], COPY)
        nc.vector.tensor_copy(dealt(stage0, 1)[:, SCALAR_COLUMNS:P], raw[:, SCALAR_COLUMNS:P, 0:1, :])
        nc.vector.quantize_mx(out=codes[0][:].bitcast(FP8X4), scales=w1_plane[:, 0:P], in_=stage0[:])
        nc.scalar.activation(
            stage23[:].rearrange("p (t m j) -> p m j t", t=2, j=PACK),
            w1_raw[:].rearrange("p j (m t) -> p m j t", t=PACK)[:, :, :, 2:PACK],
            COPY,
        )
        stage1 = keep.tile([P, H], BF16, name="stage1", tag="stage", align_bytes=64)
        nc.vector.tensor_copy(dealt(stage1, 1), raw[:, :, 1:2, :])
        nc.vector.quantize_mx(out=codes[1][:].bitcast(FP8X4), scales=w1_plane[:, P:2 * P], in_=stage1[:])
        nc.vector.quantize_mx(out=codes23[:].bitcast(FP8X4), scales=w1_plane[:, 2 * P:H], in_=stage23[:])
        w1_codes = [codes[0][:], codes[1][:], codes23[:, 0:P], codes23[:, P:2 * P]]

        out_plane = keep.tile([P, 2 * N], U8, name="out_plane", tag="scale_table", align_bytes=64)
        out_words = keep.tile([P, 4 * N], U8, name="out_words", tag="w1_raw", align_bytes=64)
        w3_sb, w2_sb = out_words[:, 0:2 * N], out_words[:, 2 * N:4 * N]
        w2_plane, w3_plane = out_plane[:, 0:N], out_plane[:, N:2 * N]
        nc.gpsimd.memset(out_plane[:].bitcast(I32), 0)
        nc.sync.dma_start(w3_sb.bitcast(I32), w3_words[0].bitcast(I32))
        nc.sync.dma_start(w2_sb.bitcast(I32), w2_words[0].bitcast(I32))
        for scales, first in ((w3_scales, N), (w2_scales, 0)):
            for r in range(PACK):
                nc.sync.dma_start(
                    out_plane[r:P:QUADRANT, first:first + N].bitcast(I32), scales[0, r:SCALE_ROWS:PACK, :].bitcast(I32)
                )

        h = [keep.tile([P, S], F32, name=f"h{t}", align_bytes=64) for t in range(PACK)]
        for t in range(PACK):
            edges = PLANE0_EDGES if t == 0 else range(0, S + 1, BANK // 2 if t == 1 else BANK)
            for lo, hi in zip(edges, edges[1:]):
                acc = psum.tile([P, hi - lo], F32, name="acc", tag="bank")
                nc.tensor.matmul_mx(
                    out=acc[:],
                    lhsT=w1_codes[t].bitcast(FP8X4),
                    lhsT_scale=w1_plane[:, t * P:(t + 1) * P],
                    rhs=picked_words[:, lo:hi].bitcast(FP8X4),
                    rhs_scale=x_plane[:, lo:hi],
                    start=True,
                    stop=True,
                )
                if t == 0 and hi == S:
                    nc.vector.tensor_scalar_max(h[t][:, lo:hi], acc[:], 0.0)
                else:
                    nc.scalar.activation(h[t][:, lo:hi], acc[:], RELU)

        def fetch_vector(dst, t, offsets):
            nc.vector.tensor_copy(dst, h[t][:].indirect(offsets))

        def fetch_scalar(dst, t, offsets):
            nc.scalar.activation(dst, h[t][:].indirect(offsets), COPY)

        def run(tile, index, width=V):
            return tile[:, index * width:(index + 1) * width]

        def entries(tile, lo, hi):
            return tile[:, lo // GROUP:hi // GROUP]

        cuts = ((0, HALF), (HALF, HALF + QUARTER), (HALF + QUARTER, V))
        centres = keep.tile([P, PACK * V], BF16, name="centres", tag="planes", align_bytes=64)
        near = keep.tile([P, 3 * NEIGHBOURS * V], BF16, name="near", align_bytes=64)
        pairs = keep.tile([P, 3 * 2 * V], BF16, name="pairs", align_bytes=64)
        early3 = keep.tile([P, 6 * HALF], BF16, name="early3", align_bytes=64)
        late3 = [keep.tile([P, HALF], BF16, name=f"late3_{d}", align_bytes=64) for d in range(2, NEIGHBOURS)]
        three3 = keep.tile([P, HALF], BF16, name="three3", align_bytes=64)

        def larger_half(dst, tile):
            width = tile.shape[1] // 2
            nc.vector.tensor_tensor(dst, run(tile, 0, width), run(tile, 1, width), MAX)

        def neighbours(t, d):
            return run(near, 6 * (d % 2) + 2 * t + d // 2)

        for d in range(NEIGHBOURS):
            fetch_vector(neighbours(0, d), 0, pos_sb[d][:])
        fetch_vector(run(centres, 0), 0, cen_sb[:])
        for d in range(NEIGHBOURS):
            fetch_vector(neighbours(1, d), 1, pos_sb[d][:])
        fetch_vector(early3[:, 4 * HALF:4 * HALF + VECTOR_TARGETS], 3, entries(pos_sb[0], 0, VECTOR_TARGETS))
        for t in range(1, PACK):
            fetch_scalar(run(centres, t), t, cen_sb[:])
        for d in range(NEIGHBOURS):
            fetch_scalar(neighbours(2, d), 2, pos_sb[d][:])
        fetch_scalar(run(early3, 0, HALF), 3, entries(pos_sb[2], 0, HALF))
        fetch_scalar(run(early3, 3, HALF), 3, entries(pos_sb[3], 0, HALF))
        fetch_scalar(early3[:, HALF:3 * HALF], 3, pos_sb[1][:])
        fetch_scalar(early3[:, 4 * HALF + VECTOR_TARGETS:6 * HALF], 3, entries(pos_sb[0], VECTOR_TARGETS, V))
        for d in range(2, NEIGHBOURS):
            fetch_scalar(late3[d - 2][:], 3, entries(pos_sb[d], HALF, V))

        lead = keep.tile([P, V], F32, name="lead", align_bytes=64)
        gain = keep.tile([P, V], F32, name="gain", align_bytes=64)
        for e, width in enumerate((V, GPSIMD_TARGETS)):
            a, b = neighbours(0, 2 * e)[:, 0:width], neighbours(0, 2 * e + 1)[:, 0:width]
            nc.gpsimd.tensor_tensor(lead[:, 0:width], b, a, SUBTRACT)
            nc.gpsimd.tensor_scalar(gain[:, 0:width], lead[:, 0:width], LARGEST, 0.0, MIN, MAX)
            nc.gpsimd.tensor_tensor(run(pairs, e)[:, 0:width], a, gain[:, 0:width], ADD)
        centres_woven = keep.tile([P, PACK * V], BF16, name="centres_woven", align_bytes=64)
        pairs3, two3 = centres_woven[:, 0:V], centres_woven[:, V:V + HALF]
        centre_codes = keep.tile([P, V], U32, name="centre_codes", align_bytes=64)
        centre_plane = keep.tile([P, V], U8, name="centre_plane", align_bytes=64)
        nc.gpsimd.tensor_scalar(
            centres_woven[:].rearrange("p (v t) -> p v t", t=PACK), centres[:].rearrange("p (t v) -> p v t", t=PACK),
            1.0, 0.0, MULT, ADD,
        )
        rest = V + GPSIMD_TARGETS
        nc.vector.tensor_tensor(pairs[:, rest:6 * V], near[:, rest:6 * V], near[:, 6 * V + rest:12 * V], MAX)
        nc.vector.quantize_mx(out=centre_codes[:].bitcast(FP8X4), scales=centre_plane[:], in_=centres_woven[:])
        z = keep.tile([P, PACK * V], BF16, name="z", tag="planes", align_bytes=64)
        paired = pairs[:].rearrange("p (t e v) -> p e t v", e=2, v=V)
        nc.vector.tensor_tensor(z[:, 0:3 * V].rearrange("p (t v) -> p t v", v=V), paired[:, 0], paired[:, 1], MAX)
        nc.vector.tensor_tensor(pairs3, early3[:, 0:V], early3[:, 3 * HALF:5 * HALF], MAX)

        sums = [psum.tile([P, hi - lo], F32, name=f"sums{lo}", tag="bank") for lo, hi in cuts]
        for i, (lo, hi) in enumerate(cuts):
            nc.tensor.matmul_mx(
                out=sums[i][:], lhsT=w2_sb.bitcast(FP4X4), lhsT_scale=w2_plane,
                rhs=centre_codes[:, lo:hi].bitcast(FP8X4), rhs_scale=centre_plane[:, lo:hi], start=True, stop=False,
            )

        z_woven = [keep.tile([P, PACK * (hi - lo)], BF16, name=f"z_woven{lo}", align_bytes=64) for lo, hi in cuts]
        z_codes = [keep.tile([P, hi - lo], U32, name=f"z_codes{lo}", align_bytes=64) for lo, hi in cuts]
        z_plane = [keep.tile([P, hi - lo], U8, name=f"z_plane{lo}", align_bytes=64) for lo, hi in cuts]
        result = [keep.tile([P, hi - lo], F32, name=f"result{lo}", align_bytes=64) for lo, hi in cuts]
        z_runs = z[:].rearrange("p (t c r) -> p c t r", t=PACK, r=RUN)

        def largest3(lo, hi):
            late = slice(lo - HALF, hi - HALF)
            nc.vector.tensor_tensor(z[:, 3 * V + lo:3 * V + hi], three3[:, late], late3[1][:, late], MAX)

        def weave(copy, i, lo, hi):
            start = cuts[i][0]
            woven = z_woven[i][:].rearrange("p (c r t) -> p c t r", t=PACK, r=RUN)
            copy(woven[:, (lo - start) // RUN:(hi - start) // RUN], z_runs[:, lo // RUN:hi // RUN])

        def finish(i):
            lo, hi = cuts[i]
            nc.vector.quantize_mx(out=z_codes[i][:].bitcast(FP8X4), scales=z_plane[i][:], in_=z_woven[i][:])
            nc.tensor.matmul_mx(
                out=sums[i][:], lhsT=w3_sb.bitcast(FP4X4), lhsT_scale=w3_plane,
                rhs=z_codes[i][:].bitcast(FP8X4), rhs_scale=z_plane[i][:], start=False, stop=True,
            )
            if i != 2:
                nc.scalar.activation(result[i][:], sums[i][:], RELU)
            else:
                nc.vector.tensor_scalar_max(result[i][:], sums[i][:], 0.0)
            nc.sync.dma_start(out[:, lo:hi], result[i][:])

        nc.vector.tensor_tensor(two3, run(early3, 2, HALF), run(early3, 5, HALF), MAX)
        larger_half(z[:, 3 * V:3 * V + HALF], pairs3)
        nc.vector.tensor_tensor(three3[:], two3, late3[0][:], MAX)
        weave(nc.vector.tensor_copy, 0, 0, HALF)
        finish(0)
        largest3(HALF, V)
        weave(nc.scalar.copy, 1, *cuts[1])
        weave(nc.vector.tensor_copy, 2, *cuts[2])
        finish(1)
        finish(2)
